import numpy as np, ml_dtypes
CORES = [10,34,74,98]
N = 4
BF = ml_dtypes.bfloat16
V, G, W, CAP, QA, QB, RO = 1024, 768, 2560, 128, 4, 2, 4
def deal(rng, a):
    return np.stack([rng.permutation(np.resize(np.array(a), 8)) for q in range(N)])
def parts(rng):
    sh = (N, 8, 16, V)
    mid = rng.integers(20, 236, (N, 8, 16, 16)); kin = rng.integers(0, 16, (N, 8, 1, V))
    x = np.take_along_axis(mid, kin, 3) + rng.integers(-20, 21, sh)
    low = deal(rng, [0.003, 0.01, 0.03])[:, :, None, None]; flat = deal(rng, [0, 1])[:, :, None, None] == 1
    r = np.where(flat, 255, rng.integers(130, 256, sh)); r = np.where(rng.random(sh) < low, rng.integers(1, 130, sh), r)
    p = np.where(rng.random(sh) < 0.15, rng.integers(1, 130, sh), 0)
    keep = deal(rng, [0.4, 0.7, 0.9])[:, :, None, None]
    s = np.where(rng.random(sh) < keep, np.arange(V), rng.integers(0, W, sh))
    c = np.where(rng.random(sh) < 0.5, rng.integers(0, V, sh), rng.integers(0, W, sh))
    h = deal(rng, [180, 230, 500, 1000, 1200]) + rng.integers(0, 32, (N, 8))
    return x, r, p, c, s, h
def pack(x, r, p, c, s, h):
    v = {"x": x, "reach": r, "past": p}
    d = {k: np.ascontiguousarray(v[k].reshape(N, 128, V)).astype(np.float32).astype(BF) for k in v}
    d["cand"] = np.ascontiguousarray(c.reshape(N, 128, V)).astype(np.int32); d["succ"] = np.ascontiguousarray(s.reshape(N, 128, V)).astype(np.int32)
    d["th"] = h.reshape(N, 8, 1).astype(np.int32)
    return d
def setup_inputs(rng):
    return pack(*parts(rng))
def setup_inputs_ends(rng):
    sh = (N, 8, 16, V); one = (N, 8, 1, V)
    x = 255 * np.where(rng.random(one) < 0.7, rng.integers(0, 2, one), rng.integers(0, 2, sh))
    x = np.where((rng.random(one) < 0.2) & (rng.random(sh) < 0.3), x + np.where(x == 0, 1, -1), x)
    k = rng.random(one); r = np.where(k < 0.5, 255, np.where(k < 0.6, 1, np.where(rng.random(sh) < 0.5, 1, 255)))
    p = 255 * ((rng.random(one) < 0.25) & (rng.random(sh) < 0.2)).astype(np.int64)
    c = np.where(rng.random(sh) < 0.65, (W - 1) * rng.integers(0, 2, sh), rng.integers(0, W, sh))
    s = np.where((rng.random(one) < 0.5) | (rng.random(sh) < 0.65), (W - 1) * rng.integers(0, 2, sh), rng.integers(0, W, sh))
    h = 4095 * rng.integers(0, 2, (N, 8)); h[:, 0] = 0; h[:, 4] = 4095; h[:, 7] = 4095
    for a in (0, 1, V - QA, V - 1, G - 1): p[..., a] = 0; r[..., a] = 255
    p[..., 2] = 255; r[..., 2] = 1; x[..., 0] = 0; x[..., V - QA] = 0
    for a in (1, V - 1): x[:, 1::2, :, a] = 255; x[:, ::2, :, a] = 0
    c[..., 0] = 2; c[:, :, 15, 0] = V - 1
    c[..., V - QA] = 2; c[:, :, 14, V - QA] = V - 1; c[:, :, 15, V - QA] = 1
    s[..., 0] = 0; s[..., G - 1] = W - 1
    return pack(x, r, p, c, s, h)
def setup_inputs_corners(rng):
    x, r, p, c, s, h = parts(rng); act = np.arange(0, G, QB); here = np.arange(V); ptr = np.array([0, V - 1, V, V + G - 1, V + G, W - 1])
    for q in range(N):
        for g in range(8):
            k = (g + q) % 8
            if k < 6:
                n = (0, 1, CAP - 1, CAP, CAP + 1, len(act))[k]; a = rng.permutation(act)[:n]
                h[q, g] = 0; x[q, g] = x[q, g][:, rng.integers(0, 16, V)]; r[q, g] = 200; r[q, g, :, V - 1] = 5
                p[q, g] = np.where(rng.random((16, V)) < 0.05, 10, 0)
                w = np.tile(here, (16, 1)); w[rng.integers(0, 16, n), a] = V - 1; s[q, g] = w
            elif k == 6:
                h[q, g] = 4095; p[q, g] = 0; c[q, g] = here - here % QA + (here + QA - 1) % QA
            else:
                h[q, g] = 4095; full = rng.random(V) < 0.5; full[0] = True; full[V - 1] = False; m = rng.random(V) < 0.5; n = int(np.count_nonzero(m))
                w = p[q, g].copy(); w[:, full] = 255; p[q, g] = w
                w = np.where(rng.random((16, V)) < 0.5, rng.integers(V, W, (16, V)), (here + QA * rng.integers(0, V // QA, (16, V))) % V)
                w[:, m] = rng.choice(here[full], (16, n)); w[15, m] = rng.integers(0, V, n); c[q, g] = w
                s[q, g] = np.where(rng.random((16, V)) < 0.3, here, ptr[rng.integers(0, 6, (16, V))])
    return pack(x, r, p, c, s, h)
def setup_inputs_ties(rng):
    x, r, p, c, s, h = parts(rng); sh = (N, 8, 16, V)
    x = 8 * rng.integers(0, 2, sh); pool = rng.integers(0, V, (N, 8, 1, 24)); pool[..., 0] = 0; pool[..., 1] = V - 1; pool[..., 2] = V; pool[..., 3] = W - 1
    few = np.take_along_axis(pool, rng.integers(0, 24, sh), 3); c[:, ::2] = few[:, ::2]
    m = np.arange(16)[:, None] == rng.integers(0, 16, (N, 8, 1, 1))
    r = np.where(m, rng.integers(100, 102, sh), rng.integers(101, 256, sh)); p = np.where(m, rng.integers(99, 101, sh), 0)
    h = deal(rng, [24, 32, 40, 48, 64])
    return pack(x, r, p, c, s, h)
def setup_inputs_border(rng):
    x, r, p, c, s, h = parts(rng); x = rng.integers(0, 256, x.shape); h = rng.integers(1, 33, h.shape); s[...] = np.arange(V)
    goal = np.zeros((N, 8, 3), np.int64); e, y, w = G - 1, V - 3, V - 2
    for q in range(N):
        for g in range(8):
            n, turn = ((0, 0), (0, int(rng.integers(1, 3))), (CAP - 1, 0), (CAP, 0), (CAP + 1, 0), (G, 0))[(g + q) % 6]
            o = [4 * rng.permutation(G // 4 - 1) + i for i in range(4)]
            v = o[turn][0]; j = o[0][1]; v1 = o[1][1]; u = o[1][2]; b = o[3][1]; z = o[3][2]
            for a in (v, e, j, y, v1, w, u, b): s[q, g, :, a] = z; c[q, g, :, a] = rng.integers(V, W, 16)
            for a in (v, v1, u): r[q, g, :, a] = rng.integers(140, 200, 16); p[q, g, :, a] = rng.integers(0, 41, 16)
            for a in (e, j): r[q, g, :, a] = rng.integers(200, 255, 16); p[q, g, :, a] = 0
            for a in (y, w): r[q, g, :, a] = 255; p[q, g, :, a] = 0
            r[q, g, :, z] = 255; r[q, g, :, V - 1] = 1
            i, k = rng.integers(0, 16, 2); d = int(rng.integers(1, 41))
            r[q, g, :, b] = r[q, g, :, u]; p[q, g, :, b] = p[q, g, :, u]; r[q, g, i, b] -= d; p[q, g, k, b] += d
            for a, f in ((v, e), (j, y), (v1, y), (w, y), (u, b)): x[q, g, :, a] = x[q, g, :, f]
            for a, f in ((v, e), (j, y), (v1, j), (w, y), (u, b)): c[q, g, int(rng.integers(0, 16)), a] = f
            a = rng.permutation(np.setdiff1d(np.arange(0, G, QB), np.array([v, j])))[:n]
            s[q, g][rng.integers(0, 16, len(a)), a] = V - 1
            goal[q, g] = (e, u, j)
    k = np.arange(G, V - 3)
    for q in range(N):
        for g in range(8):
            see = np.concatenate([V + goal[(q + 1) % N, g], V + G + goal[(q - 1) % N, g]])
            r[q, g, :, G:V - 3] = 255; p[q, g, :, G:V - 3] = 0
            s[q, g][rng.integers(0, 16, len(k)), k] = see[((k - G) // 4) % 6]
    return pack(x, r, p, c, s, h)
def setup_inputs_spread(rng):
    sh = (N, 8, 16, V); one = (N, 8, 1, V)
    def uneven(): return np.floor(np.exp2(8 * rng.random(one)) * rng.random(sh)).astype(np.int64)
    def lean():
        e = deal(rng, [1.0, 2.0, 4.0])[:, :, None, None]; v = np.minimum((W * rng.random(sh) ** e).astype(np.int64), W - 1)
        return np.where(deal(rng, [0, 0, 1])[:, :, None, None] == 1, W - 1 - v, v)
    x = uneven(); r = np.maximum(255 - uneven(), 1); p = np.where(rng.random(one) < 0.3, uneven(), 0)
    c = lean(); s = np.where(rng.random(one) < rng.random(sh), np.arange(V), lean())
    h = np.minimum(np.floor(np.exp2(12 * rng.random((N, 8)))).astype(np.int64), 4095)
    return pack(x, r, p, c, s, h)
def check_inputs(d):
    bad = []
    for k, lo, hi in (("x", 0, 255), ("reach", 1, 255), ("past", 0, 255), ("cand", 0, W - 1), ("succ", 0, W - 1), ("th", 0, 4095)):
        a = np.asarray(d[k]).astype(np.float64)
        if not (np.all(a >= lo) and np.all(a <= hi)): bad.append("range of " + k)
        elif not np.all(a == np.floor(a)): bad.append("whole numbers in " + k)
    return bad
def at(a, ix):
    return np.take_along_axis(a, ix[:, :, None, :], 3)
def reference(x, reach, past, cand, succ, th):
    X = x.astype(np.float32).astype(np.int32).reshape(N, 8, 16, V)
    R = reach.astype(np.float32).astype(np.int32).reshape(N, 8, 16, V); P = past.astype(np.float32).astype(np.int32).reshape(N, 8, 16, V)
    R = np.concatenate([R, np.roll(R[..., :G], -1, axis=0), np.roll(R[..., :G], 1, axis=0)], axis=3)
    P = np.concatenate([P, np.roll(P[..., :G], -1, axis=0), np.roll(P[..., :G], 1, axis=0)], axis=3)
    C = cand.astype(np.int64).reshape(N, 8, 16, V); S = succ.astype(np.int64).reshape(N, 8, 16, V); H = th.astype(np.int64).reshape(N, 8)
    F = np.zeros((N, 8, W), np.int64) + np.arange(W); M = np.zeros(N, np.int64); odd = (np.arange(16) % 2 == 1)[:, None]; NONE = 2 ** 20
    qi, gi = np.arange(N)[:, None, None], np.arange(8)[None, :, None]
    for t in range(RO):
        r_old, p_old, f_old = R[..., :G].copy(), P[..., :G].copy(), F[..., :G].copy()
        a = slice(t % QA, V, QA); v = np.arange(t % QA, V, QA); L = len(v)
        c = np.take_along_axis(F, C[..., a].reshape(N, 8, 16 * L), 2)
        xc, rc, pc = [at(w, i).reshape(N, 8, 16, 16, L) for w, i in ((X, np.minimum(c, V - 1)), (R, c), (P, c))]
        xv, rv, pv = [w[..., a][:, :, :, None, :] for w in (X, R, P)]
        c = c.reshape(N, 8, 16, L); ordered = np.any((rv <= pc) | (rc <= pv), axis=2)
        fit = ~ordered & (c < V) & (c % QA != t % QA)
        D = np.where(fit, np.add.reduce(np.abs(xc - xv), axis=2), NONE)
        k = np.argmin(D, axis=2)[:, :, None, :]
        b = np.take_along_axis(c, k, 2)[:, :, 0]; D = np.take_along_axis(D, k, 2)[:, :, 0].astype(np.int64); has = D < NONE; b = np.where(has, b, 0)
        C[..., a] = np.where(ordered & has[:, :, None, :], at(C, b), C[..., a])
        asks = has & (D < H[:, :, None] + (M & 31)[:, None, None]); key = np.where(asks, D * V + v, 2 ** 40)
        best = np.full((N, 8, V), 2 ** 40, np.int64); np.minimum.at(best, (qi, gi, b), key)
        win = asks & (np.take_along_axis(best, b, 2) == key); m = win[:, :, None, :]
        xb, rb, pb, sb = at(X, b), at(R, b), at(P, b), at(S, b)
        X[..., a] = np.where(m, (X[..., a] + xb) >> 1, X[..., a])
        R[..., a] = np.where(m, np.minimum(R[..., a], rb), R[..., a]); P[..., a] = np.where(m, np.maximum(P[..., a], pb), P[..., a])
        S[..., a] = np.where(m & odd, sb, S[..., a])
        i, j, l = np.nonzero(win); F[i, j, b[i, j, l]] = v[l]
        M = np.add.reduce(win.astype(np.int64).reshape(N, -1), axis=1)
        a = slice(t % QB, V, QB); L = len(range(t % QB, V, QB))
        c = np.take_along_axis(F, S[..., a].reshape(N, 8, 16 * L), 2)
        low = np.min(at(R, c).reshape(N, 8, 16, 16, L), axis=3); R[..., a] = np.minimum(R[..., a], low)
        ch = np.any(R[..., :G] != r_old, axis=2) | np.any(P[..., :G] != p_old, axis=2) | (F[..., :G] != f_old)
        go = ch & (np.add.accumulate(ch.astype(np.int64), axis=2) <= CAP)
        for turn, o in ((-1, V), (1, V + G)):
            w = np.roll(go, turn, axis=0); m = w[:, :, None, :]; f = np.roll(F[..., :G], turn, axis=0)
            R[..., o:o + G] = np.where(m, np.roll(R[..., :G], turn, axis=0), R[..., o:o + G])
            P[..., o:o + G] = np.where(m, np.roll(P[..., :G], turn, axis=0), P[..., o:o + G])
            F[..., o:o + G] = np.where(w & (f < G), f + o, F[..., o:o + G])
    return {"yx": X.reshape(N, 128, V).astype(np.float32).astype(BF), "yr": np.ascontiguousarray(R[..., :V]).reshape(N, 128, V).astype(np.float32).astype(BF), "yc": C.reshape(N, 128, V).astype(np.float32)}

@@ -1,0 +1,640 @@
+import math
+from concourse.bass import DstId, RemoteDMATransfer
+from concourse.mybir import AluOpType as ALU, AxisListType, ActivationFunctionType as AF
+
+V, G, W, N, ROUNDS = 1024, 768, 2560, 4, 4
+BIGX = 8192.0
+HASLIM = 4100.0 * 1024
+EQ = 1048576.0
+NS_P = ((0, 1, 2, 3, 4, 5, 6, 7),) + ((3, 4, 5, 6, 7),) * 3
+NX_S = ()
+NV3 = 1
+
+b, f, i4, u2 = "bfloat16", "float32", "int32", "uint16"
+_S = {
+    "X": (1024, b), "R": (1024, b), "P": (1024, b), "xF": (2560, b), "RF": (2560, b), "PF": (2560, b), "xm": (1024, b),
+    "FB": (1280, b), "IB": (1024, b), "ni": (256, i4),
+    "ci": (1024, i4), "si": (1024, i4), "CF": (1024, f), "CfE": (1024, f), "CfO": (1024, f), "NHI": (256, b), "NLO": (256, b),
+    "SO": (1024, f), "SE": (1024, f), "SL0": (512, u2), "SL1": (512, u2),
+    "D1": (512, f), "T1": (512, f), "T2": (496, f), "ckf": (256, f), "CK0": (256, u2), "CK1": (256, u2), "CK2": (256, u2), "CK3": (256, u2),
+    "ones": (512, b), "I": (128, b), "nI": (128, b), "bI": (128, b), "U": (128, b), "E0": (128, b), "B16": (128, b),
+    "EK": (2048, b), "BL": (2048, b), "SelL": (2048, b), "RH": (2048, b), "kc": (512, b), "rst": (1024, b),
+    "SA": (128, b), "SB": (128, b), "SN": (128, b), "rows2": (256, b), "zb": (128, b),
+    "selD": (16, b), "selO": (16, b), "selp": (16, b), "seln": (16, b), "sFp": (16, b), "sFn": (16, b), "FS": (16, b), "FH": (16, b), "gm": (16, f),
+    "gmi": (16, i4), "mi16": (16, f), "mp": (16, f), "pw": (16, f), "sj": (16, f),
+    "pi": (1, i4), "gi": (1, i4), "ii": (1, i4), "ei": (1, i4), "oki": (1, i4), "mI": (128, i4), "mG": (128, i4), "mGf": (128, f),
+    "pf": (1, f), "gf": (1, f), "iF": (1, f), "i4c": (1, f), "modd": (1, f), "meven": (1, f), "okc": (1, f), "ekc": (1, f),
+    "wcol": (1, f), "il1": (1, f), "wlo": (1, f), "whi": (1, f), "wF": (1, f), "wFn": (1, f), "fhc": (1, f), "c7": (1, f), "c8": (1, f), "mone": (1, f), "c64": (1, f),
+    "cb": (2, f), "VL": (128, f), "VR": (96, f), "CC": (96, f), "V0": (96, f), "NG": (96, b), "NG1": (96, b), "kI": (128, b), "chz": (96, b), "thT": (16, f), "thA": (16, f),
+    "thr": (8, i4), "thb": (8, i4), "thK": (16, f), "thC": (16, f), "Mf": (1, f), "Mi": (1, i4), "Mj": (1, i4), "Mk": (1, f),
+    "xv2": (512, b), "Rv2": (512, b), "Pv2": (512, b), "dx": (4096, b), "ab": (4096, b), "oR": (4096, b), "oP": (4096, b), "pc": (4096, b),
+    "ka": (256, f), "t1": (256, f), "wk": (512, f), "wi": (128, i4), "dec": (32, b), "dec2": (48, b), "rowsN": (256, b), "nl": (16, u2),
+    "bits": (256, b), "Ae": (256, b), "Ao": (256, b), "Bk": (256, b), "tr": (512, b), "mx": (16, f), "win": (16, b), "rowsW": (512, b),
+    "bd": (32, f), "bl": (16, f), "bq": (32, f), "bq2": (32, f), "LL": (32, u2), "bu": (16, u2), "Rn": (256, b), "Pn": (256, b), "xs": (256, f), "xi": (256, i4),
+    "sn": (256, f), "FL": (64, u2), "g3": (8192, b), "s3": (8192, b), "oi": (256, f), "dC": (256, f),
+    "ch": (96, b), "xw": (768, f), "pos": (96, b), "FpT": (96, f), "dF": (96, f), "Fpb": (96, b), "rowsP": (768, b), "rowsF": (768, b), "pl": (48, u2), "SLB": (896, b),
+    "GRa": (896, b), "GRb": (896, b), "GPa": (896, b), "GPb": (896, b),
+}
+_WHERE, _POOL = {}, {f: 0, i4: 0, u2: 0, b: 0}
+SCRATCH = {}
+_OWN = ("nl", "pl", "FL", "LL", "bu", "SelL", "SA", "SB", "SN")
+for _n, (_c, _d) in _S.items():
+    if _c <= 128 and _n not in _OWN:
+        _WHERE[_n] = ("pool_" + _d, _POOL[_d]); _POOL[_d] += _c + (-_c) % 16
+    else:
+        SCRATCH[_n] = ("sbuf", [128, _c], _d); _WHERE[_n] = (_n, 0)
+for _d in _POOL:
+    if _POOL[_d]:
+        SCRATCH["pool_" + _d] = ("sbuf", [128, _POOL[_d]], _d)
+for _r in range(3):
+    for _n, _c, _d in (("SRP%d", 256, b), ("SLL%d", 56, u2), ("LRa%d", 256, b), ("LRb%d", 256, b), ("LLa%d", 56, u2), ("LLb%d", 56, u2)):
+        SCRATCH[_n % _r] = ("sbuf", [128, _c], _d); _WHERE[_n % _r] = (_n % _r, 0)
+for _r in range(8):
+    SCRATCH["pb%d" % _r] = ("psum", [128, 512], f); _WHERE["pb%d" % _r] = ("pb%d" % _r, 0)
+ND = 24
+SEMAPHORES = ["qv", "qs", "qt", "qg", "iR", "iP", "loc", "li"] + ["aR%d" % r for r in range(3)] + ["aL%d" % r for r in range(3)] + ["d%d" % k for k in range(ND)]
+
+
+def rank_program(g, core, T, topo):
+    rank = T.rank_of(core)
+    if rank is None:
+        return
+    eng = {"v": g.vector, "s": g.scalar, "t": g.tensor, "g": g, "y": g.sync}
+    cnt = {q: 0 for q in eng}; clk = {q: {} for q in eng}; hist = {}; info = []; total = {}; nd = [0]
+
+    def A(n, c0=0, c1=None, st=1, p0=0, p1=128):
+        t, o = _WHERE[n]
+        if c1 is None:
+            c1 = _S[n][0] if n in _S else SCRATCH[n][1][1]
+        ap = T[t][p0:p1, o + c0:o + c1] if st == 1 else T[t][p0:p1, o + c0:o + c1:st]
+        return (ap, [(n, c0, c1, st)])
+
+    def IND(w, o):
+        return (w[0].indirect(o[0]), w[1] + o[1])
+
+    def HB(ap):
+        return (ap, [])
+
+    def covers(a0, a1, st, e):
+        return a0 <= e[0] and e[1] <= a1 and (st == 1 or (e[4] == st and (e[0] - a0) % st == 0))
+
+    def sync(q, rd, wr, me):
+        need = set()
+        for regs, isw in ((rd, False), (wr, True)):
+            for n, a0, a1, st in regs:
+                ps = n[:2] == "pb"
+                for e in hist.get(n, ()):
+                    over = e[0] < a1 and a0 < e[1] and (e[0] - a0) % math.gcd(st, e[4]) == 0
+                    eq = info[e[2]][0]
+                    if ps:
+                        if eq != q or (over and e[3] and q != "t"):
+                            need.add(e[2])
+                    elif over and (e[3] or isw):
+                        need.add(e[2])
+        for o in sorted(need, reverse=True):
+            _, sem, val, ck = info[o]
+            if clk[q].get(sem, 0) >= val:
+                continue
+            eng[q].wait_ge(T.sem[sem], val)
+            for s, v in list(ck.items()) + [(sem, val)]:
+                if clk[q].get(s, 0) < v:
+                    clk[q][s] = v
+        for regs, isw in ((rd, False), (wr, True)):
+            for n, a0, a1, st in regs:
+                ps = n[:2] == "pb"
+                if ps:
+                    h = [e for e in hist.get(n, ()) if info[e[2]][0] == me[1] and not (covers(a0, a1, st, e) and isw == e[3])]
+                elif isw:
+                    h = [e for e in hist.get(n, ()) if not covers(a0, a1, st, e)]
+                else:
+                    h = [e for e in hist.get(n, ()) if not (not e[3] and covers(a0, a1, st, e) and info[e[2]][0] == q)]
+                h.append((a0, a1, me[0], isw, st)); hist[n] = h
+
+    def op(q, call, rd, wr):
+        me = len(info)
+        rr = [x for r in rd for x in r[1]]; ww = [x for r in wr for x in r[1]]
+        info.append((q, "q" + q, cnt[q] + 1, {}))
+        sync(q, rr, ww, (me, q))
+        if q == "g" and clk[q].get("qg", 0) < cnt[q]:
+            g.wait_ge(T.sem["qg"], cnt[q]); clk[q]["qg"] = cnt[q]
+        cnt[q] += 1
+        info[me] = (q, "q" + q, cnt[q], dict(clk[q]))
+        call(eng[q]).then_inc(T.sem["q" + q], 1); total["q" + q] = cnt[q]
+
+    def dma(q, out, in_):
+        me = len(info); s = "d%d" % nd[0]; nd[0] += 1
+        info.append(("d" + s, s, 16, {}))
+        sync(q, in_[1], out[1], (me, "d" + s))
+        info[me] = ("d" + s, s, 16, dict(clk[q])); total[s] = 16
+        eng[q].dma_start(out=out[0], in_=in_[0]).then_inc(T.sem[s], 16)
+
+    def arrive(sem, val, regs):
+        me = len(info); info.append(("x", sem, val, {})); total[sem] = val
+        for r in regs:
+            for n, a0, a1, st in r[1]:
+                hist.setdefault(n, []).append((a0, a1, me, True, st))
+
+    prev, nxt = T.cores[(rank - 1) % N], T.cores[(rank + 1) % N]
+    mk = min(topo.mask(core, prev), topo.mask(core, nxt))
+    ne = len([e for e in topo.engines(core, prev) if mk >> e & 1])
+
+    def send(src, to_prev, to_next, sem, loc="loc"):
+        sync("g", src[1], [], (len(info), "x")); info.append(("x", loc, 2 * ne, {}))
+        ids = []
+        for d in (prev, nxt):
+            rid, pid, _ = topo.addr(d); ids.append(DstId(rid=rid, pnc=pid))
+        g.remote_dma_fused([RemoteDMATransfer(dst_ids=ids, dma_engine_mask=mk, remote_sem=T.sem[sem], srcs=[src[0]], dsts=[to_prev[0], to_next[0]])], local_sem=T.sem[loc])
+        total[loc] = total.get(loc, 0) + ne
+
+    def cp(q, out, in_):
+        if q == "s":
+            op("s", lambda e: e.activation(out=out[0], in_=in_[0], func=AF.Copy), [in_], [out])
+        else:
+            op("v", lambda e: e.tensor_copy(out=out[0], in_=in_[0]), [in_], [out])
+
+    def tt(out, a, c, o):
+        op("v", lambda e: e.tensor_tensor(out=out[0], in0=a[0], in1=c[0], op=o), [a, c], [out])
+
+    def ts(out, a, s1, o1, s2=None, o2=None):
+        rd = [a] + [s for s in (s1, s2) if isinstance(s, tuple)]
+        v1 = s1[0] if isinstance(s1, tuple) else s1
+        v2 = s2[0] if isinstance(s2, tuple) else s2
+        if o2 is None:
+            op("v", lambda e: e.tensor_scalar(out=out[0], in0=a[0], scalar1=v1, scalar2=None, op0=o1), rd, [out])
+        else:
+            op("v", lambda e: e.tensor_scalar(out=out[0], in0=a[0], scalar1=v1, scalar2=v2, op0=o1, op1=o2), rd, [out])
+
+    def act(out, in_, fn, bias=None, scale=None, accum=None):
+        kw = {}
+        rd = [in_]; wr = [out]
+        if bias is not None:
+            kw["bias"] = bias[0]; rd.append(bias)
+        if scale is not None:
+            kw["scale"] = scale[0]; rd.append(scale)
+        if accum is not None:
+            kw["accum_out"] = accum[0]; wr.append(accum)
+        op("s", lambda e: e.activation(out=out[0], in_=in_[0], func=fn, **kw), rd, wr)
+
+    def ms(out, c):
+        op("v", lambda e: e.memset(out[0], c), [], [out])
+
+    def mm(out, l, r, start, stop):
+        op("t", lambda e: e.matmul(out=out[0], lhsT=l[0], rhs=r[0], start=start, stop=stop), [l, r], [out])
+
+    def iota(out, pat, base, cmul, small=False):
+        kw = {"allow_small_or_imprecise_dtypes": True} if small else {}
+        op("g", lambda e: e.iota(out[0], pat, base, cmul, **kw), [], [out])
+
+    def sel(out, in_, pat, o, fill, base, cmul):
+        op("g", lambda e: e.affine_select(out[0], in_[0], pat, o, fill, base, cmul), [in_], [out])
+
+    def rsum(out, in_):
+        op("v", lambda e: e.tensor_reduce(out=out[0], in_=in_[0], axis=AxisListType.X, op=ALU.add), [in_], [out])
+
+    def dup(q, out, src, t):
+        for h in (0, 256):
+            cp(q, A(out, h, h + 256), A(src, t, V, 4))
+
+    def cklist_d(t):
+        for e, src in ((0, "CfE"), (1, "CfO")):
+            for i in range(16):
+                sel(A("D1", 16 * e + i, 512, 32), A(src, 4 * i + t, V, 64), [[0, 16]], ALU.is_equal, 0.0, 0, 0)
+
+    def turn():
+        op("v", lambda e: e.transpose(out=A("T1")[0], in_=A("D1")[0]), [A("D1")], [A("T1")])
+
+    def cklist_t():
+        turn()
+        tt(A("T2"), A("T1", 0, 496), A("T1", 16, 512), ALU.add)
+        for k in range(16):
+            sel(A("ckf", 16 * k, 16 * k + 16), A("T2", k, 496, 32), [[0, 16]], ALU.is_equal, 0.0, 0, 0)
+
+    def halves(t, which):
+        n, o, s = (("NHI", ALU.arith_shift_right, 6), ("NLO", ALU.bitwise_and, 63))[which]
+        ts(A("ni"), A("ci", t, V, 4), s, o); cp("v", A(n), A("ni"))
+
+    def xgather(t, kk):
+        s = (512 * kk, 512 * kk + 512)
+        tt(A("dx", *s), IND(A("xF"), A("CK%d" % t, 32 * kk, 32 * kk + 32)), A("xv2"), ALU.subtract)
+
+    def xscalar(t, kk):
+        s, bank = (512 * kk, 512 * kk + 512), A("pb%d" % (2 + kk % 2))
+        cp("s", A("dx", *s), IND(A("xF"), A("CK%d" % t, 32 * kk, 32 * kk + 32)))
+        mm(bank, A("I"), A("dx", *s), True, False); mm(bank, A("nI"), A("xv2"), False, True)
+
+    def xabs(kk):
+        s = (512 * kk, 512 * kk + 512)
+        act(A("ab", *s), A("dx", *s), AF.Abs)
+
+    def keyinit():
+        for half in (0, 1):
+            o = A("pb%d" % half, 0, 256)
+            mm(o, A("E0"), A("kc", 256 * half, 256 * half + 256), True, False)
+            for hv in range(4):
+                h, var = hv // 2, hv % 2
+                mm(o, A(("NHI", "NLO")[var], 128 * h, 128 * h + 128), A("RH", 512 * hv + 256 * half, 512 * hv + 256 * half + 256), False, False)
+
+    def keymm(kk, buf, w, last=False):
+        bank = "pb%d" % (kk // 4)
+        for k in (2 * kk, 2 * kk + 1):
+            for h in (0, 1):
+                o = 32 * (k % 8) + h
+                mm(A(bank, o, o + 32 - h, 2), A(buf, 256 * k + 128 * h, 256 * k + 128 * h + 128), A(w), False, last and k % 8 == 7 and h == 1)
+
+    def bits2list(out, src, n):
+        for i in range(16):
+            mm(out, A("BL", 128 * i, 128 * i + 128), A(src, i, n, 16), i == 0, i == 15)
+
+    def rows2list(out, src, n, kp):
+        for i in range(16):
+            mm(out, A("SelL", 128 * i, 128 * i + 128, p1=kp), A(src, i, n, 16, p1=kp), i == 0, i == 15)
+
+    def chsum(buf, w, cs=range(6), stop=False):
+        for c in cs:
+            mm(A("pb4", 16 * c, 16 * c + 16), A(buf, 128 * c, 128 * c + 128), A(w), False, stop and c == 5)
+
+    def ftsum(col, w):
+        for c in range(6):
+            mm(A("pb6", col + 16 * c, col + 16 * c + 16), A("FB", 128 * c, 128 * c + 128), A(w), True, True)
+
+    dma("s", A("R", 0, G), HB(T.reach[:, 0:G])); dma("y", A("ci"), HB(T.cand[:]))
+    dma("s", A("P", 0, G), HB(T.past[:, 0:G])); dma("y", A("X"), HB(T.x[:]))
+    dma("s", A("R", G, V), HB(T.reach[:, G:V])); dma("y", A("thr", p1=1), HB(T.th[:]))
+    dma("s", A("P", G, V), HB(T.past[:, G:V])); dma("y", A("si"), HB(T.succ[:]))
+    dma("y", A("RF", 0, V), HB(T.reach[:])); dma("y", A("PF", 0, V), HB(T.past[:]))
+
+    iota(A("pi"), [[0, 1]], 0, 1)
+    ms(A("ones"), 1.0)
+    iota(A("gmi"), [[0, 2], [1, 8]], 0, 0)
+    iota(A("mi16"), [[1, 16]], 0, 0, True)
+    iota(A("mI"), [[1, 128]], 0, 0)
+    iota(A("VL", 0, 16), [[64, 16]], 0, 0, True); iota(A("VL", 16, 32), [[16, 16]], 1024, 0, True)
+    send(A("R", 0, G), A("RF", V, V + G), A("RF", V + G, W), "iR", "li")
+    send(A("P", 0, G), A("PF", V, V + G), A("PF", V + G, W), "iP", "li")
+    arrive("iR", 2 * ne, [A("RF", V, W)]); arrive("iP", 2 * ne, [A("PF", V, W)])
+    sel(A("xF", 0, V), A("X"), [[0, 256], [1, 4]], ALU.not_equal, BIGX, 0, 0)
+    ts(A("gi"), A("pi"), 4, ALU.arith_shift_right); ts(A("ii"), A("pi"), 15, ALU.bitwise_and)
+    ts(A("ei"), A("gi"), 1, ALU.bitwise_and)
+    cp("v", A("modd"), A("ei")); cp("v", A("iF"), A("ii")); cp("v", A("gf"), A("gi")); cp("v", A("gm"), A("gmi"))
+    ts(A("meven"), A("modd"), -1.0, ALU.mult, 1.0, ALU.add)
+    ts(A("gm"), A("gm"), A("gf"), ALU.is_equal)
+    ts(A("selD"), A("gm"), 1024.0, ALU.mult); ts(A("selO"), A("gm"), 8388608.0, ALU.mult)
+    ms(A("xF", V, W), BIGX)
+    ms(A("cb", 0, 1), -10.0 * EQ); ms(A("cb", 1, 2), 1.0)
+    ts(A("mi16"), A("mi16"), A("iF"), ALU.is_equal)
+    ts(A("sj"), A("mi16"), -2.0, ALU.mult, 1.0, ALU.add)
+    ts(A("c64"), A("iF"), 8.0, ALU.is_lt, 63.0, ALU.mult); ts(A("c64"), A("c64"), 1.0, ALU.add)
+    ts(A("il1"), A("iF"), 10.0, ALU.is_lt)
+    ts(A("IB", 0, 1), A("il1"), -1.0, ALU.mult)
+    ms(A("EK"), 0.0)
+    ts(A("mG"), A("mI"), 4, ALU.arith_shift_right); cp("v", A("mGf"), A("mG")); ts(A("B16"), A("mGf"), A("gf"), ALU.is_equal)
+    ts(A("CfE", 0, 256), A("ci", 0, V, 4), A("meven"), ALU.mult)
+    ts(A("CfO", 0, 256), A("ci", 0, V, 4), A("modd"), ALU.mult)
+    for i in range(16):
+        cp("s" if i < 11 else "v", A("D1", i, 512, 32), A("CfE", i, 256, 16))
+    for i in range(16):
+        cp("v", A("D1", 16 + i, 512, 32), A("CfO", i, 256, 16))
+    turn()
+    dup("s", "xv2", "X", 0)
+    for k in range(16):
+        cp("s", A("EK", 128 * k + k, 128 * k + 128, 16), A("B16", k, 128, 16))
+    for j in range(10):
+        act(A("IB", 2 ** j, 2 ** (j + 1)), A("IB", 0, 2 ** j), AF.Copy, scale=A("sj", j, j + 1))
+    for k in range(16):
+        tt(A("ckf", 16 * k, 16 * k + 16), A("T1", k, 512, 32), A("T1", 16 + k, 512, 32), ALU.add)
+    cp("v", A("CK0"), A("ckf"))
+    for kk in range(7):
+        xgather(0, kk)
+    halves(0, 0); halves(0, 1)
+    dma("y", A("SelL", p1=8), (T.EK[0:128:16, :], A("EK")[1])); dma("y", A("SelL", p0=8, p1=16), (T.EK[0:128:16, :], A("EK")[1]))
+    ms(A("rows2"), 0.0)
+    sel(A("E0"), A("ones", 0, 128), [[0, 128]], ALU.is_equal, 0.0, 0, 1)
+    iota(A("kc"), [[64, 16], [0, 32]], 0, 0, True)
+    for hv in range(4):
+        sel(A("RH", 512 * hv, 512 * hv + 512), A("ones"), [[-1, 16], [-16, 16], [4096, 2]], ALU.is_equal, 0.0, 128 * (hv % 2) - 4096 * (hv // 2), 1)
+    sel(A("I"), A("ones", 0, 128), [[-1, 128]], ALU.is_equal, 0.0, 0, 1)
+    sel(A("nI"), A("I"), [[-1, 128]], ALU.not_equal, -1.0, 0, 1)
+    xscalar(0, 7)
+    for kk in range(7):
+        xabs(kk)
+    act(A("ab", 3584, 4096), A("pb3"), AF.Abs)
+    iota(A("SN", p1=65), [[0, 128]], 0, 0, True)
+    sel(A("SN", p1=65), A("SN", p1=65), [[1, 8], [0, 16]], ALU.not_equal, -32768.0, 16, -1)
+    iota(A("rows2", p0=32, p1=33), [[1, 256]], 0, 0, True)
+    op("g", lambda e: e.partition_broadcast(A("thb")[0], A("thr", p1=1)[0], 128), [A("thr")], [A("thb")])
+    iota(A("VR"), [[0, 6], [1, 2], [0, 8]], 0, 0, True); iota(A("CC"), [[128, 6], [0, 16]], 128, 0, True)
+    keyinit()
+    for kk in range(8):
+        keymm(kk, "ab", "selD")
+
+    def later():
+        cp("v", A("CF"), A("ci"))
+        ms(A("pw"), 0.0)
+        for i in range(10):
+            ms(A("pw", i, i + 1), 2.0 ** (i - 1))
+        tt(A("mp"), A("mi16"), A("pw"), ALU.mult); rsum(A("wcol"), A("mp"))
+        ms(A("zb"), 0.0)
+        ms(A("rows2", p0=64, p1=65), 1.0)
+        for n in ("SA", "SB"):
+            ms(A(n, p1=65), 0.0)
+        ms(A("rst"), 0.0)
+        for n, r, i, w in (("SA", 32, 12, 1.0), ("SA", 64, 13, 1.0), ("SA", 64, 14, 1.0), ("SA", 64, 15, 1.0), ("SB", 64, 10, 4096.0), ("SB", 64, 11, 256.0), ("SB", 64, 12, 1.0), ("SB", 32, 15, -1.0)):
+            ms(A(n, i, 128, 16, p0=r, p1=r + 1), w)
+        for n, c, i, w in (("SA", 0, 10, 1.0), ("SA", 8, 11, 1.0), ("SB", 0, 13, -4096.0), ("SB", 8, 14, -256.0)):
+            ts(A(n, i, 128, 16, p1=16), A("I", c, c + 8, p1=16), w, ALU.mult)
+        ms(A("rst", 0, 1024, 16), 1000.0)
+        ms(A("thT"), 1.0); ms(A("thT", 0, 16, 2), 10.0 * EQ + 1.0)
+        sel(A("U"), A("ones", 0, 128), [[1, 128]], ALU.is_ge, 0.0, 0, -1)
+        dma("y", A("FB", 0, V), A("IB"))
+        ts(A("bI"), A("I"), EQ, ALU.mult)
+        ts(A("oki"), A("ii"), 1, ALU.bitwise_and); cp("v", A("okc"), A("oki")); ts(A("ekc"), A("okc"), -1.0, ALU.mult, 1.0, ALU.add)
+        for h in (0, 1):
+            ts(A("thK", h, 16, 2), A("thb"), 1024.0, ALU.mult)
+        cp("v", A("thC"), A("thK"))
+        ts(A("i4c"), A("iF"), 4.0, ALU.mult)
+        ts(A("VL", 16, 32), A("VL", 16, 32), A("iF"), ALU.add)
+        for t in (1, 2, 3):
+            ts(A("VL", 32 * t, 32 * t + 16), A("VL", 0, 16), A("i4c"), ALU.add, float(t), ALU.add)
+            cp("v", A("VL", 32 * t + 16, 32 * t + 32), A("VL", 16, 32))
+        ts(A("VL", 0, 16), A("VL", 0, 16), A("i4c"), ALU.add)
+        cp("v", A("SO"), A("si"))
+
+    def later1():
+        act(A("SE"), A("SO"), AF.Copy, scale=A("ekc"))
+        act(A("SO"), A("SO"), AF.Copy, scale=A("okc"))
+        cp("v", A("SL0"), A("si", 0, V, 2))
+        cp("s", A("SLB", 0, 128), A("IB", G, G + 128))
+
+    def later2():
+        cp("v", A("SL1"), A("si", 1, V, 2))
+        cp("v", A("pf"), A("pi"))
+        ts(A("c7"), A("iF"), 7.0, ALU.is_lt); tt(A("wlo"), A("c7"), A("wcol"), ALU.mult); tt(A("whi"), A("wcol"), A("wlo"), ALU.subtract)
+        ts(A("c8"), A("iF"), 8.0, ALU.is_ge); tt(A("fhc"), A("c8"), A("il1"), ALU.mult)
+        ts(A("wF"), A("wcol"), 16384.0, ALU.mult); ts(A("wFn"), A("wcol"), -16384.0, ALU.mult)
+        ms(A("mone"), -1.0)
+        cp("s", A("selp"), A("gm"))
+        for o, w in (("seln", "mone"), ("sFp", "wF"), ("sFn", "wFn"), ("FH", "fhc")):
+            act(A(o), A("gm"), AF.Copy, scale=A(w))
+        act(A("FS", 0, 8), A("gm", 0, 8), AF.Copy, scale=A("wlo")); act(A("FS", 8, 16), A("gm", 8, 16), AF.Copy, scale=A("whi"))
+        ts(A("V0"), A("VR"), -1.0, ALU.mult, 1.0, ALU.add)
+        tt(A("CC"), A("VR"), A("CC"), ALU.mult); ts(A("VR"), A("V0"), A("pf"), ALU.mult); tt(A("NG"), A("CC"), A("VR"), ALU.add); tt(A("NG1"), A("NG"), A("V0"), ALU.add)
+        ts(A("kI"), A("I"), -1024.0, ALU.mult)
+        ftsum(0, "FS"); cp("v", A("FpT"), A("pb6", 0, 96))
+        for s, d in (("RF", "GR"), ("PF", "GP")):
+            dma("y", A(d + "a", 0, G), A(s, V, V + G)); dma("y", A(d + "b", 0, G), A(s, V + G, W))
+
+    for t in range(ROUNDS):
+        last = t == ROUNDS - 1
+        ckt = "CK%d" % t; u = t + 1
+        if t == 0:
+            dup("s", "Pv2", "P", t); dup("s", "Rv2", "R", t)
+        nsp = NS_P[t]; first = [True]
+
+        def vchunk(n, kk):
+            s = (512 * kk, 512 * kk + 512); off = A(ckt, 32 * kk, 32 * kk + 32)
+            if n == "oR":
+                tt(A("oR", *s), IND(A("RF"), off), A("Pv2"), ALU.is_le)
+            else:
+                tt(A("oP", *s), IND(A("PF"), off), A("Rv2"), ALU.is_ge)
+
+        def pgather(kk):
+            s = (512 * kk, 512 * kk + 512)
+            cp("s", A("pc", *s), IND(A("PF"), A(ckt, 32 * kk, 32 * kk + 32)))
+            bank = A("pb%d" % (2 + kk % 2))
+            mm(bank, A("I"), A("pc", *s), True, False); mm(bank, A("nI"), A("Rv2"), False, True)
+
+        def prelu(kk):
+            act(A("oP", 512 * kk, 512 * kk + 512), A("pb%d" % (2 + kk % 2)), AF.Relu, bias=A("cb", 1, 2))
+
+        def olist(kk):
+            for k in (2 * kk, 2 * kk + 1):
+                for n in ("oR", "oP"):
+                    mm(A("pb7", 0, 256), A("EK", 128 * k, 128 * k + 128), A(n, 256 * k, 256 * k + 256), first[0], False)
+                    first[0] = False
+        work = [(n, kk) for kk in range(8) for n in ("oR", "oP") if n == "oR" or kk not in nsp]
+        ev = [(i + 1.0, 0, n, kk) for i, (n, kk) in enumerate(work)]
+        ev += [(1.7 * j + 1.0, 1, "g", kk) for j, kk in enumerate(nsp)] + [(1.7 * j + 2.8, 2, "r", kk) for j, kk in enumerate(nsp)]
+        left = {0: 16, 1: 16}
+        for _, _, n, kk in sorted(ev):
+            if n == "g":
+                pgather(kk)
+                continue
+            if n == "r":
+                prelu(kk)
+            else:
+                vchunk(n, kk)
+            n = "oP" if n == "r" else n
+            left[kk // 4] -= 2
+            keymm(kk, n, "selO", left[kk // 4] == 0)
+        if t == 0:
+            later()
+            act(A("CfE"), A("CF"), AF.Copy, scale=A("meven")); act(A("CfO"), A("CF"), AF.Copy, scale=A("modd"))
+            act(A("BL"), A("EK"), AF.Copy, scale=A("wcol"))
+            cklist_d(1)
+        if not last:
+            halves(u, 0); halves(u, 1)
+        cp("s", A("ka"), A("pb0", 0, 256))
+        tt(A("t1"), A("pb1", 0, 256), A("ka"), ALU.min)
+        tt(A("wk", 0, 128), A("t1", 0, 128), A("t1", 128, 256), ALU.min)
+        tt(A("wk", 128, 192), A("wk", 0, 64), A("wk", 64, 128), ALU.min)
+        tt(A("wk", 192, 224), A("wk", 128, 160), A("wk", 160, 192), ALU.min)
+        m0 = A("wk", 192, 208)
+        ts(A("wi", 0, 32), A("wk", 192, 224), 16777215.0, ALU.min)
+        ts(A("wk", 224, 256), A("wk", 192, 224), HASLIM, ALU.is_lt)
+        ts(A("wi", 32, 64), A("wi", 0, 32), 63, ALU.bitwise_and)
+        tt(A("dec"), A("wi", 32, 64), A("wk", 224, 256), ALU.mult)
+        for h in (0, 1):
+            mm(A("pb5", 128 * h, 128 * h + 128, p1=16), A("dec", h, 32, 2), A("I"), True, True)
+        act(A("rowsN", p1=16), A("pb5", 0, 256, p1=16), AF.Copy, scale=A("c64", p1=16))
+        rows2list(A("pb6", 0, 16), "rowsN", 256, 16)
+        tt(A("wk", 272, 288), m0, A("thC"), ALU.is_ge)
+        ts(A("wk", 304, 320), m0, 4095.0 * 1024, ALU.min)
+        ts(A("wk", 288, 304), A("wk", 272, 288), 4095.0 * 1024, ALU.mult)
+        ts(A("dec2", 32, 48), m0, HASLIM, ALU.is_ge)
+        tt(A("wi", 64, 80), A("wk", 288, 304), A("wk", 304, 320), ALU.max)
+        ts(A("wi", 80, 96), A("wi", 64, 80), 14, ALU.arith_shift_right)
+        ts(A("wi", 112, 128), A("wi", 64, 80), 10, ALU.arith_shift_right)
+        ts(A("wi", 96, 112), A("wi", 112, 128), 15, ALU.bitwise_and)
+        cp("v", A("dec2", 0, 32), A("wi", 80, 112))
+        for h in (0, 1):
+            mm(A("pb2", 128 * h, 128 * h + 128, p1=24), A("dec2", h, 48, 2), A("I"), True, True)
+        cp("s", A("rows2", p1=24), A("pb2", 0, 256, p1=24))
+        cp("v", A("nl"), A("pb6", 0, 16))
+        cp("v", A("bits"), IND(A("FB", 0, V), A("nl")))
+        tt(A("wk", 320, 336), A("wk", 272, 288), A("thT"), ALU.mult)
+        tt(A("thA"), A("thT"), A("wk", 320, 336), ALU.subtract); ts(A("thA"), A("thA"), 1.0, ALU.subtract)
+        mm(A("pb5", 0, 256), A("SA", p1=65), A("rows2", p1=65), True, False); mm(A("pb6", 0, 256), A("SB", p1=65), A("rows2", p1=65), True, False)
+        mm(A("pb5", 0, 256), A("I"), A("bits"), False, True); mm(A("pb6", 0, 256), A("bI"), A("bits"), False, True)
+        ts(A("Ae"), A("pb5", 0, 256), A("meven"), ALU.mult)
+        cp("s", A("Bk"), A("pb6", 0, 256))
+        ts(A("Ao"), A("pb5", 0, 256), A("modd"), ALU.mult)
+        for gp in range(4):
+            for e in (0, 1):
+                for h in (0, 1):
+                    mm(A("pb%d" % (2 * h + gp % 2), 256 * e, 256 * e + 256), A(("Ae", "Ao")[e], 128 * h, 128 * h + 128, p0=32 * gp, p1=32 * gp + 32), A("Bk", p0=32 * gp, p1=32 * gp + 32), True, True)
+            for e in (0, 1):
+                gg = 2 * gp + e
+                bk = A("pb%d" % (gp % 2), 256 * e, 256 * e + 256)
+                op("v", lambda q, bk=bk, gg=gg: q.tensor_reduce(out=A("mx", 2 * gg, 2 * gg + 1)[0], in_=bk[0], axis=AxisListType.X, op=ALU.max), [bk], [A("mx", 2 * gg, 2 * gg + 1)])
+                act(A("tr", 256 * e, 256 * e + 256), A("pb%d" % (2 + gp % 2), 256 * e, 256 * e + 256), AF.Relu, bias=A("cb", 0, 1), accum=A("mx", 2 * gg + 1, 2 * gg + 2))
+        bits2list(A("pb5", 0, 16), "bits", 256)
+        tt(A("win"), A("mx"), A("thA"), ALU.is_le)
+        ts(A("bl"), A("pb5", 0, 16), 511.5, ALU.add)
+        for d, bank in ((0, "pb5"), (256, "pb0")):
+            for h in (0, 1):
+                mm(A(bank, 128 * h, 128 * h + 128, p1=8), A("win", h, 16, 2), A("I"), True, True)
+        tt(A("bd", 0, 16), A("bl"), A("VL", 32 * t, 32 * t + 16), ALU.subtract); tt(A("bd", 16, 32), A("bl"), A("VL", 32 * t + 16, 32 * t + 32), ALU.subtract)
+        cp("s", A("rowsW", 0, 256, p1=8), A("pb5", 0, 256, p1=8)); cp("v", A("rowsW", 256, 512, p1=8), A("pb0", 0, 256, p1=8))
+        rows2list(A("pb6", 0, 32), "rowsW", 512, 8)
+        if t == 0:
+            later1()
+        cp("v", A("bu"), A("bl"))
+        tt(A("dC"), IND(A("CF"), A("bu")), A("ci", t, V, 4), ALU.subtract)
+        tt(A("bq"), A("pb6", 0, 32), A("bd"), ALU.mult)
+        tt(A("bq2"), A("bq"), A("VL", 32 * t, 32 * t + 32), ALU.add)
+        cp("v", A("LL"), A("bq2"))
+        be, bt = A("LL", 0, 16), A("LL", 16, 32)
+        if not last:
+            if t == 0:
+                later2()
+            mm(A("pb4", 0, 96), A("zb"), A("rst", 0, 96), True, False)
+            chsum("R", "selp"); chsum("P", "seln"); chsum("FB", "sFn")
+        cp("v", IND(A("FB"), bt), A("IB", t, V, 4))
+        bits2list(A("pb5", 0, 64), "FB", V)
+        tt(A("Rn"), IND(A("R"), be), A("Rv2", 0, 256), ALU.min)
+        cp("s", A("R", t, V, 4), A("Rn"))
+        tt(A("sn"), IND(A("SO"), be), A("SE", t, V, 4), ALU.add)
+        cp("v", A("SL%d" % (t % 2), t // 2, 512, 2), A("sn"))
+        ts(A("FL"), A("pb5", 0, 64), 511.5, ALU.add)
+        cp("v", A("RF", 0, 512), IND(A("R"), A("FL", 0, 32))); cp("s", A("RF", 512, V), IND(A("R"), A("FL", 32, 64)))
+        par = t % 2
+
+        def g3(q, c):
+            cp(q, A("g3", 1024 * c, 1024 * c + 1024), IND(A("RF"), A("SL%d" % par, 64 * c, 64 * c + 64)))
+
+        def s3(c):
+            s = (1024 * c, 1024 * c + 1024)
+            op("v", lambda e: e.tensor_tensor_scan(out=A("s3", *s)[0], data0=A("rst")[0], data1=A("g3", *s)[0], initial=0.0, op0=ALU.max, op1=ALU.min), [A("rst"), A("g3", *s)], [A("s3", *s)])
+        tt(A("xs"), IND(A("X"), be), A("xv2", 0, 256), ALU.add)
+        if not last:
+            tt(A("Pn"), IND(A("P"), be), A("Pv2", 0, 256), ALU.max)
+        for c in range(NV3, 8):
+            g3("s", c)
+            if c == NV3 and not last:
+                cp("s", A("P", t, V, 4), A("Pn"))
+        ts(A("xi"), A("xs"), -0.5, ALU.add, 0.5, ALU.mult)
+        cp("v", A("X", t, V, 4), A("xi"))
+        if last:
+            dma("y", HB(T.yx[:]), A("X"))
+        else:
+            sel(A("xm"), A("X"), [[0, 256], [1, 4]], ALU.not_equal, BIGX, -u, 0)
+        for c in range(NV3):
+            g3("v", c)
+        if not last:
+            mm(A("pb6", 192, 208), A("ones", 0, 128), A("win"), True, True)
+            ftsum(0, "FS"); ftsum(96, "FH")
+            chsum("FB", "sFp"); chsum("P", "selp")
+            rsum(A("Mf"), A("pb6", 192, 208))
+            ts(A("xw", 0, 96), A("pb6", 96, 192), 1.0, ALU.is_lt)
+            tt(A("dF"), A("pb6", 0, 96), A("FpT"), ALU.subtract)
+            tt(A("dF"), A("dF"), A("xw", 0, 96), ALU.mult)
+            cklist_t()
+        for kk in range(8):
+            olist(kk)
+        mm(A("pb7", 0, 256), A("SN", p1=65), A("rows2", p1=65), False, True)
+
+        def cupdate():
+            tt(A("oi"), A("oi"), A("dC"), ALU.mult)
+            tt(A("CF", t, V, 4), A("oi"), A("CF", t, V, 4), ALU.add)
+        for c0, c1 in ((0, 5), (5, 8)):
+            for c in range(c0, c1):
+                s3(c)
+            if c0 == 0 and last:
+                ts(A("oi"), A("pb7", 0, 256), 0.0, ALU.is_gt); cupdate()
+                dma("y", HB(T.yc[:]), A("CF"))
+            o = A("R", par + 128 * c0, 128 * c1, 2)
+            tt(o, A("s3", 1024 * c0 + 15, 1024 * c1, 16), o, ALU.min)
+            if not last:
+                chsum("R", "seln", range(c0, min(c1, 6)), c1 == 8)
+            else:
+                dma("sy"[c0 // 5], HB(T.yr[:, 128 * c0:128 * c1]), A("R", 128 * c0, 128 * c1))
+        if last:
+            break
+        cp("s", A("xF", 0, V), IND(A("xm"), A("FL")))
+        dup("s", "xv2", "X", u); dup("s", "Pv2", "P", u)
+        ts(A("ch"), A("pb4", 0, 96), 0.0, ALU.not_equal)
+        mm(A("pb5", 0, 96), A("U"), A("ch"), True, False)
+        for s in range(1, 6):
+            mm(A("pb5", 16 * s, 96), A("ones", 0, 128), A("ch", 0, 96 - 16 * s), False, False)
+        mm(A("pb5", 0, 96), A("kI"), A("ch"), False, True)
+        tt(A("chz"), A("ch"), A("V0"), ALU.mult)
+        mm(A("pb6", 0, 96), A("nI"), A("NG1"), True, False)
+        mm(A("pb6", 0, 96), A("U"), A("chz"), False, False)
+        for s in range(1, 6):
+            mm(A("pb6", 16 * s, 96), A("ones", 0, 128), A("chz", 0, 96 - 16 * s), False, s == 5)
+        cp("v", A("Mi"), A("Mf")); ts(A("Mj"), A("Mi"), 31, ALU.bitwise_and)
+        ts(A("xw", 96, 192), A("pb5", 0, 96), 128.0 - 1024.0, ALU.is_le)
+        tt(A("pos"), A("pb6", 0, 96), A("xw", 96, 192), ALU.mult)
+
+        def torows(src, rows, b0, b1, q, more=None):
+            for c in range(6):
+                bank, o = ((b0, 128 * c) if c < 4 else (b1, 128 * c - 512))
+                mm(A(bank, o, o + 128, p1=16), A(src, 16 * c, 16 * c + 16), A("I"), True, more is None)
+                if more is not None:
+                    mm(A(bank, o, o + 128, p1=16), A(more, 16 * c, 16 * c + 16), A("I"), False, True)
+            cp("s", A(rows, 0, 512, p1=16), A(b0, 0, 512, p1=16)); cp(q, A(rows, 512, G, p1=16), A(b1, 0, 256, p1=16))
+        tt(A("xw", 480, 576), A("dF"), A("xw", 96, 192), ALU.mult)
+        torows("pos", "rowsP", "pb5", "pb6", "v", "NG")
+        ts(A("oi"), A("pb7", 0, 256), 0.0, ALU.is_gt)
+        rows2list(A("pb7", 0, 48), "rowsP", G, 16)
+        cp("v", A("CK%d" % u), A("ckf"))
+        tt(A("FpT"), A("FpT"), A("xw", 480, 576), ALU.add)
+        cp("v", A("Fpb"), A("FpT"))
+        xgather(u, 0)
+        cp("v", A("pl"), A("pb7", 0, 48))
+        torows("Fpb", "rowsF", "pb2", "pb3", "s")
+        rows2list(A("pb5", 0, 48), "rowsF", G, 16)
+        cp("v", IND(A("SLB"), A("pl")), A("IB", 0, G))
+        bits2list(A("pb7", 0, 8), "SLB", 128)
+        sp, sll = "SRP%d" % t, "SLL%d" % t
+        ts(A(sll, 8, 56), A("pb5", 0, 48), 511.5, ALU.add)
+        xabs(0)
+        cp("s", A("PF", 0, V), IND(A("P"), A("FL")))
+        ts(A("Mk"), A("Mj"), 1024.0, ALU.mult); ts(A("thC"), A("thK"), A("Mk"), ALU.add)
+        ts(A(sll, 0, 8), A("pb7", 0, 8), 511.5, ALU.add)
+        cp("v", A(sp, 0, 128), IND(A("R"), A(sll, 0, 8))); cp("s", A(sp, 128, 256), IND(A("P"), A(sll, 0, 8)))
+        send(A(sll), A("LLa%d" % t), A("LLb%d" % t), "aL%d" % t)
+        send(A(sp), A("LRa%d" % t), A("LRb%d" % t), "aR%d" % t)
+        arrive("aR%d" % t, 2 * ne, [A("LRa%d" % t), A("LRb%d" % t)]); arrive("aL%d" % t, 2 * ne, [A("LLa%d" % t), A("LLb%d" % t)])
+        cp("s", A("SLB", 0, 128), A("IB", G, G + 128))
+        cp("s", A("RF", 0, V), IND(A("R"), A("FL")))
+        for kk in range(1, 8):
+            if kk in NX_S:
+                xscalar(u, kk)
+            else:
+                xgather(u, kk)
+        for kk in range(1, 8):
+            if kk in NX_S:
+                act(A("ab", 512 * kk, 512 * kk + 512), A("pb%d" % (2 + kk % 2)), AF.Abs)
+            else:
+                xabs(kk)
+        dup("s", "Rv2", "R", u)
+        act(A("SO", t, V, 4), A("sn"), AF.Copy, scale=A("okc"))
+        keyinit()
+        for kk in range(8):
+            keymm(kk, "ab", "selD")
+        cupdate()
+        if u + 1 < ROUNDS:
+            cklist_d(u + 1)
+        ll = {d: "LL%s%d" % (d, t) for d in "ab"}
+        for k, tb in ((1, "GP"), (0, "GR")):
+            for d in "ab":
+                cp("v", IND(A(tb + d), A(ll[d], 0, 8)), A("LR%s%d" % (d, t), 128 * k, 128 * k + 128))
+        for k, d in enumerate("ab"):
+            cp("s", A("PF", V + G * k, V + G * k + G), IND(A("GP" + d), A(ll[d], 8, 56)))
+        cp("v", A("RF", V, V + G), IND(A("GRa"), A(ll["a"], 8, 56)))
+        cp("v", A("RF", V + G, V + G + 384), IND(A("GRb"), A(ll["b"], 8, 32)))
+        cp("s", A("RF", V + G + 384, W), IND(A("GRb"), A(ll["b"], 32, 56)))
+
+    for s, v in total.items():
+        g.wait_ge(T.sem[s], v)

@@ -4,637 +4,595 @@ from concourse.mybir import AluOpType as ALU, AxisListType, ActivationFunctionTy
 
 V, G, W, N, ROUNDS = 1024, 768, 2560, 4, 4
 BIGX = 8192.0
-HASLIM = 4100.0 * 1024
 EQ = 1048576.0
-NS_P = ((0, 1, 2, 3, 4, 5, 6, 7),) + ((3, 4, 5, 6, 7),) * 3
-NX_S = ()
-NV3 = 1
+ORD = 2.0 ** 30
+HUGE = 2.0 ** 80
+CMP_S = ((3, 4, 5, 6, 7),) + ((2, 3, 4, 5, 6, 7),) * 3
+ABS_V = ((), (), (), ())
+X_S = ((7,), (), (), ())
+G3_V = ((0, 1, 2),) * 3 + ((0, 1, 2, 3, 4),)
+GH_V = (("R", "a"),)
 
 b, f, i4, u2 = "bfloat16", "float32", "int32", "uint16"
 _S = {
-    "X": (1024, b), "R": (1024, b), "P": (1024, b), "xF": (2560, b), "RF": (2560, b), "PF": (2560, b), "xm": (1024, b),
-    "FB": (1280, b), "IB": (1024, b), "ni": (256, i4),
-    "ci": (1024, i4), "si": (1024, i4), "CF": (1024, f), "CfE": (1024, f), "CfO": (1024, f), "NHI": (256, b), "NLO": (256, b),
-    "SO": (1024, f), "SE": (1024, f), "SL0": (512, u2), "SL1": (512, u2),
-    "D1": (512, f), "T1": (512, f), "T2": (496, f), "ckf": (256, f), "CK0": (256, u2), "CK1": (256, u2), "CK2": (256, u2), "CK3": (256, u2),
-    "ones": (512, b), "I": (128, b), "nI": (128, b), "bI": (128, b), "U": (128, b), "E0": (128, b), "B16": (128, b),
-    "EK": (2048, b), "BL": (2048, b), "SelL": (2048, b), "RH": (2048, b), "kc": (512, b), "rst": (1024, b),
-    "SA": (128, b), "SB": (128, b), "SN": (128, b), "rows2": (256, b), "zb": (128, b),
-    "selD": (16, b), "selO": (16, b), "selp": (16, b), "seln": (16, b), "sFp": (16, b), "sFn": (16, b), "FS": (16, b), "FH": (16, b), "gm": (16, f),
-    "gmi": (16, i4), "mi16": (16, f), "mp": (16, f), "pw": (16, f), "sj": (16, f),
-    "pi": (1, i4), "gi": (1, i4), "ii": (1, i4), "ei": (1, i4), "oki": (1, i4), "mI": (128, i4), "mG": (128, i4), "mGf": (128, f),
-    "pf": (1, f), "gf": (1, f), "iF": (1, f), "i4c": (1, f), "modd": (1, f), "meven": (1, f), "okc": (1, f), "ekc": (1, f),
-    "wcol": (1, f), "il1": (1, f), "wlo": (1, f), "whi": (1, f), "wF": (1, f), "wFn": (1, f), "fhc": (1, f), "c7": (1, f), "c8": (1, f), "mone": (1, f), "c64": (1, f),
-    "cb": (2, f), "VL": (128, f), "VR": (96, f), "CC": (96, f), "V0": (96, f), "NG": (96, b), "NG1": (96, b), "kI": (128, b), "chz": (96, b), "thT": (16, f), "thA": (16, f),
-    "thr": (8, i4), "thb": (8, i4), "thK": (16, f), "thC": (16, f), "Mf": (1, f), "Mi": (1, i4), "Mj": (1, i4), "Mk": (1, f),
-    "xv2": (512, b), "Rv2": (512, b), "Pv2": (512, b), "dx": (4096, b), "ab": (4096, b), "oR": (4096, b), "oP": (4096, b), "pc": (4096, b),
-    "ka": (256, f), "t1": (256, f), "wk": (512, f), "wi": (128, i4), "dec": (32, b), "dec2": (48, b), "rowsN": (256, b), "nl": (16, u2),
-    "bits": (256, b), "Ae": (256, b), "Ao": (256, b), "Bk": (256, b), "tr": (512, b), "mx": (16, f), "win": (16, b), "rowsW": (512, b),
-    "bd": (32, f), "bl": (16, f), "bq": (32, f), "bq2": (32, f), "LL": (32, u2), "bu": (16, u2), "Rn": (256, b), "Pn": (256, b), "xs": (256, f), "xi": (256, i4),
-    "sn": (256, f), "FL": (64, u2), "g3": (8192, b), "s3": (8192, b), "oi": (256, f), "dC": (256, f),
-    "ch": (96, b), "xw": (768, f), "pos": (96, b), "FpT": (96, f), "dF": (96, f), "Fpb": (96, b), "rowsP": (768, b), "rowsF": (768, b), "pl": (48, u2), "SLB": (896, b),
+    "R": (3072, b), "P": (3072, b), "XM": (3072, b), "xF": (W, b), "RF": (W, b), "PF": (W, b), "FB": (3072, b), "IB": (V, b),
+    "ci": (1152, i4), "CF": (3072, f), "SO": (3072, i4), "SE": (V, i4), "si": (V, i4), "SL0": (512, u2), "SL1": (512, u2),
+    "T1": (544, i4), "CK0": (256, u2), "CK1": (256, u2), "CK2": (256, u2), "CK3": (256, u2), "NH": (256, b),
+    "dx": (4096, b), "ab": (4096, b), "oR": (4096, b), "oP": (4096, b), "pc": (4096, b), "g3": (8192, b), "s3": (8192, b),
+    "ks": (512, f), "rst": (1024, b), "dk": (1024, b), "Wn": (512, b), "DM": (512, b), "KD": (512, b),
+    "Kr": (256, b), "Ae": (256, b), "Ao": (256, b), "Bk": (256, b), "tr": (256, b), "W2": (256, b), "fl": (256, b),
+    "Rn": (256, b), "Pn": (256, b), "xs": (256, f), "xi": (256, i4), "sn": (256, f), "dC": (256, f), "oi": (256, f),
+    "rs56": (448, b), "sv": (448, b), "f1": (448, b), "f2": (448, b), "f3": (128, b), "srow": (128, b),
+    "col": (144, b), "EK": (144, b), "nEK": (144, b), "BL": (144, b), "BL8": (144, b),
+    "ones": (128, b), "I": (128, b), "nI": (128, b), "I32": (128, f), "n64I": (128, b), "kI": (128, b), "I16": (128, b), "hI": (128, b),
+    "B16": (128, b), "nB16": (128, b), "nLs": (128, b), "gcol": (128, b),
+    "wi": (32, i4), "wn": (32, i4), "wd": (64, i4), "wD": (32, i4), "mx": (32, f), "thr": (32, f), "thb": (32, f), "nb": (32, f), "bs": (8, f),
+    "lose": (32, b), "thK": (32, f), "thC": (32, f), "th1": (8, i4), "th2": (8, i4), "Mf": (1, f), "Mi": (1, i4), "Mj": (1, i4), "Mk": (1, f),
+    "blf": (16, f), "btf": (16, f), "nh": (16, f), "nh2": (16, f), "buf": (16, f), "dl": (64, f), "FLf": (48, f), "dF": (48, f), "dF1": (48, f), "dF2": (48, f),
+    "Fp": (48, f), "go": (48, f), "go2": (48, f), "Wo": (48, f), "ch": (56, b), "cc": (56, b), "cw": (56, f),
+    "TL": (16, u2), "EXn": (32, u2), "EXw": (16, u2), "nl": (16, u2), "bt": (16, u2), "bu": (16, u2), "FL": (64, u2), "cu": (8, u2), "sl": (8, u2),
+    "gm": (16, b), "selD": (16, b), "selD2": (16, b), "selDn": (16, b), "selO": (16, b), "g64": (8, b), "ga": (16, b), "gD": (32, b),
+    "it": (64, i4), "k16": (16, f), "mi": (16, f), "sj": (16, f), "two": (16, f), "pw": (16, f), "wr": (16, f), "mp": (16, f), "mp2": (16, f),
+    "pi": (1, i4), "gi": (1, i4), "ii": (1, i4), "ei": (1, i4), "pa": (1, i4), "pb": (1, i4), "oki": (1, i4),
+    "pf": (1, f), "gf": (1, f), "iF": (1, f), "modd": (1, f), "meven": (1, f), "okc": (1, f), "il": (1, f), "tb": (1, f), "tb2": (1, f), "tb3": (1, f),
+    "wcol": (1, f), "w8": (1, f), "wrow": (1, f), "e15": (1, f), "sAe": (1, f), "sAo": (1, f), "cAe": (1, f), "cAo": (1, f), "ka": (1, f), "kb": (1, f),
+    "p128": (1, f), "c0": (1, f), "c1": (1, f), "one": (1, f), "nord": (1, f), "c128": (1, f),
     "GRa": (896, b), "GRb": (896, b), "GPa": (896, b), "GPb": (896, b),
 }
-_WHERE, _POOL = {}, {f: 0, i4: 0, u2: 0, b: 0}
-SCRATCH = {}
-_OWN = ("nl", "pl", "FL", "LL", "bu", "SelL", "SA", "SB", "SN")
+for _r in range(ROUNDS - 1):
+    for _n in ("MS", "La", "Lb"):
+        _S["%s%d" % (_n, _r)] = (312, u2)
+_WHERE, _POOL, SCRATCH = {}, {f: 0, i4: 0, u2: 0, b: 0}, {}
 for _n, (_c, _d) in _S.items():
-    if _c <= 128 and _n not in _OWN:
+    if _c <= 144:
         _WHERE[_n] = ("pool_" + _d, _POOL[_d]); _POOL[_d] += _c + (-_c) % 16
     else:
         SCRATCH[_n] = ("sbuf", [128, _c], _d); _WHERE[_n] = (_n, 0)
 for _d in _POOL:
-    if _POOL[_d]:
-        SCRATCH["pool_" + _d] = ("sbuf", [128, _POOL[_d]], _d)
-for _r in range(3):
-    for _n, _c, _d in (("SRP%d", 256, b), ("SLL%d", 56, u2), ("LRa%d", 256, b), ("LRb%d", 256, b), ("LLa%d", 56, u2), ("LLb%d", 56, u2)):
-        SCRATCH[_n % _r] = ("sbuf", [128, _c], _d); _WHERE[_n % _r] = (_n % _r, 0)
+    SCRATCH["pool_" + _d] = ("sbuf", [128, _POOL[_d]], _d)
 for _r in range(8):
-    SCRATCH["pb%d" % _r] = ("psum", [128, 512], f); _WHERE["pb%d" % _r] = ("pb%d" % _r, 0)
-ND = 24
-SEMAPHORES = ["qv", "qs", "qt", "qg", "iR", "iP", "loc", "li"] + ["aR%d" % r for r in range(3)] + ["aL%d" % r for r in range(3)] + ["d%d" % k for k in range(ND)]
+    _n = "ps%d" % _r
+    SCRATCH[_n] = ("psum", [128, 512], f); _WHERE[_n] = (_n, 0); _S[_n] = (512, f)
+ND = 28
+SEMAPHORES = ["qv", "qs", "qt", "qg", "iR", "iP", "loc", "li"] + ["a%d" % r for r in range(ROUNDS - 1)] + ["d%d" % k for k in range(ND)]
+
+CYC, GATH, SCAT, TCYC, WAKE, DMA0, DMAB, REM0, REMB = 0.9e-3, 1.5, 3.5, 0.45e-3, 0.1, 1.8, 180e3, 3.0, 70e3
+IDLE, PASSES = 0.5, 6
+_ORDER = {}
+
+
+def meets(a0, a1, st, e0, e1, es):
+    return e0 < a1 and a0 < e1 and (e0 - a0) % math.gcd(st, es) == 0
+
+
+def covers(a0, a1, st, e0, e1, es):
+    return a0 <= e0 and e1 <= a1 and (st == 1 or (es == st and (e0 - a0) % st == 0))
+
+
+def needs(ops):
+    hist, bank, pre = {}, {}, []
+    for me, o in enumerate(ops):
+        need = set(o["after"])
+        for regs, isw in ((o["rd"], False), (o["wr"], True)):
+            for n, a0, a1, st in regs:
+                if n[:2] == "ps":
+                    last, kind, free = bank.get(n, (set(), None, set()))
+                    k = ("add" if o["adds"] else None) if isw else "r" + o["q"]
+                    if k is not None and k == kind:
+                        need |= last; free.add(me)
+                    elif k is not None:
+                        last = (free or last) - {me}; need |= last; bank[n] = (last, k, {me})
+                    else:
+                        need |= free or last; bank[n] = ({me}, None, set())
+                    continue
+                h = hist.setdefault(n, [])
+                need.update(e[3] for e in h if (e[4] or isw) and meets(a0, a1, st, *e[:3]))
+                if isw:
+                    h[:] = [e for e in h if not covers(a0, a1, st, *e[:3])]
+                h.append((a0, a1, st, me, isw))
+        need.discard(me); pre.append(need)
+    return pre
+
+
+def order(ops):
+    pre = needs(ops); n = len(ops)
+    suc = [[] for _ in ops]
+    for i, p in enumerate(pre):
+        for j in p:
+            suc[j].append(i)
+
+    def lag(j, i):
+        if j in ops[i]["after"] and ops[i]["kind"] == "dma":
+            return ops[j]["busy"] - ops[j]["t"]
+        return 0.0 if ops[j]["q"] == ops[i]["q"] == "t" or ops[i]["q"] == "x" else WAKE
+    way = [0.0] * n
+    for i in reversed(range(n)):
+        way[i] = ops[i]["t"] + max([lag(i, k) + way[k] for k in suc[i]], default=0.0)
+    best = None
+    for _ in range(PASSES):
+        out, end = forward(ops, pre, suc, lag, way)
+        if best is None or max(end) < best[0]:
+            best = (max(end), out)
+        way = backward(ops, pre, suc, lag, end)
+    return best[1]
+
+
+def backward(ops, pre, suc, lag, end):
+    n = len(ops); way = [None] * n; left = [len(s) for s in suc]
+    free = {}; open_ = {i: 0.0 for i in range(n) if not suc[i]}
+    while open_:
+        key = lambda i: ops[i]["kind"] or ops[i]["q"]
+        st = {i: max(r, free.get(key(i), 0.0)) for i, r in open_.items()}
+        now = min(st.values())
+        i = max((k for k in open_ if st[k] <= now + 1e-9), key=lambda k: (end[k], k))
+        o = ops[i]; way[i] = now + o["t"]
+        if o["q"] != "x":
+            free[key(i)] = way[i] - o.get("t0", 0.0)
+        del open_[i]
+        for j in pre[i]:
+            left[j] -= 1
+            if left[j] == 0:
+                open_[j] = max(0.0, max(way[k] + lag(j, k) for k in suc[j]))
+    return way
+
+
+def forward(ops, pre, suc, lag, way):
+    n = len(ops)
+    free = {q: 0.0 for q in "vstgyx"}; line = {"dma": 0.0, "rem": 0.0}
+    end = [None] * n; left = [len(p) for p in pre]; open_ = {i for i in range(n) if not pre[i]}; out = []
+
+    def ready(i):
+        return max([end[j] + lag(j, i) if lag(j, i) >= 0 else 0.0 for j in pre[i]], default=0.0)
+
+    def soon(i, depth):
+        t = 0.0
+        for j in pre[i]:
+            if end[j] is not None:
+                t = max(t, end[j] + lag(j, i))
+            elif depth == 0 or ops[j]["q"] == ops[i]["q"]:
+                return None
+            else:
+                s = soon(j, depth - 1)
+                if s is None:
+                    return None
+                t = max(t, max(s, free[ops[j]["q"]]) + ops[j]["t"] + lag(j, i))
+        return t
+    while open_:
+        st = {i: max(ready(i), free[ops[i]["q"]]) for i in open_}
+        now = min(st.values())
+        i = max((k for k in open_ if st[k] <= now + 1e-9), key=lambda k: (way[k], -k))
+        q = ops[i]["q"]
+        if q in "vsg":
+            near = {k: st[k] for k in open_ if ops[k]["q"] == q and way[k] > way[i]}
+            edge = {k for j in open_ if ops[j]["q"] != q for k in suc[j]}
+            edge |= {m for k in edge if ops[k]["q"] != q for m in suc[k]}
+            for k in edge:
+                if ops[k]["q"] == q and way[k] > way[i] and k not in open_:
+                    s = soon(k, 3)
+                    if s is not None:
+                        near[k] = max(s, now)
+            hold = [s for k, s in near.items() if s < now + ops[i]["t"] and
+                    max(s + way[k], s + ops[k]["t"] + way[i]) + IDLE * (s - now) < max(now + way[i], now + ops[i]["t"] + way[k])]
+            if hold and min(hold) > now + 1e-6:
+                free[q] = min(hold); continue
+        o = ops[i]
+        if o["kind"] in line:
+            e = max(now + o["t0"], line[o["kind"]]) + o["t"] - o["t0"]; line[o["kind"]] = e; end[i] = e; free[q] = now + o["busy"]
+        else:
+            end[i] = now + o["t"]; free[q] = end[i] if q != "x" else 0.0
+        out.append(i); open_.discard(i)
+        for k in suc[i]:
+            left[k] -= 1
+            if left[k] == 0:
+                open_.add(k)
+    return out, end
 
 
 def rank_program(g, core, T, topo):
     rank = T.rank_of(core)
     if rank is None:
         return
-    eng = {"v": g.vector, "s": g.scalar, "t": g.tensor, "g": g, "y": g.sync}
-    cnt = {q: 0 for q in eng}; clk = {q: {} for q in eng}; hist = {}; info = []; total = {}; nd = [0]
+    ops = []
 
-    def A(n, c0=0, c1=None, st=1, p0=0, p1=128):
+    def A(n, c0=0, c1=None, st=1, p0=0, p1=128, ps=1):
         t, o = _WHERE[n]
-        if c1 is None:
-            c1 = _S[n][0] if n in _S else SCRATCH[n][1][1]
-        ap = T[t][p0:p1, o + c0:o + c1] if st == 1 else T[t][p0:p1, o + c0:o + c1:st]
-        return (ap, [(n, c0, c1, st)])
+        c1 = _S[n][0] if c1 is None else c1
+        ap = T[t][p0:p1:ps, o + c0:o + c1:st] if ps > 1 or st > 1 else T[t][p0:p1, o + c0:o + c1]
+        return (ap, [(n, c0, c1, st)], len(range(c0, c1, st)), _S[n][1], "")
 
     def IND(w, o):
-        return (w[0].indirect(o[0]), w[1] + o[1])
+        return (w[0].indirect(o[0]), w[1] + o[1], 16 * o[2], w[3], "i")
 
     def HB(ap):
-        return (ap, [])
+        return (ap, [], 0, None, "")
 
-    def covers(a0, a1, st, e):
-        return a0 <= e[0] and e[1] <= a1 and (st == 1 or (e[4] == st and (e[0] - a0) % st == 0))
+    def op(q, call, rd, wr, t, kind="", adds=False, after=(), **more):
+        ops.append(dict(q=q, call=call, rd=[x for r in rd for x in r[1]], wr=[x for r in wr for x in r[1]], t=t, kind=kind, adds=adds, after=after, **more))
+        return len(ops) - 1
 
-    def sync(q, rd, wr, me):
-        need = set()
-        for regs, isw in ((rd, False), (wr, True)):
-            for n, a0, a1, st in regs:
-                ps = n[:2] == "pb"
-                for e in hist.get(n, ()):
-                    over = e[0] < a1 and a0 < e[1] and (e[0] - a0) % math.gcd(st, e[4]) == 0
-                    eq = info[e[2]][0]
-                    if ps:
-                        if eq != q or (over and e[3] and q != "t"):
-                            need.add(e[2])
-                    elif over and (e[3] or isw):
-                        need.add(e[2])
-        for o in sorted(need, reverse=True):
-            _, sem, val, ck = info[o]
-            if clk[q].get(sem, 0) >= val:
-                continue
-            eng[q].wait_ge(T.sem[sem], val)
-            for s, v in list(ck.items()) + [(sem, val)]:
-                if clk[q].get(s, 0) < v:
-                    clk[q][s] = v
-        for regs, isw in ((rd, False), (wr, True)):
-            for n, a0, a1, st in regs:
-                ps = n[:2] == "pb"
-                if ps:
-                    h = [e for e in hist.get(n, ()) if info[e[2]][0] == me[1] and not (covers(a0, a1, st, e) and isw == e[3])]
-                elif isw:
-                    h = [e for e in hist.get(n, ()) if not covers(a0, a1, st, e)]
-                else:
-                    h = [e for e in hist.get(n, ()) if not (not e[3] and covers(a0, a1, st, e) and info[e[2]][0] == q)]
-                h.append((a0, a1, me[0], isw, st)); hist[n] = h
+    def cost(out, a, per):
+        if a[4]:
+            return 0.06 + out[2] * GATH * CYC
+        if out[4]:
+            return 0.05 + a[2] * SCAT * CYC
+        return max(64, out[2] * per) * CYC
 
-    def op(q, call, rd, wr):
-        me = len(info)
-        rr = [x for r in rd for x in r[1]]; ww = [x for r in wr for x in r[1]]
-        info.append((q, "q" + q, cnt[q] + 1, {}))
-        sync(q, rr, ww, (me, q))
-        if q == "g" and clk[q].get("qg", 0) < cnt[q]:
-            g.wait_ge(T.sem["qg"], cnt[q]); clk[q]["qg"] = cnt[q]
-        cnt[q] += 1
-        info[me] = (q, "q" + q, cnt[q], dict(clk[q]))
-        call(eng[q]).then_inc(T.sem["q" + q], 1); total["q" + q] = cnt[q]
+    def half(*x):
+        return 0.5 if all(y[3] in (b, u2) for y in x) else 1
 
-    def dma(q, out, in_):
-        me = len(info); s = "d%d" % nd[0]; nd[0] += 1
-        info.append(("d" + s, s, 16, {}))
-        sync(q, in_[1], out[1], (me, "d" + s))
-        info[me] = ("d" + s, s, 16, dict(clk[q])); total[s] = 16
-        eng[q].dma_start(out=out[0], in_=in_[0]).then_inc(T.sem[s], 16)
+    def in_ps(x):
+        return x[1][0][0][:2] == "ps"
 
-    def arrive(sem, val, regs):
-        me = len(info); info.append(("x", sem, val, {})); total[sem] = val
-        for r in regs:
-            for n, a0, a1, st in r[1]:
-                hist.setdefault(n, []).append((a0, a1, me, True, st))
+    chain = {}
+
+    def dma(q, out, in_, nbytes):
+        chain[q] = op(q, lambda e: e.dma_start(out=out[0], in_=in_[0]), [in_], [out], DMA0 + nbytes / DMAB, "dma", t0=DMA0, busy=0.06, after=[chain[q]] if q in chain else [])
+        ops[chain[q]]["issue"] = True
 
     prev, nxt = T.cores[(rank - 1) % N], T.cores[(rank + 1) % N]
     mk = min(topo.mask(core, prev), topo.mask(core, nxt))
     ne = len([e for e in topo.engines(core, prev) if mk >> e & 1])
+    ids = []
+    for d in (prev, nxt):
+        rid, pid, _ = topo.addr(d); ids.append(DstId(rid=rid, pnc=pid))
 
-    def send(src, to_prev, to_next, sem, loc="loc"):
-        sync("g", src[1], [], (len(info), "x")); info.append(("x", loc, 2 * ne, {}))
-        ids = []
-        for d in (prev, nxt):
-            rid, pid, _ = topo.addr(d); ids.append(DstId(rid=rid, pnc=pid))
-        g.remote_dma_fused([RemoteDMATransfer(dst_ids=ids, dma_engine_mask=mk, remote_sem=T.sem[sem], srcs=[src[0]], dsts=[to_prev[0], to_next[0]])], local_sem=T.sem[loc])
-        total[loc] = total.get(loc, 0) + ne
+    def send(src, to_prev, to_next, sem, loc="loc", first=0.0):
+        call = lambda e: e.remote_dma_fused([RemoteDMATransfer(dst_ids=ids, dma_engine_mask=mk, remote_sem=T.sem[sem], srcs=[src[0]], dsts=[to_prev[0], to_next[0]])], local_sem=T.sem[loc])
+        s = op("g", call, [src], [], REM0 + first + 2 * 256 * src[2] / REMB, "rem", t0=REM0 + first, busy=0.3, loc=loc)
+        op("x", sem, [], [to_prev, to_next], 0.0, after=[s])
 
     def cp(q, out, in_):
         if q == "s":
-            op("s", lambda e: e.activation(out=out[0], in_=in_[0], func=AF.Copy), [in_], [out])
+            act(out, in_, AF.Copy)
+        elif q == "g":
+            sel(out, in_, [[0, out[2]]], ALU.is_equal, 0.0, 0, 0)
         else:
-            op("v", lambda e: e.tensor_copy(out=out[0], in_=in_[0]), [in_], [out])
+            op("v", lambda e: e.tensor_copy(out=out[0], in_=in_[0]), [in_], [out], cost(out, in_, half(out, in_)))
 
     def tt(out, a, c, o):
-        op("v", lambda e: e.tensor_tensor(out=out[0], in0=a[0], in1=c[0], op=o), [a, c], [out])
+        op("v", lambda e: e.tensor_tensor(out=out[0], in0=a[0], in1=c[0], op=o), [a, c], [out], cost(out, a, 1 if in_ps(a) or in_ps(c) else 2))
 
     def ts(out, a, s1, o1, s2=None, o2=None):
         rd = [a] + [s for s in (s1, s2) if isinstance(s, tuple)]
-        v1 = s1[0] if isinstance(s1, tuple) else s1
-        v2 = s2[0] if isinstance(s2, tuple) else s2
-        if o2 is None:
-            op("v", lambda e: e.tensor_scalar(out=out[0], in0=a[0], scalar1=v1, scalar2=None, op0=o1), rd, [out])
-        else:
-            op("v", lambda e: e.tensor_scalar(out=out[0], in0=a[0], scalar1=v1, scalar2=v2, op0=o1, op1=o2), rd, [out])
+        kw = dict(out=out[0], in0=a[0], scalar1=s1[0] if isinstance(s1, tuple) else s1, scalar2=s2[0] if isinstance(s2, tuple) else s2, op0=o1)
+        if o2 is not None:
+            kw["op1"] = o2
+        op("v", lambda e: e.tensor_scalar(**kw), rd, [out], cost(out, a, half(out, a)))
 
     def act(out, in_, fn, bias=None, scale=None, accum=None):
-        kw = {}
-        rd = [in_]; wr = [out]
-        if bias is not None:
-            kw["bias"] = bias[0]; rd.append(bias)
-        if scale is not None:
-            kw["scale"] = scale[0]; rd.append(scale)
+        kw = {}; rd = [in_]; wr = [out]
+        for k, x in (("bias", bias), ("scale", scale)):
+            if isinstance(x, tuple):
+                kw[k] = x[0]; rd.append(x)
+            elif x is not None:
+                kw[k] = x
         if accum is not None:
             kw["accum_out"] = accum[0]; wr.append(accum)
-        op("s", lambda e: e.activation(out=out[0], in_=in_[0], func=fn, **kw), rd, wr)
+        op("s", lambda e: e.activation(out=out[0], in_=in_[0], func=fn, **kw), rd, wr, cost(out, in_, 1) + (0.02 if accum else 0))
 
     def ms(out, c):
-        op("v", lambda e: e.memset(out[0], c), [], [out])
+        op("v", lambda e: e.memset(out[0], c), [], [out], cost(out, out, half(out)))
 
-    def mm(out, l, r, start, stop):
-        op("t", lambda e: e.matmul(out=out[0], lhsT=l[0], rhs=r[0], start=start, stop=stop), [l, r], [out])
+    group = {}
 
-    def iota(out, pat, base, cmul, small=False):
-        kw = {"allow_small_or_imprecise_dtypes": True} if small else {}
-        op("g", lambda e: e.iota(out[0], pat, base, cmul, **kw), [], [out])
+    def mm(out, l, r, start=False):
+        n = out[1][0][0]
+        if start:
+            group[n] = len(ops)
+        op("t", lambda e, stop: e.matmul(out=out[0], lhsT=l[0], rhs=r[0], start=start, stop=stop), [l, r], [out],
+           max(64, r[2]) * TCYC * (4 if l[3] == f else 1), adds=not start, group=group[n])
+
+    def iota(out, pat, base=0, cmul=0):
+        kw = {} if out[3] == i4 else {"allow_small_or_imprecise_dtypes": True}
+        op("g", lambda e: e.iota(out[0], pat, base, cmul, **kw), [], [out], 0.23 + 2 * out[2] * CYC)
 
     def sel(out, in_, pat, o, fill, base, cmul):
-        op("g", lambda e: e.affine_select(out[0], in_[0], pat, o, fill, base, cmul), [in_], [out])
+        op("g", lambda e: e.affine_select(out[0], in_[0], pat, o, fill, base, cmul), [in_], [out], 0.27 + 2 * out[2] * CYC)
 
-    def rsum(out, in_):
-        op("v", lambda e: e.tensor_reduce(out=out[0], in_=in_[0], axis=AxisListType.X, op=ALU.add), [in_], [out])
+    def red(out, in_, o):
+        op("v", lambda e: e.tensor_reduce(out=out[0], in_=in_[0], axis=AxisListType.X, op=o), [in_], [out], max(64, in_[2]) * CYC)
 
-    def dup(q, out, src, t):
-        for h in (0, 256):
-            cp(q, A(out, h, h + 256), A(src, t, V, 4))
+    def scan(out, d0, d1, o0, o1, init=0.0):
+        op("v", lambda e: e.tensor_tensor_scan(out=out[0], data0=d0[0], data1=d1[0], initial=init, op0=o0, op1=o1), [d0, d1], [out], cost(out, d1, half(out, d0, d1)))
 
-    def cklist_d(t):
-        for e, src in ((0, "CfE"), (1, "CfO")):
-            for i in range(16):
-                sel(A("D1", 16 * e + i, 512, 32), A(src, 4 * i + t, V, 64), [[0, 16]], ALU.is_equal, 0.0, 0, 0)
+    def turn(out, in_):
+        op("v", lambda e: e.transpose(out=out[0], in_=in_[0]), [in_], [out], cost(out, in_, 1))
 
-    def turn():
-        op("v", lambda e: e.transpose(out=A("T1")[0], in_=A("D1")[0]), [A("D1")], [A("T1")])
+    def ext(n, t, c0=0, c1=512):
+        return A(n, V + 512 * t + c0, V + 512 * t + c1)
 
-    def cklist_t():
-        turn()
-        tt(A("T2"), A("T1", 0, 496), A("T1", 16, 512), ALU.add)
-        for k in range(16):
-            sel(A("ckf", 16 * k, 16 * k + 16), A("T2", k, 496, 32), [[0, 16]], ALU.is_equal, 0.0, 0, 0)
+    def win(n, t):
+        return A(n, 0, V + 512 * t + 256)
 
-    def halves(t, which):
-        n, o, s = (("NHI", ALU.arith_shift_right, 6), ("NLO", ALU.bitwise_and, 63))[which]
-        ts(A("ni"), A("ci", t, V, 4), s, o); cp("v", A(n), A("ni"))
+    def fill_ext(q, n, t, src=None, copies=2):
+        for h in range(copies):
+            cp(q, ext(n, t, 256 * h, 256 * h + 256), A(src or n, t, V, 4))
 
-    def xgather(t, kk):
-        s = (512 * kk, 512 * kk + 512)
-        tt(A("dx", *s), IND(A("xF"), A("CK%d" % t, 32 * kk, 32 * kk + 32)), A("xv2"), ALU.subtract)
+    def tolist(out, w, src, n, start, rows=range(16)):
+        for k, i in enumerate(rows):
+            mm(out, A(w, 15 - i, 143 - i), A(src, i, n, 16), start and k == 0)
 
-    def xscalar(t, kk):
-        s, bank = (512 * kk, 512 * kk + 512), A("pb%d" % (2 + kk % 2))
-        cp("s", A("dx", *s), IND(A("xF"), A("CK%d" % t, 32 * kk, 32 * kk + 32)))
-        mm(bank, A("I"), A("dx", *s), True, False); mm(bank, A("nI"), A("xv2"), False, True)
+    def cklist(t):
+        turn(A("T1", 0, 256), A("ci", 64 + t, 1088, 4)); turn(A("T1", 256, 544), A("ci", t, 1152, 4))
+        cp("v", A("CK%d" % t), IND(A("T1"), A("TL")))
 
-    def xabs(kk):
-        s = (512 * kk, 512 * kk + 512)
-        act(A("ab", *s), A("dx", *s), AF.Abs)
+    def keyinit(t):
+        act(A("NH"), ext("CF", t, 0, 256), AF.Identity, bias=A("c128"), scale=1.0 / 64)
+        mm(A("ps0"), A("ones"), A("KD"), True)
+        for h in (0, 1):
+            lo, hi, nh = A("ps0", 256 * h, 256 * h + 128), A("ps0", 256 * h + 128, 256 * h + 256), A("NH", 128 * h, 128 * h + 128)
+            mm(lo, ext("CF", t, 128 * h, 128 * h + 128), A("I32")); mm(lo, nh, A("n64I")); mm(hi, nh, A("I"))
 
-    def keyinit():
-        for half in (0, 1):
-            o = A("pb%d" % half, 0, 256)
-            mm(o, A("E0"), A("kc", 256 * half, 256 * half + 256), True, False)
-            for hv in range(4):
-                h, var = hv // 2, hv % 2
-                mm(o, A(("NHI", "NLO")[var], 128 * h, 128 * h + 128), A("RH", 512 * hv + 256 * half, 512 * hv + 256 * half + 256), False, False)
-
-    def keymm(kk, buf, w, last=False):
-        bank = "pb%d" % (kk // 4)
+    def keymm(kk, buf, w):
         for k in (2 * kk, 2 * kk + 1):
             for h in (0, 1):
-                o = 32 * (k % 8) + h
-                mm(A(bank, o, o + 32 - h, 2), A(buf, 256 * k + 128 * h, 256 * k + 128 * h + 128), A(w), False, last and k % 8 == 7 and h == 1)
+                mm(A("ps0", 256 * h + k, 256 * h + 256, 16), A(buf, 256 * k + 128 * h, 256 * k + 128 * h + 128), A(w))
 
-    def bits2list(out, src, n):
-        for i in range(16):
-            mm(out, A("BL", 128 * i, 128 * i + 128), A(src, i, n, 16), i == 0, i == 15)
+    nb = [0]
 
-    def rows2list(out, src, n, kp):
-        for i in range(16):
-            mm(out, A("SelL", 128 * i, 128 * i + 128, p1=kp), A(src, i, n, 16, p1=kp), i == 0, i == 15)
+    def by_scalar(out, table, off, own, sign, fn, kk, bias=None):
+        s = A("pc", 512 * kk, 512 * kk + 512); bank = A("ps%d" % (2 + nb[0] % 2)); nb[0] += 1
+        cp("s", s, IND(table, off))
+        mm(bank, A(("I", "nI")[sign < 0]), s, True); mm(bank, A(("nI", "I")[sign < 0]), own)
+        act(out, bank, fn, bias=bias)
 
-    def chsum(buf, w, cs=range(6), stop=False):
-        for c in cs:
-            mm(A("pb4", 16 * c, 16 * c + 16), A(buf, 128 * c, 128 * c + 128), A(w), False, stop and c == 5)
+    def distances(t):
+        for kk in range(8):
+            s = (512 * kk, 512 * kk + 512); off = A("CK%d" % t, 32 * kk, 32 * kk + 32)
+            if kk in X_S[t]:
+                by_scalar(A("ab", *s), A("xF"), off, ext("XM", t), 1, AF.Abs, kk)
+            else:
+                tt(A("dx", *s), IND(A("xF"), off), ext("XM", t), ALU.subtract)
+                if kk in ABS_V[t]:
+                    ts(A("ab", *s), A("dx", *s), 0.0, ALU.max); keymm(kk, "dx", "selDn")
+                else:
+                    act(A("ab", *s), A("dx", *s), AF.Abs)
+            keymm(kk, "ab", "selD2" if kk in ABS_V[t] else "selD")
 
-    def ftsum(col, w):
-        for c in range(6):
-            mm(A("pb6", col + 16 * c, col + 16 * c + 16), A("FB", 128 * c, 128 * c + 128), A(w), True, True)
+    def sums(start, rows):
+        o = A("ps1", 0, 48)
+        tolist(o, "nEK", "P", G, start); tolist(o, "BL8", "FB", G, False); tolist(o, "EK", "R", G, False, rows)
 
-    dma("s", A("R", 0, G), HB(T.reach[:, 0:G])); dma("y", A("ci"), HB(T.cand[:]))
-    dma("s", A("P", 0, G), HB(T.past[:, 0:G])); dma("y", A("X"), HB(T.x[:]))
-    dma("s", A("R", G, V), HB(T.reach[:, G:V])); dma("y", A("thr", p1=1), HB(T.th[:]))
-    dma("s", A("P", G, V), HB(T.past[:, G:V])); dma("y", A("si"), HB(T.succ[:]))
-    dma("y", A("RF", 0, V), HB(T.reach[:])); dma("y", A("PF", 0, V), HB(T.past[:]))
-
-    iota(A("pi"), [[0, 1]], 0, 1)
-    ms(A("ones"), 1.0)
-    iota(A("gmi"), [[0, 2], [1, 8]], 0, 0)
-    iota(A("mi16"), [[1, 16]], 0, 0, True)
-    iota(A("mI"), [[1, 128]], 0, 0)
-    iota(A("VL", 0, 16), [[64, 16]], 0, 0, True); iota(A("VL", 16, 32), [[16, 16]], 1024, 0, True)
-    send(A("R", 0, G), A("RF", V, V + G), A("RF", V + G, W), "iR", "li")
+    KB = 256
+    dma("s", A("R", 0, G), HB(T.reach[:, 0:G]), G * KB); dma("y", A("ci", 64, 1088), HB(T.cand[:]), 2 * V * KB)
+    dma("s", A("P", 0, G), HB(T.past[:, 0:G]), G * KB); dma("y", A("xF", 0, V), HB(T.x[:]), V * KB)
+    dma("s", A("R", G, V), HB(T.reach[:, G:V]), 256 * KB); dma("y", A("RF", 0, V), HB(T.reach[:]), V * KB)
+    dma("s", A("P", G, V), HB(T.past[:, G:V]), 256 * KB); dma("y", A("PF", 0, V), HB(T.past[:]), V * KB)
+    dma("y", A("th1", p1=1), HB(T.th[:]), 32); dma("y", A("XM", 0, V), HB(T.x[:]), V * KB); dma("y", A("si"), HB(T.succ[:]), 2 * V * KB)
+    send(A("R", 0, G), A("RF", V, V + G), A("RF", V + G, W), "iR", "li", 3.0)
     send(A("P", 0, G), A("PF", V, V + G), A("PF", V + G, W), "iP", "li")
-    arrive("iR", 2 * ne, [A("RF", V, W)]); arrive("iP", 2 * ne, [A("PF", V, W)])
-    sel(A("xF", 0, V), A("X"), [[0, 256], [1, 4]], ALU.not_equal, BIGX, 0, 0)
+
+    iota(A("pi"), [[0, 1]], 0, 1); iota(A("k16"), [[1, 16]]); iota(A("col"), [[1, 144]]); iota(A("gcol"), [[1, 8], [0, 16]])
+    iota(A("it", 0, 32), [[1, 32]]); iota(A("it", 32, 48), [[16, 2], [1, 8]]); iota(A("dl"), [[512, 4], [16, 16]], V)
+    iota(A("DM"), [[0, 32], [1, 16]]); iota(A("sv"), [[16, 8], [0, 56]]); iota(A("srow"), [[1, 128]])
+    ms(A("ci", 0, 64), 0); ms(A("ci", 1088, 1152), 0); ms(A("xF", V, W), BIGX); ms(A("ones"), 1.0)
     ts(A("gi"), A("pi"), 4, ALU.arith_shift_right); ts(A("ii"), A("pi"), 15, ALU.bitwise_and)
-    ts(A("ei"), A("gi"), 1, ALU.bitwise_and)
-    cp("v", A("modd"), A("ei")); cp("v", A("iF"), A("ii")); cp("v", A("gf"), A("gi")); cp("v", A("gm"), A("gmi"))
+    ts(A("ei"), A("gi"), 1, ALU.bitwise_and); ts(A("oki"), A("pi"), 1, ALU.bitwise_and)
+    for o, s in (("pf", "pi"), ("gf", "gi"), ("iF", "ii"), ("modd", "ei"), ("okc", "oki")):
+        cp("v", A(o), A(s))
     ts(A("meven"), A("modd"), -1.0, ALU.mult, 1.0, ALU.add)
-    ts(A("gm"), A("gm"), A("gf"), ALU.is_equal)
-    ts(A("selD"), A("gm"), 1024.0, ALU.mult); ts(A("selO"), A("gm"), 8388608.0, ALU.mult)
-    ms(A("xF", V, W), BIGX)
-    ms(A("cb", 0, 1), -10.0 * EQ); ms(A("cb", 1, 2), 1.0)
-    ts(A("mi16"), A("mi16"), A("iF"), ALU.is_equal)
-    ts(A("sj"), A("mi16"), -2.0, ALU.mult, 1.0, ALU.add)
-    ts(A("c64"), A("iF"), 8.0, ALU.is_lt, 63.0, ALU.mult); ts(A("c64"), A("c64"), 1.0, ALU.add)
-    ts(A("il1"), A("iF"), 10.0, ALU.is_lt)
-    ts(A("IB", 0, 1), A("il1"), -1.0, ALU.mult)
-    ms(A("EK"), 0.0)
-    ts(A("mG"), A("mI"), 4, ALU.arith_shift_right); cp("v", A("mGf"), A("mG")); ts(A("B16"), A("mGf"), A("gf"), ALU.is_equal)
-    ts(A("CfE", 0, 256), A("ci", 0, V, 4), A("meven"), ALU.mult)
-    ts(A("CfO", 0, 256), A("ci", 0, V, 4), A("modd"), ALU.mult)
-    for i in range(16):
-        cp("s" if i < 11 else "v", A("D1", i, 512, 32), A("CfE", i, 256, 16))
-    for i in range(16):
-        cp("v", A("D1", 16 + i, 512, 32), A("CfO", i, 256, 16))
-    turn()
-    dup("s", "xv2", "X", 0)
-    for k in range(16):
-        cp("s", A("EK", 128 * k + k, 128 * k + 128, 16), A("B16", k, 128, 16))
+    tt(A("tb"), A("modd"), A("okc"), ALU.not_equal); ts(A("tb2"), A("iF"), 16.0, ALU.mult)
+    ts(A("tb3"), A("tb"), 272.0, ALU.mult, A("tb2"), ALU.add); ts(A("TL"), A("k16"), A("tb3"), ALU.add)
+    ts(A("I"), A("col", 0, 128), A("pf"), ALU.is_equal)
+    for n, w in (("nI", -1.0), ("I32", 1.0), ("n64I", -64.0), ("kI", -1024.0), ("I16", 16.0), ("hI", 0.5)):
+        act(A(n), A("I"), AF.Copy, scale=w)
+    ts(A("ka"), A("iF"), 192.0, ALU.add, 64.0, ALU.mult); ts(A("kb"), A("iF"), -3.0, ALU.add, 64.0, ALU.mult)
+    for j in range(4):
+        act(A("KD", 128 * j, 128 * j + 128), A("I"), AF.Copy, scale=A(("ka", "kb")[j % 2]))
+    ts(A("B16"), A("gcol"), A("gf"), ALU.is_equal); act(A("nB16"), A("B16"), AF.Copy, scale=-1.0)
+    sel(A("nLs"), A("nB16"), [[-1, 128]], ALU.is_gt, 0.0, 0, 1)
+    for h in (0, 8):
+        cp("v", A("gm", h, h + 8), A("B16", 0, 128, 16))
+    for n, w in (("selD", 1024.0), ("selD2", 2048.0), ("selDn", -1024.0), ("selO", ORD)):
+        act(A(n), A("gm"), AF.Copy, scale=w)
+    ts(A("p128"), A("pf"), 128.0, ALU.add)
+    act(A("g64"), A("gm", 0, 8), AF.Copy, scale=64.0); act(A("ga", 0, 8), A("gm", 0, 8), AF.Copy, scale=A("pf")); act(A("ga", 8, 16), A("gm", 0, 8), AF.Copy, scale=A("p128"))
+    for t in range(ROUNDS):
+        act(A("gD", 8 * t, 8 * t + 8), A("gm", 0, 8), AF.Copy, scale=V + 512.0 * t)
+    ms(A("one"), 1.0); ms(A("nord"), -ORD / 2); ms(A("c128"), 192.0 - 31.5 / 64)
+    ts(A("mi"), A("k16"), A("iF"), ALU.is_equal); ts(A("sj"), A("mi"), -2.0, ALU.mult, 1.0, ALU.add); ts(A("il"), A("iF"), 10.0, ALU.is_lt)
+    ts(A("IB", 0, 1), A("il"), -1.0, ALU.mult)
     for j in range(10):
         act(A("IB", 2 ** j, 2 ** (j + 1)), A("IB", 0, 2 ** j), AF.Copy, scale=A("sj", j, j + 1))
-    for k in range(16):
-        tt(A("ckf", 16 * k, 16 * k + 16), A("T1", k, 512, 32), A("T1", 16 + k, 512, 32), ALU.add)
-    cp("v", A("CK0"), A("ckf"))
-    for kk in range(7):
-        xgather(0, kk)
-    halves(0, 0); halves(0, 1)
-    dma("y", A("SelL", p1=8), (T.EK[0:128:16, :], A("EK")[1])); dma("y", A("SelL", p0=8, p1=16), (T.EK[0:128:16, :], A("EK")[1]))
-    ms(A("rows2"), 0.0)
-    sel(A("E0"), A("ones", 0, 128), [[0, 128]], ALU.is_equal, 0.0, 0, 1)
-    iota(A("kc"), [[64, 16], [0, 32]], 0, 0, True)
-    for hv in range(4):
-        sel(A("RH", 512 * hv, 512 * hv + 512), A("ones"), [[-1, 16], [-16, 16], [4096, 2]], ALU.is_equal, 0.0, 128 * (hv % 2) - 4096 * (hv // 2), 1)
-    sel(A("I"), A("ones", 0, 128), [[-1, 128]], ALU.is_equal, 0.0, 0, 1)
-    sel(A("nI"), A("I"), [[-1, 128]], ALU.not_equal, -1.0, 0, 1)
-    xscalar(0, 7)
-    for kk in range(7):
-        xabs(kk)
-    act(A("ab", 3584, 4096), A("pb3"), AF.Abs)
-    iota(A("SN", p1=65), [[0, 128]], 0, 0, True)
-    sel(A("SN", p1=65), A("SN", p1=65), [[1, 8], [0, 16]], ALU.not_equal, -32768.0, 16, -1)
-    iota(A("rows2", p0=32, p1=33), [[1, 256]], 0, 0, True)
-    op("g", lambda e: e.partition_broadcast(A("thb")[0], A("thr", p1=1)[0], 128), [A("thr")], [A("thb")])
-    iota(A("VR"), [[0, 6], [1, 2], [0, 8]], 0, 0, True); iota(A("CC"), [[128, 6], [0, 16]], 128, 0, True)
-    keyinit()
-    for kk in range(8):
-        keymm(kk, "ab", "selD")
+    dma("y", A("FB", 0, V), A("IB"), V * KB)
+    ms(A("two"), 2.0); ms(A("wr"), 0.0)
+    scan(A("pw"), A("two"), A("wr"), ALU.mult, ALU.add, 0.25); tt(A("mp"), A("mi"), A("pw"), ALU.mult); red(A("tb"), A("mp"), ALU.add)
+    tt(A("wcol"), A("tb"), A("il"), ALU.mult); ts(A("w8"), A("wcol"), 8192.0, ALU.mult)
+    for i, w in ((10, -4096.0), (11, -256.0), (12, -1.0), (13, -4 * EQ)):
+        ms(A("wr", i, i + 1), w)
+    tt(A("mp2"), A("mi"), A("wr"), ALU.mult); red(A("wrow"), A("mp2"), ALU.add)
+    for e, m in (("e", "meven"), ("o", "modd")):
+        ts(A("sA" + e), A("il"), EQ, ALU.mult, A(m), ALU.mult); tt(A("cA" + e), A("wrow"), A(m), ALU.mult)
+    ts(A("e15"), A("gf"), 16.0, ALU.mult, 15.0, ALU.add)
+    ts(A("EK"), A("col"), A("e15"), ALU.is_equal)
+    for n, w in (("nEK", -1.0), ("BL", A("wcol")), ("BL8", A("w8"))):
+        act(A(n), A("EK"), AF.Copy, scale=w)
+    ts(A("DM"), A("DM"), A("iF"), ALU.is_equal); ts(A("sv"), A("sv"), A("iF"), ALU.add); ts(A("dl"), A("dl"), A("iF"), ALU.add)
+    cp("v", A("EXn"), A("it", 0, 32)); cp("v", A("EXw"), A("it", 32, 48))
+    ms(A("rst"), 0.0); ms(A("rst", 0, 1024, 16), HUGE); ms(A("rs56"), 1.0); ms(A("rs56", 0, 448, 56), 0.0); ms(A("ch", 48, 56), 1.0)
+    ms(A("dk"), 0.0); ts(A("dk", 12, 128, 16), A("ones", 0, 8), A("pf"), ALU.mult); ts(A("dk", 268, 384, 16), A("ones", 0, 8), A("p128"), ALU.mult)
+    ms(A("mx"), HUGE); ms(A("thb"), 0.0)
+    ts(A("c0"), A("pf"), -1.0, ALU.mult, 10 * EQ, ALU.add); ts(A("c1"), A("pf"), 128.0 - 10 * EQ, ALU.add)
+    op("g", lambda e: e.partition_broadcast(A("th2")[0], A("th1", p1=1)[0], 128), [A("th1")], [A("th2")], 0.3)
+    for j in range(4):
+        ts(A("thK", 8 * j, 8 * j + 8), A("th2"), 1024.0, ALU.mult)
+    cp("v", A("thC"), A("thK"))
+    ts(A("Fp", 0, 16), A("dl", 0, 16), -float(V), ALU.add)
+    for j in (1, 2):
+        ts(A("Fp", 16 * j, 16 * j + 16), A("dl", 0, 16), 256.0 * j - V, ALU.add)
 
-    def later():
-        cp("v", A("CF"), A("ci"))
-        ms(A("pw"), 0.0)
-        for i in range(10):
-            ms(A("pw", i, i + 1), 2.0 ** (i - 1))
-        tt(A("mp"), A("mi16"), A("pw"), ALU.mult); rsum(A("wcol"), A("mp"))
-        ms(A("zb"), 0.0)
-        ms(A("rows2", p0=64, p1=65), 1.0)
-        for n in ("SA", "SB"):
-            ms(A(n, p1=65), 0.0)
-        ms(A("rst"), 0.0)
-        for n, r, i, w in (("SA", 32, 12, 1.0), ("SA", 64, 13, 1.0), ("SA", 64, 14, 1.0), ("SA", 64, 15, 1.0), ("SB", 64, 10, 4096.0), ("SB", 64, 11, 256.0), ("SB", 64, 12, 1.0), ("SB", 32, 15, -1.0)):
-            ms(A(n, i, 128, 16, p0=r, p1=r + 1), w)
-        for n, c, i, w in (("SA", 0, 10, 1.0), ("SA", 8, 11, 1.0), ("SB", 0, 13, -4096.0), ("SB", 8, 14, -256.0)):
-            ts(A(n, i, 128, 16, p1=16), A("I", c, c + 8, p1=16), w, ALU.mult)
-        ms(A("rst", 0, 1024, 16), 1000.0)
-        ms(A("thT"), 1.0); ms(A("thT", 0, 16, 2), 10.0 * EQ + 1.0)
-        sel(A("U"), A("ones", 0, 128), [[1, 128]], ALU.is_ge, 0.0, 0, -1)
-        dma("y", A("FB", 0, V), A("IB"))
-        ts(A("bI"), A("I"), EQ, ALU.mult)
-        ts(A("oki"), A("ii"), 1, ALU.bitwise_and); cp("v", A("okc"), A("oki")); ts(A("ekc"), A("okc"), -1.0, ALU.mult, 1.0, ALU.add)
-        for h in (0, 1):
-            ts(A("thK", h, 16, 2), A("thb"), 1024.0, ALU.mult)
-        cp("v", A("thC"), A("thK"))
-        ts(A("i4c"), A("iF"), 4.0, ALU.mult)
-        ts(A("VL", 16, 32), A("VL", 16, 32), A("iF"), ALU.add)
-        for t in (1, 2, 3):
-            ts(A("VL", 32 * t, 32 * t + 16), A("VL", 0, 16), A("i4c"), ALU.add, float(t), ALU.add)
-            cp("v", A("VL", 32 * t + 16, 32 * t + 32), A("VL", 16, 32))
-        ts(A("VL", 0, 16), A("VL", 0, 16), A("i4c"), ALU.add)
-        cp("v", A("SO"), A("si"))
-
-    def later1():
-        act(A("SE"), A("SO"), AF.Copy, scale=A("ekc"))
-        act(A("SO"), A("SO"), AF.Copy, scale=A("okc"))
-        cp("v", A("SL0"), A("si", 0, V, 2))
-        cp("s", A("SLB", 0, 128), A("IB", G, G + 128))
-
-    def later2():
-        cp("v", A("SL1"), A("si", 1, V, 2))
-        cp("v", A("pf"), A("pi"))
-        ts(A("c7"), A("iF"), 7.0, ALU.is_lt); tt(A("wlo"), A("c7"), A("wcol"), ALU.mult); tt(A("whi"), A("wcol"), A("wlo"), ALU.subtract)
-        ts(A("c8"), A("iF"), 8.0, ALU.is_ge); tt(A("fhc"), A("c8"), A("il1"), ALU.mult)
-        ts(A("wF"), A("wcol"), 16384.0, ALU.mult); ts(A("wFn"), A("wcol"), -16384.0, ALU.mult)
-        ms(A("mone"), -1.0)
-        cp("s", A("selp"), A("gm"))
-        for o, w in (("seln", "mone"), ("sFp", "wF"), ("sFn", "wFn"), ("FH", "fhc")):
-            act(A(o), A("gm"), AF.Copy, scale=A(w))
-        act(A("FS", 0, 8), A("gm", 0, 8), AF.Copy, scale=A("wlo")); act(A("FS", 8, 16), A("gm", 8, 16), AF.Copy, scale=A("whi"))
-        ts(A("V0"), A("VR"), -1.0, ALU.mult, 1.0, ALU.add)
-        tt(A("CC"), A("VR"), A("CC"), ALU.mult); ts(A("VR"), A("V0"), A("pf"), ALU.mult); tt(A("NG"), A("CC"), A("VR"), ALU.add); tt(A("NG1"), A("NG"), A("V0"), ALU.add)
-        ts(A("kI"), A("I"), -1024.0, ALU.mult)
-        ftsum(0, "FS"); cp("v", A("FpT"), A("pb6", 0, 96))
-        for s, d in (("RF", "GR"), ("PF", "GP")):
-            dma("y", A(d + "a", 0, G), A(s, V, V + G)); dma("y", A(d + "b", 0, G), A(s, V + G, W))
+    cklist(0)
+    fill_ext("s", "XM", 0, "xF"); ms(A("xF", 0, V, 4), BIGX)
+    cp("v", ext("CF", 0, 0, 256), A("ci", 64, 1088, 4))
+    keyinit(0); distances(0)
+    fill_ext("s", "P", 0); fill_ext("s", "R", 0)
+    cp("v", A("CF", 0, V), A("ci", 64, 1088))
+    iota(A("SO", 0, V), [[0, V]]); iota(A("SE"), [[0, V]])
+    dma("y", A("SO", 0, V, p0=1, ps=2), HB(T.succ[1:128:2, :]), V * KB); dma("y", A("SE", p0=0, ps=2), HB(T.succ[0:128:2, :]), V * KB)
+    cp("v", A("SL0"), A("si", 0, V, 2)); cp("v", A("SL1"), A("si", 1, V, 2))
+    for s, d in (("RF", "GR"), ("PF", "GP")):
+        dma("y", A(d + "a", 0, G), A(s, V, V + G), G * KB); dma("y", A(d + "b", 0, G), A(s, V + G, W), G * KB)
+    fill_ext("g", "SO", 0, copies=1); fill_ext("g", "R", 1)
+    sums(True, range(16)); cp("v", A("Wo"), A("ps1", 0, 48))
 
     for t in range(ROUNDS):
-        last = t == ROUNDS - 1
-        ckt = "CK%d" % t; u = t + 1
-        if t == 0:
-            dup("s", "Pv2", "P", t); dup("s", "Rv2", "R", t)
-        nsp = NS_P[t]; first = [True]
-
-        def vchunk(n, kk):
-            s = (512 * kk, 512 * kk + 512); off = A(ckt, 32 * kk, 32 * kk + 32)
-            if n == "oR":
-                tt(A("oR", *s), IND(A("RF"), off), A("Pv2"), ALU.is_le)
-            else:
-                tt(A("oP", *s), IND(A("PF"), off), A("Rv2"), ALU.is_ge)
-
-        def pgather(kk):
-            s = (512 * kk, 512 * kk + 512)
-            cp("s", A("pc", *s), IND(A("PF"), A(ckt, 32 * kk, 32 * kk + 32)))
-            bank = A("pb%d" % (2 + kk % 2))
-            mm(bank, A("I"), A("pc", *s), True, False); mm(bank, A("nI"), A("Rv2"), False, True)
-
-        def prelu(kk):
-            act(A("oP", 512 * kk, 512 * kk + 512), A("pb%d" % (2 + kk % 2)), AF.Relu, bias=A("cb", 1, 2))
-
-        def olist(kk):
-            for k in (2 * kk, 2 * kk + 1):
-                for n in ("oR", "oP"):
-                    mm(A("pb7", 0, 256), A("EK", 128 * k, 128 * k + 128), A(n, 256 * k, 256 * k + 256), first[0], False)
-                    first[0] = False
-        work = [(n, kk) for kk in range(8) for n in ("oR", "oP") if n == "oR" or kk not in nsp]
-        ev = [(i + 1.0, 0, n, kk) for i, (n, kk) in enumerate(work)]
-        ev += [(1.7 * j + 1.0, 1, "g", kk) for j, kk in enumerate(nsp)] + [(1.7 * j + 2.8, 2, "r", kk) for j, kk in enumerate(nsp)]
-        left = {0: 16, 1: 16}
-        for _, _, n, kk in sorted(ev):
-            if n == "g":
-                pgather(kk)
-                continue
-            if n == "r":
-                prelu(kk)
-            else:
-                vchunk(n, kk)
-            n = "oP" if n == "r" else n
-            left[kk // 4] -= 2
-            keymm(kk, n, "selO", left[kk // 4] == 0)
-        if t == 0:
-            later()
-            act(A("CfE"), A("CF"), AF.Copy, scale=A("meven")); act(A("CfO"), A("CF"), AF.Copy, scale=A("modd"))
-            act(A("BL"), A("EK"), AF.Copy, scale=A("wcol"))
-            cklist_d(1)
+        last, u, par, ck = t == ROUNDS - 1, t + 1, t % 2, "CK%d" % t
         if not last:
-            halves(u, 0); halves(u, 1)
-        cp("s", A("ka"), A("pb0", 0, 256))
-        tt(A("t1"), A("pb1", 0, 256), A("ka"), ALU.min)
-        tt(A("wk", 0, 128), A("t1", 0, 128), A("t1", 128, 256), ALU.min)
-        tt(A("wk", 128, 192), A("wk", 0, 64), A("wk", 64, 128), ALU.min)
-        tt(A("wk", 192, 224), A("wk", 128, 160), A("wk", 160, 192), ALU.min)
-        m0 = A("wk", 192, 208)
-        ts(A("wi", 0, 32), A("wk", 192, 224), 16777215.0, ALU.min)
-        ts(A("wk", 224, 256), A("wk", 192, 224), HASLIM, ALU.is_lt)
-        ts(A("wi", 32, 64), A("wi", 0, 32), 63, ALU.bitwise_and)
-        tt(A("dec"), A("wi", 32, 64), A("wk", 224, 256), ALU.mult)
-        for h in (0, 1):
-            mm(A("pb5", 128 * h, 128 * h + 128, p1=16), A("dec", h, 32, 2), A("I"), True, True)
-        act(A("rowsN", p1=16), A("pb5", 0, 256, p1=16), AF.Copy, scale=A("c64", p1=16))
-        rows2list(A("pb6", 0, 16), "rowsN", 256, 16)
-        tt(A("wk", 272, 288), m0, A("thC"), ALU.is_ge)
-        ts(A("wk", 304, 320), m0, 4095.0 * 1024, ALU.min)
-        ts(A("wk", 288, 304), A("wk", 272, 288), 4095.0 * 1024, ALU.mult)
-        ts(A("dec2", 32, 48), m0, HASLIM, ALU.is_ge)
-        tt(A("wi", 64, 80), A("wk", 288, 304), A("wk", 304, 320), ALU.max)
-        ts(A("wi", 80, 96), A("wi", 64, 80), 14, ALU.arith_shift_right)
-        ts(A("wi", 112, 128), A("wi", 64, 80), 10, ALU.arith_shift_right)
-        ts(A("wi", 96, 112), A("wi", 112, 128), 15, ALU.bitwise_and)
-        cp("v", A("dec2", 0, 32), A("wi", 80, 112))
-        for h in (0, 1):
-            mm(A("pb2", 128 * h, 128 * h + 128, p1=24), A("dec2", h, 48, 2), A("I"), True, True)
-        cp("s", A("rows2", p1=24), A("pb2", 0, 256, p1=24))
-        cp("v", A("nl"), A("pb6", 0, 16))
-        cp("v", A("bits"), IND(A("FB", 0, V), A("nl")))
-        tt(A("wk", 320, 336), A("wk", 272, 288), A("thT"), ALU.mult)
-        tt(A("thA"), A("thT"), A("wk", 320, 336), ALU.subtract); ts(A("thA"), A("thA"), 1.0, ALU.subtract)
-        mm(A("pb5", 0, 256), A("SA", p1=65), A("rows2", p1=65), True, False); mm(A("pb6", 0, 256), A("SB", p1=65), A("rows2", p1=65), True, False)
-        mm(A("pb5", 0, 256), A("I"), A("bits"), False, True); mm(A("pb6", 0, 256), A("bI"), A("bits"), False, True)
-        ts(A("Ae"), A("pb5", 0, 256), A("meven"), ALU.mult)
-        cp("s", A("Bk"), A("pb6", 0, 256))
-        ts(A("Ao"), A("pb5", 0, 256), A("modd"), ALU.mult)
-        for gp in range(4):
-            for e in (0, 1):
-                for h in (0, 1):
-                    mm(A("pb%d" % (2 * h + gp % 2), 256 * e, 256 * e + 256), A(("Ae", "Ao")[e], 128 * h, 128 * h + 128, p0=32 * gp, p1=32 * gp + 32), A("Bk", p0=32 * gp, p1=32 * gp + 32), True, True)
-            for e in (0, 1):
-                gg = 2 * gp + e
-                bk = A("pb%d" % (gp % 2), 256 * e, 256 * e + 256)
-                op("v", lambda q, bk=bk, gg=gg: q.tensor_reduce(out=A("mx", 2 * gg, 2 * gg + 1)[0], in_=bk[0], axis=AxisListType.X, op=ALU.max), [bk], [A("mx", 2 * gg, 2 * gg + 1)])
-                act(A("tr", 256 * e, 256 * e + 256), A("pb%d" % (2 + gp % 2), 256 * e, 256 * e + 256), AF.Relu, bias=A("cb", 0, 1), accum=A("mx", 2 * gg + 1, 2 * gg + 2))
-        bits2list(A("pb5", 0, 16), "bits", 256)
-        tt(A("win"), A("mx"), A("thA"), ALU.is_le)
-        ts(A("bl"), A("pb5", 0, 16), 511.5, ALU.add)
-        for d, bank in ((0, "pb5"), (256, "pb0")):
-            for h in (0, 1):
-                mm(A(bank, 128 * h, 128 * h + 128, p1=8), A("win", h, 16, 2), A("I"), True, True)
-        tt(A("bd", 0, 16), A("bl"), A("VL", 32 * t, 32 * t + 16), ALU.subtract); tt(A("bd", 16, 32), A("bl"), A("VL", 32 * t + 16, 32 * t + 32), ALU.subtract)
-        cp("s", A("rowsW", 0, 256, p1=8), A("pb5", 0, 256, p1=8)); cp("v", A("rowsW", 256, 512, p1=8), A("pb0", 0, 256, p1=8))
-        rows2list(A("pb6", 0, 32), "rowsW", 512, 8)
-        if t == 0:
-            later1()
-        cp("v", A("bu"), A("bl"))
-        tt(A("dC"), IND(A("CF"), A("bu")), A("ci", t, V, 4), ALU.subtract)
-        tt(A("bq"), A("pb6", 0, 32), A("bd"), ALU.mult)
-        tt(A("bq2"), A("bq"), A("VL", 32 * t, 32 * t + 32), ALU.add)
-        cp("v", A("LL"), A("bq2"))
-        be, bt = A("LL", 0, 16), A("LL", 16, 32)
-        if not last:
-            if t == 0:
-                later2()
-            mm(A("pb4", 0, 96), A("zb"), A("rst", 0, 96), True, False)
-            chsum("R", "selp"); chsum("P", "seln"); chsum("FB", "sFn")
-        cp("v", IND(A("FB"), bt), A("IB", t, V, 4))
-        bits2list(A("pb5", 0, 64), "FB", V)
-        tt(A("Rn"), IND(A("R"), be), A("Rv2", 0, 256), ALU.min)
-        cp("s", A("R", t, V, 4), A("Rn"))
-        tt(A("sn"), IND(A("SO"), be), A("SE", t, V, 4), ALU.add)
-        cp("v", A("SL%d" % (t % 2), t // 2, 512, 2), A("sn"))
-        ts(A("FL"), A("pb5", 0, 64), 511.5, ALU.add)
-        cp("v", A("RF", 0, 512), IND(A("R"), A("FL", 0, 32))); cp("s", A("RF", 512, V), IND(A("R"), A("FL", 32, 64)))
-        par = t % 2
-
-        def g3(q, c):
-            cp(q, A("g3", 1024 * c, 1024 * c + 1024), IND(A("RF"), A("SL%d" % par, 64 * c, 64 * c + 64)))
-
-        def s3(c):
-            s = (1024 * c, 1024 * c + 1024)
-            op("v", lambda e: e.tensor_tensor_scan(out=A("s3", *s)[0], data0=A("rst")[0], data1=A("g3", *s)[0], initial=0.0, op0=ALU.max, op1=ALU.min), [A("rst"), A("g3", *s)], [A("s3", *s)])
-        tt(A("xs"), IND(A("X"), be), A("xv2", 0, 256), ALU.add)
-        if not last:
-            tt(A("Pn"), IND(A("P"), be), A("Pv2", 0, 256), ALU.max)
-        for c in range(NV3, 8):
-            g3("s", c)
-            if c == NV3 and not last:
-                cp("s", A("P", t, V, 4), A("Pn"))
-        ts(A("xi"), A("xs"), -0.5, ALU.add, 0.5, ALU.mult)
-        cp("v", A("X", t, V, 4), A("xi"))
-        if last:
-            dma("y", HB(T.yx[:]), A("X"))
-        else:
-            sel(A("xm"), A("X"), [[0, 256], [1, 4]], ALU.not_equal, BIGX, -u, 0)
-        for c in range(NV3):
-            g3("v", c)
-        if not last:
-            mm(A("pb6", 192, 208), A("ones", 0, 128), A("win"), True, True)
-            ftsum(0, "FS"); ftsum(96, "FH")
-            chsum("FB", "sFp"); chsum("P", "selp")
-            rsum(A("Mf"), A("pb6", 192, 208))
-            ts(A("xw", 0, 96), A("pb6", 96, 192), 1.0, ALU.is_lt)
-            tt(A("dF"), A("pb6", 0, 96), A("FpT"), ALU.subtract)
-            tt(A("dF"), A("dF"), A("xw", 0, 96), ALU.mult)
-            cklist_t()
+            cklist(u)
+            for n in ("XM", "P"):
+                fill_ext("g", n, u)
+            fill_ext("g", "CF", u, copies=1); fill_ext("g", "SO", u, copies=1)
         for kk in range(8):
-            olist(kk)
-        mm(A("pb7", 0, 256), A("SN", p1=65), A("rows2", p1=65), False, True)
-
-        def cupdate():
-            tt(A("oi"), A("oi"), A("dC"), ALU.mult)
-            tt(A("CF", t, V, 4), A("oi"), A("CF", t, V, 4), ALU.add)
-        for c0, c1 in ((0, 5), (5, 8)):
-            for c in range(c0, c1):
-                s3(c)
-            if c0 == 0 and last:
-                ts(A("oi"), A("pb7", 0, 256), 0.0, ALU.is_gt); cupdate()
-                dma("y", HB(T.yc[:]), A("CF"))
-            o = A("R", par + 128 * c0, 128 * c1, 2)
-            tt(o, A("s3", 1024 * c0 + 15, 1024 * c1, 16), o, ALU.min)
-            if not last:
-                chsum("R", "seln", range(c0, min(c1, 6)), c1 == 8)
+            s = (512 * kk, 512 * kk + 512); off = A(ck, 32 * kk, 32 * kk + 32)
+            tt(A("oR", *s), IND(A("RF"), off), ext("P", t), ALU.is_le); keymm(kk, "oR", "selO")
+            if kk in CMP_S[t]:
+                by_scalar(A("oP", *s), A("PF"), off, ext("R", t), 1, AF.Relu, kk, A("one"))
             else:
-                dma("sy"[c0 // 5], HB(T.yr[:, 128 * c0:128 * c1]), A("R", 128 * c0, 128 * c1))
+                tt(A("oP", *s), IND(A("PF"), off), ext("R", t), ALU.is_ge)
+            keymm(kk, "oP", "selO")
+        scan(A("ks"), A("rst", 0, 512), A("ps0"), ALU.max, ALU.min)
+        km = A("ks", 15, 512, 16)
+        ts(A("wi"), km, 2.0 ** 22 - 1, ALU.min)
+        ts(A("wn"), A("wi"), 63, ALU.bitwise_and)
+        tt(A("Wn"), IND(A("wn"), A("EXn")), A("DM"), ALU.mult)
+        for j in range(4):
+            mm(A("ps6", 8 * (j // 2), 8 * (j // 2) + 8), A("Wn", 128 * j, 128 * j + 128), A("g64") if j % 2 else A("gm", 0, 8), j % 2 == 0)
+        ts(A("nl"), A("ps6", 0, 16), V - 1.0, ALU.min)
+        ts(A("nh"), A("ps6", 0, 16), float(V), ALU.is_ge)
+        tt(A("dk", 13, 512, 16), km, A("thC"), ALU.is_ge)
+        ts(A("wd", 0, 32), A("wi"), 14, ALU.arith_shift_right); ts(A("wd", 32, 64), A("wi"), 10, ALU.arith_shift_right, 15, ALU.bitwise_and)
+        cp("v", A("dk", 10, 1024, 16), A("wd"))
+        for h in (0, 1):
+            o = A("ps7", 128 * h, 128 * h + 128)
+            mm(o, A("dk", 256 * h, 256 * h + 128), A("I"), True); mm(o, A("dk", 511 + 256 * h, 639 + 256 * h), A("I"))
+        cp("s", A("Kr"), A("ps7", 0, 256))
+        ts(A("wD"), A("wi"), 2 ** 22 - 1024, ALU.bitwise_and)
+        ts(A("bs"), A("wD", 16, 24), 0.25, ALU.mult, A("c1"), ALU.add)
+        ts(A("thb", 0, 8), A("wD", 0, 8), -0.25, ALU.mult, A("c0"), ALU.add)
+        ts(A("nb"), A("dk", 13, 512, 16), -32 * EQ, ALU.mult); tt(A("thr"), A("nb"), A("thb"), ALU.add)
+        for h in (0, 1):
+            act(A("fl", 128 * h, 128 * h + 128), A("ps0", 256 * h, 256 * h + 128), AF.Sign, bias=A("nord"))
+        fb = IND(A("FB", 0, V), A("nl"))
+        tt(A("Bk"), fb, A("Kr"), ALU.add)
+        act(A("Ae"), fb, AF.Identity, bias=A("cAe"), scale=A("sAe"))
+        ts(A("Ao"), fb, A("sAo"), ALU.mult, A("cAo"), ALU.add)
+        for s, gg in enumerate((0, 2, 4, 6, 1, 3, 5, 7)):
+            for h in (1, 0):
+                z, m = A("ps%d" % (2 + 2 * h + s % 2), 0, 256), A("mx", 16 * h + gg, 16 * h + gg + 1)
+                rows = dict(p0=32 * (gg // 2), p1=32 * (gg // 2) + 32)
+                mm(z, A(("Ae", "Ao")[gg % 2], 128 * h, 128 * h + 128, **rows), A("Bk", **rows), True)
+                if h:
+                    act(A("pc", 256 * s, 256 * s + 256), z, AF.Relu, bias=A("bs", gg, gg + 1), accum=m)
+                else:
+                    red(m, z, ALU.max)
+        tolist(A("ps6", 16, 32), "BL", "Bk", 256, True)
+        ts(A("blf"), A("ps6", 16, 32), 511.5, ALU.add)
+        tt(A("lose"), A("mx"), A("thr"), ALU.is_gt)
+        tt(A("W2"), IND(A("lose"), A("EXw")), A("DM", 0, 256), ALU.mult)
+        for j in range(4):
+            h = j // 2
+            mm(A("ps6", 32 + 8 * h, 40 + 8 * h), A("W2", 128 * h, 128 * h + 128), A("gD", 8 * t, 8 * t + 8) if j % 2 else A("ga", 8 * h, 8 * h + 8), j % 2 == 0)
+        tt(A("btf"), A("ps6", 32, 48), A("blf"), ALU.max); cp("v", A("bt"), A("btf"))
+        bt = A("bt")
+        cp("v", IND(win("FB", t), bt), A("IB", t, V, 4))
+        tolist(A("ps6", 64, 128), "BL", "FB", V, True)
+        ts(A("FL"), A("ps6", 64, 128), 511.5, ALU.add)
+        tt(A("Rn"), IND(win("R", t), bt), ext("R", t, 256, 512), ALU.min); cp("s", A("R", t, V, 4), A("Rn"))
+        tt(A("sn"), IND(win("SO", t), bt), A("SE", t, V, 4), ALU.add); cp("v", A("SL%d" % par, t // 2, 512, 2), A("sn"))
+        cp("v", A("RF", 0, 512), IND(A("R", 0, V), A("FL", 0, 32))); cp("s", A("RF", 512, V), IND(A("R", 0, V), A("FL", 32, 64)))
+        tt(A("xs"), IND(win("XM", t), bt), ext("XM", t, 256, 512), ALU.add)
+        ts(A("xi"), A("xs"), -0.5, ALU.add, 0.5, ALU.mult); cp("v", A("XM", t, V, 4), A("xi"))
+        tt(A("nh2"), A("nh"), A("dl", 16 * t, 16 * t + 16), ALU.mult); tt(A("buf"), A("nh2"), A("blf"), ALU.max); cp("v", A("bu"), A("buf"))
+
+        def candidates():
+            tt(A("dC"), IND(win("CF", t), A("bu")), A("ci", 64 + t, 1088, 4), ALU.subtract)
+            for h in (0, 1):
+                o = A("ps1", 256 + 128 * h, 384 + 128 * h)
+                mm(o, A("fl", 128 * h, 128 * h + 128), A("hI"), True); mm(o, A("ones"), A("hI"))
+            tt(A("oi"), A("ps1", 256, 512), A("dC"), ALU.mult); tt(A("CF", t, V, 4), A("oi"), ext("CF", t, 0, 256), ALU.add)
+        if last:
+            candidates()
+            dma("y", HB(T.yx[:]), A("XM", 0, V), V * KB); dma("y", HB(T.yc[:]), A("CF", 0, V), 2 * V * KB)
+        else:
+            tt(A("Pn"), IND(win("P", t), bt), ext("P", t, 256, 512), ALU.max); cp("g", A("P", t, V, 4), A("Pn"))
+            ts(A("SO", t, V, 4), A("sn"), A("okc"), ALU.mult)
+            ms(A("XM", u, V, 4), BIGX)
+            cp("s", A("xF", 0, V), IND(A("XM", 0, V), A("FL"))); cp("s", A("PF", 0, V), IND(A("P", 0, V), A("FL")))
+            mm(A("ps4", 0, 32), A("ones"), A("lose"), True); red(A("Mf"), A("ps4", 0, 32), ALU.add)
+            ts(A("Mi"), A("Mf"), -1.0, ALU.mult, 4096.0, ALU.add); ts(A("Mj"), A("Mi"), 31, ALU.bitwise_and)
+            ts(A("Mk"), A("Mj"), 1024.0, ALU.mult); ts(A("thC"), A("thK"), A("Mk"), ALU.add)
+            ts(A("FLf"), A("ps6", 64, 112), 511.5, ALU.add)
+            tt(A("dF1"), A("FLf"), A("Fp"), ALU.subtract); ts(A("dF2"), A("FLf"), float(G), ALU.is_lt); tt(A("dF"), A("dF1"), A("dF2"), ALU.mult)
+            sums(True, range(1 - par, 16, 2))
+        mm(A("ps5"), A("I"), A("R", par, V, 2), True)
+        for c0, c1 in ((0, 6), (6, 8)) if not last else ((0, 4), (4, 7), (7, 8)):
+            for c in range(c0, c1):
+                for d in (2 * c, 2 * c + 1):
+                    cp("v" if d in G3_V[t] else "s", A("g3", 512 * d, 512 * d + 512), IND(A("RF"), A("SL%d" % par, 32 * d, 32 * d + 32)))
+                s = (1024 * c, 1024 * c + 1024)
+                scan(A("s3", *s), A("rst"), A("g3", *s), ALU.max, ALU.min)
+            tt(A("R", par + 128 * c0, 128 * c1, 2), A("s3", 1024 * c0 + 15, 1024 * c1, 16), A("ps5", 64 * c0, 64 * c1), ALU.min)
+            if last:
+                dma("sy"[c0 % 2], HB(T.yr[:, 128 * c0:128 * c1]), A("R", 128 * c0, 128 * c1), 128 * (c1 - c0) * KB)
         if last:
             break
-        cp("s", A("xF", 0, V), IND(A("xm"), A("FL")))
-        dup("s", "xv2", "X", u); dup("s", "Pv2", "P", u)
-        ts(A("ch"), A("pb4", 0, 96), 0.0, ALU.not_equal)
-        mm(A("pb5", 0, 96), A("U"), A("ch"), True, False)
-        for s in range(1, 6):
-            mm(A("pb5", 16 * s, 96), A("ones", 0, 128), A("ch", 0, 96 - 16 * s), False, False)
-        mm(A("pb5", 0, 96), A("kI"), A("ch"), False, True)
-        tt(A("chz"), A("ch"), A("V0"), ALU.mult)
-        mm(A("pb6", 0, 96), A("nI"), A("NG1"), True, False)
-        mm(A("pb6", 0, 96), A("U"), A("chz"), False, False)
-        for s in range(1, 6):
-            mm(A("pb6", 16 * s, 96), A("ones", 0, 128), A("chz", 0, 96 - 16 * s), False, s == 5)
-        cp("v", A("Mi"), A("Mf")); ts(A("Mj"), A("Mi"), 31, ALU.bitwise_and)
-        ts(A("xw", 96, 192), A("pb5", 0, 96), 128.0 - 1024.0, ALU.is_le)
-        tt(A("pos"), A("pb6", 0, 96), A("xw", 96, 192), ALU.mult)
+        msg = "MS%d" % t
+        tolist(A("ps1", 0, 48), "EK", "R", G, False, range(par, 16, 2))
+        tt(A("ch", 0, 48), A("ps1", 0, 48), A("Wo"), ALU.not_equal); cp("v", A("Wo"), A("ps1", 0, 48))
+        scan(A("cc"), A("ones", 0, 56), A("ch"), ALU.mult, ALU.add)
+        for c in range(8):
+            mm(A("ps4", 56 * c, 56 * c + 56), A("B16"), A("cc"), True)
+        for o in (128, 192):
+            mm(A("ps6", o, o + 56), A("B16"), A("cc"), True); mm(A("ps6", o, o + 56), A("nLs"), A("ch"))
+        mm(A("ps6", 192, 248), A("kI"), A("ch"))
+        tt(A("f1"), A("ps4", 0, 448), A("sv"), ALU.is_le)
+        scan(A("f2"), A("rs56"), A("f1"), ALU.mult, ALU.add)
+        cp("v", A("cu"), A("f2", 55, 448, 56)); cp("v", A("cw"), A("ps6", 128, 184))
+        ts(A("go"), A("ps6", 192, 240), 128.0 - 1024.0, ALU.is_le)
+        tt(A("f3"), IND(A("cw"), A("cu")), A("srow"), ALU.is_le)
+        tolist(A("ps7", 0, 8), "EK", "f3", 128, True); mm(A("ps7", 0, 8), A("I16"), A("f2", 55, 448, 56))
+        ts(A("sl"), A("ps7", 0, 8), G - 1.0, ALU.min); cp("v", A(msg, 256, 264), A("ps7", 0, 8))
+        tt(A("go2"), A("go"), A("dF"), ALU.mult); tt(A("Fp"), A("Fp"), A("go2"), ALU.add); cp("v", A(msg, 264, 312), A("Fp"))
+        for k, n in enumerate("RP"):
+            cp("v", A(msg, 128 * k, 128 * k + 128), IND(A(n, 0, G), A("sl")))
+        send(A(msg), A("La%d" % t), A("Lb%d" % t), "a%d" % t)
+        cp("s", A("RF", 0, V), IND(A("R", 0, V), A("FL")))
+        if t + 2 < ROUNDS:
+            fill_ext("g", "R", t + 2)
+        keyinit(u); distances(u); candidates()
+        for k, n in ((1, "P"), (0, "R")):
+            for j, d in enumerate("ab"):
+                land = "L%s%d" % (d, t)
+                cp("v", IND(A("G" + n + d), A(land, 256, 264)), A(land, 128 * k, 128 * k + 128))
+                cp("v" if (n, d) in GH_V else "s", A(n + "F", V + G * j, V + G * j + G), IND(A("G" + n + d), A(land, 264, 312)))
 
-        def torows(src, rows, b0, b1, q, more=None):
-            for c in range(6):
-                bank, o = ((b0, 128 * c) if c < 4 else (b1, 128 * c - 512))
-                mm(A(bank, o, o + 128, p1=16), A(src, 16 * c, 16 * c + 16), A("I"), True, more is None)
-                if more is not None:
-                    mm(A(bank, o, o + 128, p1=16), A(more, 16 * c, 16 * c + 16), A("I"), False, True)
-            cp("s", A(rows, 0, 512, p1=16), A(b0, 0, 512, p1=16)); cp(q, A(rows, 512, G, p1=16), A(b1, 0, 256, p1=16))
-        tt(A("xw", 480, 576), A("dF"), A("xw", 96, 192), ALU.mult)
-        torows("pos", "rowsP", "pb5", "pb6", "v", "NG")
-        ts(A("oi"), A("pb7", 0, 256), 0.0, ALU.is_gt)
-        rows2list(A("pb7", 0, 48), "rowsP", G, 16)
-        cp("v", A("CK%d" % u), A("ckf"))
-        tt(A("FpT"), A("FpT"), A("xw", 480, 576), ALU.add)
-        cp("v", A("Fpb"), A("FpT"))
-        xgather(u, 0)
-        cp("v", A("pl"), A("pb7", 0, 48))
-        torows("Fpb", "rowsF", "pb2", "pb3", "s")
-        rows2list(A("pb5", 0, 48), "rowsF", G, 16)
-        cp("v", IND(A("SLB"), A("pl")), A("IB", 0, G))
-        bits2list(A("pb7", 0, 8), "SLB", 128)
-        sp, sll = "SRP%d" % t, "SLL%d" % t
-        ts(A(sll, 8, 56), A("pb5", 0, 48), 511.5, ALU.add)
-        xabs(0)
-        cp("s", A("PF", 0, V), IND(A("P"), A("FL")))
-        ts(A("Mk"), A("Mj"), 1024.0, ALU.mult); ts(A("thC"), A("thK"), A("Mk"), ALU.add)
-        ts(A(sll, 0, 8), A("pb7", 0, 8), 511.5, ALU.add)
-        cp("v", A(sp, 0, 128), IND(A("R"), A(sll, 0, 8))); cp("s", A(sp, 128, 256), IND(A("P"), A(sll, 0, 8)))
-        send(A(sll), A("LLa%d" % t), A("LLb%d" % t), "aL%d" % t)
-        send(A(sp), A("LRa%d" % t), A("LRb%d" % t), "aR%d" % t)
-        arrive("aR%d" % t, 2 * ne, [A("LRa%d" % t), A("LRb%d" % t)]); arrive("aL%d" % t, 2 * ne, [A("LLa%d" % t), A("LLb%d" % t)])
-        cp("s", A("SLB", 0, 128), A("IB", G, G + 128))
-        cp("s", A("RF", 0, V), IND(A("R"), A("FL")))
-        for kk in range(1, 8):
-            if kk in NX_S:
-                xscalar(u, kk)
-            else:
-                xgather(u, kk)
-        for kk in range(1, 8):
-            if kk in NX_S:
-                act(A("ab", 512 * kk, 512 * kk + 512), A("pb%d" % (2 + kk % 2)), AF.Abs)
-            else:
-                xabs(kk)
-        dup("s", "Rv2", "R", u)
-        act(A("SO", t, V, 4), A("sn"), AF.Copy, scale=A("okc"))
-        keyinit()
-        for kk in range(8):
-            keymm(kk, "ab", "selD")
-        cupdate()
-        if u + 1 < ROUNDS:
-            cklist_d(u + 1)
-        ll = {d: "LL%s%d" % (d, t) for d in "ab"}
-        for k, tb in ((1, "GP"), (0, "GR")):
-            for d in "ab":
-                cp("v", IND(A(tb + d), A(ll[d], 0, 8)), A("LR%s%d" % (d, t), 128 * k, 128 * k + 128))
-        for k, d in enumerate("ab"):
-            cp("s", A("PF", V + G * k, V + G * k + G), IND(A("GP" + d), A(ll[d], 8, 56)))
-        cp("v", A("RF", V, V + G), IND(A("GRa"), A(ll["a"], 8, 56)))
-        cp("v", A("RF", V + G, V + G + 384), IND(A("GRb"), A(ll["b"], 8, 32)))
-        cp("s", A("RF", V + G + 384, W), IND(A("GRb"), A(ll["b"], 32, 56)))
-
+    if "o" not in _ORDER:
+        _ORDER["o"] = order(ops); _ORDER["p"] = needs(ops)
+    seq, pre = _ORDER["o"], _ORDER["p"]
+    eng = {"v": g.vector, "s": g.scalar, "t": g.tensor, "g": g, "y": g.sync}
+    cnt = {q: 0 for q in eng}; clk = {q: {} for q in eng}; done = {}; total = {}; nd = 0
+    closes = {ops[i]["group"]: i for i in seq if ops[i]["q"] == "t"}
+    for i in seq:
+        o = ops[i]; q = o["q"]
+        if q == "x":
+            done[i] = (o["call"], 2 * ne, {}); total[o["call"]] = 2 * ne
+            continue
+        wait = [done[j] for j in pre[i] if j not in o["after"] and not (q == "t" == ops[j]["q"]) and done[j] is not None]
+        if q == "g" and o["kind"] == "" and cnt[q]:
+            wait.append(("qg", cnt[q], {}))
+        for sem, val, ck in sorted(wait, key=lambda w: -len(w[2])):
+            if clk[q].get(sem, 0) < val:
+                eng[q].wait_ge(T.sem[sem], val)
+                for s, v in list(ck.items()) + [(sem, val)]:
+                    clk[q][s] = max(clk[q].get(s, 0), v)
+        if o["kind"] == "dma":
+            sem = "d%d" % nd; nd += 1
+            o["call"](eng[q]).then_inc(T.sem[sem], 16); done[i] = (sem, 16, dict(clk[q])); total[sem] = 16
+        elif o["kind"] == "rem":
+            o["call"](g); done[i] = (o["loc"], 2 * ne, {}); total[o["loc"]] = total.get(o["loc"], 0) + ne
+        else:
+            cnt[q] += 1
+            ins = o["call"](eng[q], closes[o["group"]] == i) if q == "t" else o["call"](eng[q])
+            ins.then_inc(T.sem["q" + q], 1); done[i] = ("q" + q, cnt[q], dict(clk[q])); total["q" + q] = cnt[q]
     for s, v in total.items():
         g.wait_ge(T.sem[s], v)

@@ -7,7 +7,8 @@ BIGX = 8192.0
 EQ = 1048576.0
 ORD = 2.0 ** 30
 HUGE = 2.0 ** 80
-CMP_S = ((3, 4, 5, 6, 7),) + ((2, 3, 4, 5, 6, 7),) * 3
+CMP_S = ((5, 6, 7),) + ((2, 3, 4, 5, 6, 7),) * 3
+CMP_R = ((0, 1, 2, 3), (), (), ())
 ABS_V = ((), (), (), ())
 X_S = ((7,), (), (), ())
 G3_V = ((0, 1, 2),) * 3 + ((0, 1, 2, 3, 4),)
@@ -15,23 +16,23 @@ GH_V = (("R", "a"),)
 
 b, f, i4, u2 = "bfloat16", "float32", "int32", "uint16"
 _S = {
-    "R": (3072, b), "P": (3072, b), "XM": (3072, b), "xF": (W, b), "RF": (W, b), "PF": (W, b), "FB": (3072, b), "IB": (V, b),
+    "R": (3072, b), "P": (3072, b), "XM": (3072, b), "xF": (W, b), "RF": (W + 256, b), "PF": (W, b), "FB": (3072, b), "IB": (V, b),
     "ci": (1152, i4), "CF": (3072, f), "SO": (3072, i4), "SE": (V, i4), "si": (V, i4), "SL0": (512, u2), "SL1": (512, u2),
     "T1": (544, i4), "CK0": (256, u2), "CK1": (256, u2), "CK2": (256, u2), "CK3": (256, u2), "NH": (256, b),
     "dx": (4096, b), "ab": (4096, b), "oR": (4096, b), "oP": (4096, b), "pc": (4096, b), "g3": (8192, b), "s3": (8192, b),
     "ks": (512, f), "rst": (1024, b), "dk": (1024, b), "Wn": (512, b), "DM": (512, b), "KD": (512, b),
-    "Kr": (256, b), "Ae": (256, b), "Ao": (256, b), "Bk": (256, b), "tr": (256, b), "W2": (256, b), "fl": (256, b),
-    "Rn": (256, b), "Pn": (256, b), "xs": (256, f), "xi": (256, i4), "sn": (256, f), "dC": (256, f), "oi": (256, f),
+    "Kr": (256, b), "Ae": (256, b), "Ao": (256, b), "Bk": (256, b), "fn": (256, b), "W2": (256, b), "fl": (256, b),
+    "RW": (768, b), "Pn": (256, b), "xs": (256, f), "xi": (256, i4), "sn": (256, f), "dC": (256, f), "oi": (256, f),
     "rs56": (448, b), "sv": (448, b), "f1": (448, b), "f2": (448, b), "f3": (128, b), "srow": (128, b),
     "col": (144, b), "EK": (144, b), "nEK": (144, b), "BL": (144, b), "BL8": (144, b),
-    "ones": (128, b), "I": (128, b), "nI": (128, b), "I32": (128, f), "n64I": (128, b), "kI": (128, b), "I16": (128, b), "hI": (128, b),
+    "ones": (128, b), "I": (128, b), "nI": (128, b), "I32": (128, f), "nI32": (128, f), "n64I": (128, b), "n4I": (128, b), "kI": (128, b), "I16": (128, b), "hI": (128, b),
     "B16": (128, b), "nB16": (128, b), "nLs": (128, b), "gcol": (128, b),
     "wi": (32, i4), "wn": (32, i4), "wd": (64, i4), "wD": (32, i4), "mx": (32, f), "thr": (32, f), "thb": (32, f), "nb": (32, f), "bs": (8, f),
     "lose": (32, b), "thK": (32, f), "thC": (32, f), "th1": (8, i4), "th2": (8, i4), "Mf": (1, f), "Mi": (1, i4), "Mj": (1, i4), "Mk": (1, f),
-    "blf": (16, f), "btf": (16, f), "nh": (16, f), "nh2": (16, f), "buf": (16, f), "dl": (64, f), "FLf": (48, f), "dF": (48, f), "dF1": (48, f), "dF2": (48, f),
+    "wins": (64, f), "LLf": (64, f), "nsf": (16, f), "c511": (1, f), "nh": (16, f), "nh2": (16, f), "buf": (16, f), "dl": (64, f), "FLf": (48, f), "dF": (48, f), "dF1": (48, f), "dF2": (48, f),
     "Fp": (48, f), "go": (48, f), "go2": (48, f), "Wo": (48, f), "ch": (56, b), "cc": (56, b), "cw": (56, f),
-    "TL": (16, u2), "EXn": (32, u2), "EXw": (16, u2), "nl": (16, u2), "bt": (16, u2), "bu": (16, u2), "FL": (64, u2), "cu": (8, u2), "sl": (8, u2),
-    "gm": (16, b), "selD": (16, b), "selD2": (16, b), "selDn": (16, b), "selO": (16, b), "g64": (8, b), "ga": (16, b), "gD": (32, b),
+    "TL": (16, u2), "EXn": (32, u2), "EXw": (16, u2), "nl": (16, u2), "LL": (64, u2), "bu": (16, u2), "FL": (64, u2), "cu": (8, u2), "sl": (8, u2),
+    "gm": (16, b), "selD": (16, b), "selD2": (16, b), "selDn": (16, b), "selO": (16, b), "g64": (8, b), "gD": (56, b), "al": (64, b),
     "it": (64, i4), "k16": (16, f), "mi": (16, f), "sj": (16, f), "two": (16, f), "pw": (16, f), "wr": (16, f), "mp": (16, f), "mp2": (16, f),
     "pi": (1, i4), "gi": (1, i4), "ii": (1, i4), "ei": (1, i4), "pa": (1, i4), "pb": (1, i4), "oki": (1, i4),
     "pf": (1, f), "gf": (1, f), "iF": (1, f), "modd": (1, f), "meven": (1, f), "okc": (1, f), "il": (1, f), "tb": (1, f), "tb2": (1, f), "tb3": (1, f),
@@ -139,7 +140,7 @@ def backward(ops, pre, suc, lag, end):
 def forward(ops, pre, suc, lag, way):
     n = len(ops)
     free = {q: 0.0 for q in "vstgyx"}; line = {"dma": 0.0, "rem": 0.0}
-    end = [None] * n; left = [len(p) for p in pre]; open_ = {i for i in range(n) if not pre[i]}; out = []
+    end = [None] * n; left = [len(p) for p in pre]; open_ = {i: 0.0 for i in range(n) if not pre[i]}; out = []
 
     def ready(i):
         return max([end[j] + lag(j, i) if lag(j, i) >= 0 else 0.0 for j in pre[i]], default=0.0)
@@ -158,13 +159,13 @@ def forward(ops, pre, suc, lag, way):
                 t = max(t, max(s, free[ops[j]["q"]]) + ops[j]["t"] + lag(j, i))
         return t
     while open_:
-        st = {i: max(ready(i), free[ops[i]["q"]]) for i in open_}
+        st = {i: max(r, free[ops[i]["q"]]) for i, r in open_.items()}
         now = min(st.values())
         i = max((k for k in open_ if st[k] <= now + 1e-9), key=lambda k: (way[k], -k))
         q = ops[i]["q"]
-        if q in "vsg":
+        if q in "vsgt":
             near = {k: st[k] for k in open_ if ops[k]["q"] == q and way[k] > way[i]}
-            edge = {k for j in open_ if ops[j]["q"] != q for k in suc[j]}
+            edge = {k for j in open_ if ops[j]["q"] != q and way[j] > way[i] and st[j] < now + ops[i]["t"] for k in suc[j]}
             edge |= {m for k in edge if ops[k]["q"] != q for m in suc[k]}
             for k in edge:
                 if ops[k]["q"] == q and way[k] > way[i] and k not in open_:
@@ -180,11 +181,11 @@ def forward(ops, pre, suc, lag, way):
             e = max(now + o["t0"], line[o["kind"]]) + o["t"] - o["t0"]; line[o["kind"]] = e; end[i] = e; free[q] = now + o["busy"]
         else:
             end[i] = now + o["t"]; free[q] = end[i] if q != "x" else 0.0
-        out.append(i); open_.discard(i)
+        out.append(i); del open_[i]
         for k in suc[i]:
             left[k] -= 1
             if left[k] == 0:
-                open_.add(k)
+                open_[k] = ready(k)
     return out, end
 
 
@@ -203,8 +204,8 @@ def rank_program(g, core, T, topo):
     def IND(w, o):
         return (w[0].indirect(o[0]), w[1] + o[1], 16 * o[2], w[3], "i")
 
-    def HB(ap):
-        return (ap, [], 0, None, "")
+    def HB(ap, behind=None):
+        return (ap, behind[1] if behind else [], 0, None, "")
 
     def op(q, call, rd, wr, t, kind="", adds=False, after=(), **more):
         ops.append(dict(q=q, call=call, rd=[x for r in rd for x in r[1]], wr=[x for r in wr for x in r[1]], t=t, kind=kind, adds=adds, after=after, **more))
@@ -226,8 +227,8 @@ def rank_program(g, core, T, topo):
     chain = {}
 
     def dma(q, out, in_, nbytes):
-        chain[q] = op(q, lambda e: e.dma_start(out=out[0], in_=in_[0]), [in_], [out], DMA0 + nbytes / DMAB, "dma", t0=DMA0, busy=0.06, after=[chain[q]] if q in chain else [])
-        ops[chain[q]]["issue"] = True
+        after = [chain[q]] if q in chain and out[1] else []
+        chain[q] = op(q, lambda e: e.dma_start(out=out[0], in_=in_[0]), [in_], [out], DMA0 + nbytes / DMAB, "dma", t0=DMA0, busy=0.06, after=after)
 
     prev, nxt = T.cores[(rank - 1) % N], T.cores[(rank + 1) % N]
     mk = min(topo.mask(core, prev), topo.mask(core, nxt))
@@ -354,13 +355,13 @@ def rank_program(g, core, T, topo):
         tolist(o, "nEK", "P", G, start); tolist(o, "BL8", "FB", G, False); tolist(o, "EK", "R", G, False, rows)
 
     KB = 256
-    dma("s", A("R", 0, G), HB(T.reach[:, 0:G]), G * KB); dma("y", A("ci", 64, 1088), HB(T.cand[:]), 2 * V * KB)
-    dma("s", A("P", 0, G), HB(T.past[:, 0:G]), G * KB); dma("y", A("xF", 0, V), HB(T.x[:]), V * KB)
-    dma("s", A("R", G, V), HB(T.reach[:, G:V]), 256 * KB); dma("y", A("RF", 0, V), HB(T.reach[:]), V * KB)
-    dma("s", A("P", G, V), HB(T.past[:, G:V]), 256 * KB); dma("y", A("PF", 0, V), HB(T.past[:]), V * KB)
-    dma("y", A("th1", p1=1), HB(T.th[:]), 32); dma("y", A("XM", 0, V), HB(T.x[:]), V * KB); dma("y", A("si"), HB(T.succ[:]), 2 * V * KB)
-    send(A("R", 0, G), A("RF", V, V + G), A("RF", V + G, W), "iR", "li", 3.0)
-    send(A("P", 0, G), A("PF", V, V + G), A("PF", V + G, W), "iP", "li")
+    dma("s", A("RF", 0, G), HB(T.reach[:, 0:G]), G * KB); dma("y", A("ci", 64, 1088), HB(T.cand[:]), 2 * V * KB)
+    dma("s", A("xF", 0, V), HB(T.x[:]), V * KB); dma("y", A("PF", 0, V), HB(T.past[:]), V * KB)
+    dma("s", A("RF", G, V), HB(T.reach[:, G:V]), 256 * KB); dma("y", A("th1", p1=1), HB(T.th[:]), 32)
+    send(A("RF", 0, G), A("RF", V, V + G), A("RF", V + G, W), "iR", "li", 3.0)
+    send(A("PF", 0, G), A("PF", V, V + G), A("PF", V + G, W), "iP", "li")
+    dma("y", A("R", 0, V), HB(T.reach[:], A("RF", V, W)), V * KB); dma("y", A("P", 0, V), HB(T.past[:]), V * KB)
+    dma("y", A("si"), HB(T.succ[:]), 2 * V * KB)
 
     iota(A("pi"), [[0, 1]], 0, 1); iota(A("k16"), [[1, 16]]); iota(A("col"), [[1, 144]]); iota(A("gcol"), [[1, 8], [0, 16]])
     iota(A("it", 0, 32), [[1, 32]]); iota(A("it", 32, 48), [[16, 2], [1, 8]]); iota(A("dl"), [[512, 4], [16, 16]], V)
@@ -374,7 +375,7 @@ def rank_program(g, core, T, topo):
     tt(A("tb"), A("modd"), A("okc"), ALU.not_equal); ts(A("tb2"), A("iF"), 16.0, ALU.mult)
     ts(A("tb3"), A("tb"), 272.0, ALU.mult, A("tb2"), ALU.add); ts(A("TL"), A("k16"), A("tb3"), ALU.add)
     ts(A("I"), A("col", 0, 128), A("pf"), ALU.is_equal)
-    for n, w in (("nI", -1.0), ("I32", 1.0), ("n64I", -64.0), ("kI", -1024.0), ("I16", 16.0), ("hI", 0.5)):
+    for n, w in (("nI", -1.0), ("I32", 1.0), ("nI32", -1.0), ("n64I", -64.0), ("n4I", -4.0), ("kI", -1024.0), ("I16", 16.0), ("hI", 0.5)):
         act(A(n), A("I"), AF.Copy, scale=w)
     ts(A("ka"), A("iF"), 192.0, ALU.add, 64.0, ALU.mult); ts(A("kb"), A("iF"), -3.0, ALU.add, 64.0, ALU.mult)
     for j in range(4):
@@ -386,15 +387,15 @@ def rank_program(g, core, T, topo):
     for n, w in (("selD", 1024.0), ("selD2", 2048.0), ("selDn", -1024.0), ("selO", ORD)):
         act(A(n), A("gm"), AF.Copy, scale=w)
     ts(A("p128"), A("pf"), 128.0, ALU.add)
-    act(A("g64"), A("gm", 0, 8), AF.Copy, scale=64.0); act(A("ga", 0, 8), A("gm", 0, 8), AF.Copy, scale=A("pf")); act(A("ga", 8, 16), A("gm", 0, 8), AF.Copy, scale=A("p128"))
-    for t in range(ROUNDS):
-        act(A("gD", 8 * t, 8 * t + 8), A("gm", 0, 8), AF.Copy, scale=V + 512.0 * t)
+    act(A("g64"), A("gm", 0, 8), AF.Copy, scale=64.0)
+    for j, w in enumerate([V + 512 * t for t in range(ROUNDS)] + [W, 256, 512]):
+        act(A("gD", 8 * j, 8 * j + 8), A("gm", 0, 8), AF.Copy, scale=w + 1024.0)
     ms(A("one"), 1.0); ms(A("nord"), -ORD / 2); ms(A("c128"), 192.0 - 31.5 / 64)
     ts(A("mi"), A("k16"), A("iF"), ALU.is_equal); ts(A("sj"), A("mi"), -2.0, ALU.mult, 1.0, ALU.add); ts(A("il"), A("iF"), 10.0, ALU.is_lt)
     ts(A("IB", 0, 1), A("il"), -1.0, ALU.mult)
     for j in range(10):
         act(A("IB", 2 ** j, 2 ** (j + 1)), A("IB", 0, 2 ** j), AF.Copy, scale=A("sj", j, j + 1))
-    dma("y", A("FB", 0, V), A("IB"), V * KB)
+    cp("s", A("FB", 0, V), A("IB"))
     ms(A("two"), 2.0); ms(A("wr"), 0.0)
     scan(A("pw"), A("two"), A("wr"), ALU.mult, ALU.add, 0.25); tt(A("mp"), A("mi"), A("pw"), ALU.mult); red(A("tb"), A("mp"), ALU.add)
     tt(A("wcol"), A("tb"), A("il"), ALU.mult); ts(A("w8"), A("wcol"), 8192.0, ALU.mult)
@@ -417,18 +418,21 @@ def rank_program(g, core, T, topo):
     for j in range(4):
         ts(A("thK", 8 * j, 8 * j + 8), A("th2"), 1024.0, ALU.mult)
     cp("v", A("thC"), A("thK"))
-    ts(A("Fp", 0, 16), A("dl", 0, 16), -float(V), ALU.add)
-    for j in (1, 2):
+    for j in range(3):
         ts(A("Fp", 16 * j, 16 * j + 16), A("dl", 0, 16), 256.0 * j - V, ALU.add)
+    for j in range(4):
+        cp("s", A("al", 16 * j, 16 * j + 16), A("Fp", 0, 16))
+    cp("s", A("wins", 32, 64), A("al", 0, 32)); ms(A("c511"), 511.5)
 
     cklist(0)
     fill_ext("s", "XM", 0, "xF"); ms(A("xF", 0, V, 4), BIGX)
     cp("v", ext("CF", 0, 0, 256), A("ci", 64, 1088, 4))
     keyinit(0); distances(0)
-    fill_ext("s", "P", 0); fill_ext("s", "R", 0)
+    fill_ext("s", "P", 0, "PF"); fill_ext("s", "R", 0, "RF")
     cp("v", A("CF", 0, V), A("ci", 64, 1088))
     iota(A("SO", 0, V), [[0, V]]); iota(A("SE"), [[0, V]])
     dma("y", A("SO", 0, V, p0=1, ps=2), HB(T.succ[1:128:2, :]), V * KB); dma("y", A("SE", p0=0, ps=2), HB(T.succ[0:128:2, :]), V * KB)
+    dma("y", A("XM", 0, V), HB(T.x[:]), V * KB)
     cp("v", A("SL0"), A("si", 0, V, 2)); cp("v", A("SL1"), A("si", 1, V, 2))
     for s, d in (("RF", "GR"), ("PF", "GP")):
         dma("y", A(d + "a", 0, G), A(s, V, V + G), G * KB); dma("y", A(d + "b", 0, G), A(s, V + G, W), G * KB)
@@ -444,7 +448,11 @@ def rank_program(g, core, T, topo):
             fill_ext("g", "CF", u, copies=1); fill_ext("g", "SO", u, copies=1)
         for kk in range(8):
             s = (512 * kk, 512 * kk + 512); off = A(ck, 32 * kk, 32 * kk + 32)
-            tt(A("oR", *s), IND(A("RF"), off), ext("P", t), ALU.is_le); keymm(kk, "oR", "selO")
+            if kk in CMP_R[t]:
+                by_scalar(A("oR", *s), A("RF"), off, ext("P", t), -1, AF.Relu, kk, A("one"))
+            else:
+                tt(A("oR", *s), IND(A("RF"), off), ext("P", t), ALU.is_le)
+            keymm(kk, "oR", "selO")
             if kk in CMP_S[t]:
                 by_scalar(A("oP", *s), A("PF"), off, ext("R", t), 1, AF.Relu, kk, A("one"))
             else:
@@ -475,7 +483,7 @@ def rank_program(g, core, T, topo):
         fb = IND(A("FB", 0, V), A("nl"))
         tt(A("Bk"), fb, A("Kr"), ALU.add)
         act(A("Ae"), fb, AF.Identity, bias=A("cAe"), scale=A("sAe"))
-        ts(A("Ao"), fb, A("sAo"), ALU.mult, A("cAo"), ALU.add)
+        act(A("Ao"), fb, AF.Identity, bias=A("cAo"), scale=A("sAo"))
         for s, gg in enumerate((0, 2, 4, 6, 1, 3, 5, 7)):
             for h in (1, 0):
                 z, m = A("ps%d" % (2 + 2 * h + s % 2), 0, 256), A("mx", 16 * h + gg, 16 * h + gg + 1)
@@ -486,49 +494,65 @@ def rank_program(g, core, T, topo):
                 else:
                     red(m, z, ALU.max)
         tolist(A("ps6", 16, 32), "BL", "Bk", 256, True)
-        ts(A("blf"), A("ps6", 16, 32), 511.5, ALU.add)
+        for j in (0, 16):
+            act(A("wins", j, j + 16), A("ps6", 16, 32), AF.Identity, bias=A("c511"))
+        tt(A("RW", 0, 256), IND(A("RF", 0, V), A("nl")), ext("R", t, 0, 256), ALU.min)
+        cp("s", A("RW", 256, 512), A("RF", t, V, 4)); cp("s", A("RW", 512, 768), ext("R", t, 0, 256))
         tt(A("lose"), A("mx"), A("thr"), ALU.is_gt)
         tt(A("W2"), IND(A("lose"), A("EXw")), A("DM", 0, 256), ALU.mult)
+        mm(A("ps6", 32, 96), A("I"), A("al"), True); mm(A("ps6", 32, 96), A("kI"), A("ones", 0, 64))
         for j in range(4):
-            h = j // 2
-            mm(A("ps6", 32 + 8 * h, 40 + 8 * h), A("W2", 128 * h, 128 * h + 128), A("gD", 8 * t, 8 * t + 8) if j % 2 else A("ga", 8 * h, 8 * h + 8), j % 2 == 0)
-        tt(A("btf"), A("ps6", 32, 48), A("blf"), ALU.max); cp("v", A("bt"), A("btf"))
-        bt = A("bt")
-        cp("v", IND(win("FB", t), bt), A("IB", t, V, 4))
-        tolist(A("ps6", 64, 128), "BL", "FB", V, True)
-        ts(A("FL"), A("ps6", 64, 128), 511.5, ALU.add)
-        tt(A("Rn"), IND(win("R", t), bt), ext("R", t, 256, 512), ALU.min); cp("s", A("R", t, V, 4), A("Rn"))
+            for h in (0, 1):
+                c = 8 * (t if j == 0 else 3 + j)
+                mm(A("ps6", 32 + 16 * j + 8 * h, 40 + 16 * j + 8 * h), A("W2", 128 * h, 128 * h + 128), A("gD", c, c + 8))
+        tt(A("LLf"), A("ps6", 32, 96), A("wins"), ALU.max); cp("v", A("LL"), A("LLf"))
+        bt = A("LL", 0, 16)
+        cp("s", A("RF", t, V, 4), IND(A("RW"), A("LL", 32, 48))); cp("s", A("R", t, V, 4), IND(A("RW"), A("LL", 48, 64)))
         tt(A("sn"), IND(win("SO", t), bt), A("SE", t, V, 4), ALU.add); cp("v", A("SL%d" % par, t // 2, 512, 2), A("sn"))
-        cp("v", A("RF", 0, 512), IND(A("R", 0, V), A("FL", 0, 32))); cp("s", A("RF", 512, V), IND(A("R", 0, V), A("FL", 32, 64)))
+        cp("v", IND(A("RF"), A("LL", 16, 32)), A("RW", 0, 256))
         tt(A("xs"), IND(win("XM", t), bt), ext("XM", t, 256, 512), ALU.add)
-        ts(A("xi"), A("xs"), -0.5, ALU.add, 0.5, ALU.mult); cp("v", A("XM", t, V, 4), A("xi"))
-        tt(A("nh2"), A("nh"), A("dl", 16 * t, 16 * t + 16), ALU.mult); tt(A("buf"), A("nh2"), A("blf"), ALU.max); cp("v", A("bu"), A("buf"))
+        ts(A("xi"), A("xs"), -0.5, ALU.add, 0.5, ALU.mult); cp("v" if last else "g", A("XM", t, V, 4), A("xi"))
+        tt(A("nh2"), A("nh"), A("dl", 16 * t, 16 * t + 16), ALU.mult); tt(A("buf"), A("nh2"), A("wins", 0, 16), ALU.max); cp("v", A("bu"), A("buf"))
 
         def candidates():
-            tt(A("dC"), IND(win("CF", t), A("bu")), A("ci", 64 + t, 1088, 4), ALU.subtract)
+            o = [A("ps1", 256 + 128 * h, 384 + 128 * h) for h in (0, 1)]; both = A("ps1", 256, 512)
+            own = [ext("CF", t, 128 * h, 128 * h + 128) for h in (0, 1)]
             for h in (0, 1):
-                o = A("ps1", 256 + 128 * h, 384 + 128 * h)
-                mm(o, A("fl", 128 * h, 128 * h + 128), A("hI"), True); mm(o, A("ones"), A("hI"))
-            tt(A("oi"), A("ps1", 256, 512), A("dC"), ALU.mult); tt(A("CF", t, V, 4), A("oi"), ext("CF", t, 0, 256), ALU.add)
+                mm(o[h], A("fl", 128 * h, 128 * h + 128), A("hI"), True); mm(o[h], A("ones"), A("hI"))
+            if last:
+                tt(A("dC"), IND(win("CF", t), A("bu")), A("ci", 64 + t, 1088, 4), ALU.subtract)
+                tt(A("oi"), both, A("dC"), ALU.mult); tt(A("CF", t, V, 4), A("oi"), ext("CF", t, 0, 256), ALU.add)
+                return
+            cp("s", A("fn"), both); cp("s", A("dC"), IND(win("CF", t), A("bu")))
+            for h in (0, 1):
+                mm(o[h], A("I32"), A("dC", 128 * h, 128 * h + 128), True); mm(o[h], A("nI32"), own[h])
+            tt(A("oi"), both, A("fn"), ALU.mult)
+            for h in (0, 1):
+                mm(o[h], A("I32"), A("oi", 128 * h, 128 * h + 128), True); mm(o[h], A("I32"), own[h])
+            cp("s", A("CF", t, V, 4), both)
         if last:
             candidates()
             dma("y", HB(T.yx[:]), A("XM", 0, V), V * KB); dma("y", HB(T.yc[:]), A("CF", 0, V), 2 * V * KB)
         else:
+            cp("v", IND(win("FB", t), bt), A("IB", t, V, 4))
+            tolist(A("ps6", 96, 160), "BL", "FB", V, True)
+            ts(A("FL"), A("ps6", 96, 160), 511.5, ALU.add)
             tt(A("Pn"), IND(win("P", t), bt), ext("P", t, 256, 512), ALU.max); cp("g", A("P", t, V, 4), A("Pn"))
             ts(A("SO", t, V, 4), A("sn"), A("okc"), ALU.mult)
-            ms(A("XM", u, V, 4), BIGX)
+            iota(A("XM", u, V, 4), [[0, 256]], int(BIGX))
             cp("s", A("xF", 0, V), IND(A("XM", 0, V), A("FL"))); cp("s", A("PF", 0, V), IND(A("P", 0, V), A("FL")))
             mm(A("ps4", 0, 32), A("ones"), A("lose"), True); red(A("Mf"), A("ps4", 0, 32), ALU.add)
             ts(A("Mi"), A("Mf"), -1.0, ALU.mult, 4096.0, ALU.add); ts(A("Mj"), A("Mi"), 31, ALU.bitwise_and)
             ts(A("Mk"), A("Mj"), 1024.0, ALU.mult); ts(A("thC"), A("thK"), A("Mk"), ALU.add)
-            ts(A("FLf"), A("ps6", 64, 112), 511.5, ALU.add)
+            ts(A("FLf"), A("ps6", 96, 144), 511.5, ALU.add)
             tt(A("dF1"), A("FLf"), A("Fp"), ALU.subtract); ts(A("dF2"), A("FLf"), float(G), ALU.is_lt); tt(A("dF"), A("dF1"), A("dF2"), ALU.mult)
             sums(True, range(1 - par, 16, 2))
         mm(A("ps5"), A("I"), A("R", par, V, 2), True)
         for c0, c1 in ((0, 6), (6, 8)) if not last else ((0, 4), (4, 7), (7, 8)):
             for c in range(c0, c1):
-                for d in (2 * c, 2 * c + 1):
-                    cp("v" if d in G3_V[t] else "s", A("g3", 512 * d, 512 * d + 512), IND(A("RF"), A("SL%d" % par, 32 * d, 32 * d + 32)))
+                who = ["v" if d in G3_V[t] else "s" for d in (2 * c, 2 * c + 1)]
+                for q, d0, d1 in [(who[0], 2 * c, 2 * c + 2)] if who[0] == who[1] else [(who[0], 2 * c, 2 * c + 1), (who[1], 2 * c + 1, 2 * c + 2)]:
+                    cp(q, A("g3", 512 * d0, 512 * d1), IND(A("RF"), A("SL%d" % par, 32 * d0, 32 * d1)))
                 s = (1024 * c, 1024 * c + 1024)
                 scan(A("s3", *s), A("rst"), A("g3", *s), ALU.max, ALU.min)
             tt(A("R", par + 128 * c0, 128 * c1, 2), A("s3", 1024 * c0 + 15, 1024 * c1, 16), A("ps5", 64 * c0, 64 * c1), ALU.min)
@@ -560,6 +584,11 @@ def rank_program(g, core, T, topo):
         if t + 2 < ROUNDS:
             fill_ext("g", "R", t + 2)
         keyinit(u); distances(u); candidates()
+        o = A("ps7", 16, 32)
+        for i in range(16):
+            mm(o, A("BL", 15 - i, 143 - i), A("FB", u + 4 * i, V, 64), i == 0)
+        mm(o, A("n4I"), A("al", 0, 16))
+        ts(A("nsf"), o, u - 511.5, ALU.not_equal, 256.0, ALU.mult); tt(A("wins", 32, 48), A("nsf"), A("al", 0, 16), ALU.add)
         for k, n in ((1, "P"), (0, "R")):
             for j, d in enumerate("ab"):
                 land = "L%s%d" % (d, t)

import math
from concourse.bass import DstId, RemoteDMATransfer
from concourse.mybir import AluOpType as ALU, AxisListType, ActivationFunctionType as AF

V, G, W, N, ROUNDS = 1024, 768, 2560, 4, 4
BIGX = 8192.0
EQ = 1048576.0
ORD = 2.0 ** 30
HUGE = 2.0 ** 80
CMP_S = ((5, 6, 7),) + ((2, 3, 4, 5, 6, 7),) * 3
CMP_R = ((0, 1, 2, 3), (), (), ())
ABS_V = ((), (), (), ())
X_S = ((7,), (), (), ())
G3_V = ((0, 1, 2),) * 3 + ((0, 1, 2, 3, 4),)
GH_V = (("R", "a"),)

b, f, i4, u2 = "bfloat16", "float32", "int32", "uint16"
_S = {
    "R": (3072, b), "P": (3072, b), "XM": (3072, b), "xF": (W, b), "RF": (W + 256, b), "PF": (W, b), "FB": (3072, b), "IB": (V, b),
    "ci": (1152, i4), "CF": (3072, f), "SO": (3072, i4), "SE": (V, i4), "si": (V, i4), "SL0": (512, u2), "SL1": (512, u2),
    "T1": (544, i4), "CK0": (256, u2), "CK1": (256, u2), "CK2": (256, u2), "CK3": (256, u2), "NH": (256, b),
    "dx": (4096, b), "ab": (4096, b), "oR": (4096, b), "oP": (4096, b), "pc": (4096, b), "g3": (8192, b), "s3": (8192, b),
    "ks": (512, f), "rst": (1024, b), "dk": (1024, b), "Wn": (512, b), "DM": (512, b), "KD": (512, b),
    "Kr": (256, b), "Ae": (256, b), "Ao": (256, b), "Bk": (256, b), "fn": (256, b), "W2": (256, b), "fl": (256, b),
    "RW": (768, b), "Pn": (256, b), "xs": (256, f), "xi": (256, i4), "sn": (256, f), "dC": (256, f), "oi": (256, f),
    "rs56": (448, b), "sv": (448, b), "f1": (448, b), "f2": (448, b), "f3": (128, b), "srow": (128, b),
    "col": (144, b), "EK": (144, b), "nEK": (144, b), "BL": (144, b), "BL8": (144, b),
    "ones": (128, b), "I": (128, b), "nI": (128, b), "I32": (128, f), "nI32": (128, f), "n64I": (128, b), "n4I": (128, b), "kI": (128, b), "I16": (128, b), "hI": (128, b),
    "B16": (128, b), "nB16": (128, b), "nLs": (128, b), "gcol": (128, b),
    "wi": (32, i4), "wn": (32, i4), "wd": (64, i4), "wD": (32, i4), "mx": (32, f), "thr": (32, f), "thb": (32, f), "nb": (32, f), "bs": (8, f),
    "lose": (32, b), "thK": (32, f), "thC": (32, f), "th1": (8, i4), "th2": (8, i4), "Mf": (1, f), "Mi": (1, i4), "Mj": (1, i4), "Mk": (1, f),
    "wins": (64, f), "LLf": (64, f), "nsf": (16, f), "c511": (1, f), "nh": (16, f), "nh2": (16, f), "buf": (16, f), "dl": (64, f), "FLf": (48, f), "dF": (48, f), "dF1": (48, f), "dF2": (48, f),
    "Fp": (48, f), "go": (48, f), "go2": (48, f), "Wo": (48, f), "ch": (56, b), "cc": (56, b), "cw": (56, f),
    "TL": (16, u2), "EXn": (32, u2), "EXw": (16, u2), "nl": (16, u2), "LL": (64, u2), "bu": (16, u2), "FL": (64, u2), "cu": (8, u2), "sl": (8, u2),
    "gm": (16, b), "selD": (16, b), "selD2": (16, b), "selDn": (16, b), "selO": (16, b), "g64": (8, b), "gD": (56, b), "al": (64, b),
    "it": (64, i4), "k16": (16, f), "mi": (16, f), "sj": (16, f), "two": (16, f), "pw": (16, f), "wr": (16, f), "mp": (16, f), "mp2": (16, f),
    "pi": (1, i4), "gi": (1, i4), "ii": (1, i4), "ei": (1, i4), "pa": (1, i4), "pb": (1, i4), "oki": (1, i4),
    "pf": (1, f), "gf": (1, f), "iF": (1, f), "modd": (1, f), "meven": (1, f), "okc": (1, f), "il": (1, f), "tb": (1, f), "tb2": (1, f), "tb3": (1, f),
    "wcol": (1, f), "w8": (1, f), "wrow": (1, f), "e15": (1, f), "sAe": (1, f), "sAo": (1, f), "cAe": (1, f), "cAo": (1, f), "ka": (1, f), "kb": (1, f),
    "p128": (1, f), "c0": (1, f), "c1": (1, f), "one": (1, f), "nord": (1, f), "c128": (1, f),
    "GRa": (896, b), "GRb": (896, b), "GPa": (896, b), "GPb": (896, b),
}
for _r in range(ROUNDS - 1):
    for _n in ("MS", "La", "Lb"):
        _S["%s%d" % (_n, _r)] = (312, u2)
_WHERE, _POOL, SCRATCH = {}, {f: 0, i4: 0, u2: 0, b: 0}, {}
for _n, (_c, _d) in _S.items():
    if _c <= 144:
        _WHERE[_n] = ("pool_" + _d, _POOL[_d]); _POOL[_d] += _c + (-_c) % 16
    else:
        SCRATCH[_n] = ("sbuf", [128, _c], _d); _WHERE[_n] = (_n, 0)
for _d in _POOL:
    SCRATCH["pool_" + _d] = ("sbuf", [128, _POOL[_d]], _d)
for _r in range(8):
    _n = "ps%d" % _r
    SCRATCH[_n] = ("psum", [128, 512], f); _WHERE[_n] = (_n, 0); _S[_n] = (512, f)
ND = 28
SEMAPHORES = ["qv", "qs", "qt", "qg", "iR", "iP", "loc", "li"] + ["a%d" % r for r in range(ROUNDS - 1)] + ["d%d" % k for k in range(ND)]

CYC, GATH, SCAT, TCYC, WAKE, DMA0, DMAB, REM0, REMB = 0.9e-3, 1.5, 3.5, 0.45e-3, 0.1, 1.8, 180e3, 3.0, 70e3
IDLE, PASSES = 0.5, 6
_ORDER = {}


def meets(a0, a1, st, e0, e1, es):
    return e0 < a1 and a0 < e1 and (e0 - a0) % math.gcd(st, es) == 0


def covers(a0, a1, st, e0, e1, es):
    return a0 <= e0 and e1 <= a1 and (st == 1 or (es == st and (e0 - a0) % st == 0))


def needs(ops):
    hist, bank, pre = {}, {}, []
    for me, o in enumerate(ops):
        need = set(o["after"])
        for regs, isw in ((o["rd"], False), (o["wr"], True)):
            for n, a0, a1, st in regs:
                if n[:2] == "ps":
                    last, kind, free = bank.get(n, (set(), None, set()))
                    k = ("add" if o["adds"] else None) if isw else "r" + o["q"]
                    if k is not None and k == kind:
                        need |= last; free.add(me)
                    elif k is not None:
                        last = (free or last) - {me}; need |= last; bank[n] = (last, k, {me})
                    else:
                        need |= free or last; bank[n] = ({me}, None, set())
                    continue
                h = hist.setdefault(n, [])
                need.update(e[3] for e in h if (e[4] or isw) and meets(a0, a1, st, *e[:3]))
                if isw:
                    h[:] = [e for e in h if not covers(a0, a1, st, *e[:3])]
                h.append((a0, a1, st, me, isw))
        need.discard(me); pre.append(need)
    return pre


def order(ops):
    pre = needs(ops); n = len(ops)
    suc = [[] for _ in ops]
    for i, p in enumerate(pre):
        for j in p:
            suc[j].append(i)

    def lag(j, i):
        if j in ops[i]["after"] and ops[i]["kind"] == "dma":
            return ops[j]["busy"] - ops[j]["t"]
        return 0.0 if ops[j]["q"] == ops[i]["q"] == "t" or ops[i]["q"] == "x" else WAKE
    way = [0.0] * n
    for i in reversed(range(n)):
        way[i] = ops[i]["t"] + max([lag(i, k) + way[k] for k in suc[i]], default=0.0)
    best = None
    for _ in range(PASSES):
        out, end = forward(ops, pre, suc, lag, way)
        if best is None or max(end) < best[0]:
            best = (max(end), out)
        way = backward(ops, pre, suc, lag, end)
    return best[1]


def backward(ops, pre, suc, lag, end):
    n = len(ops); way = [None] * n; left = [len(s) for s in suc]
    free = {}; open_ = {i: 0.0 for i in range(n) if not suc[i]}
    while open_:
        key = lambda i: ops[i]["kind"] or ops[i]["q"]
        st = {i: max(r, free.get(key(i), 0.0)) for i, r in open_.items()}
        now = min(st.values())
        i = max((k for k in open_ if st[k] <= now + 1e-9), key=lambda k: (end[k], k))
        o = ops[i]; way[i] = now + o["t"]
        if o["q"] != "x":
            free[key(i)] = way[i] - o.get("t0", 0.0)
        del open_[i]
        for j in pre[i]:
            left[j] -= 1
            if left[j] == 0:
                open_[j] = max(0.0, max(way[k] + lag(j, k) for k in suc[j]))
    return way


def forward(ops, pre, suc, lag, way):
    n = len(ops)
    free = {q: 0.0 for q in "vstgyx"}; line = {"dma": 0.0, "rem": 0.0}
    end = [None] * n; left = [len(p) for p in pre]; open_ = {i: 0.0 for i in range(n) if not pre[i]}; out = []

    def ready(i):
        return max([end[j] + lag(j, i) if lag(j, i) >= 0 else 0.0 for j in pre[i]], default=0.0)

    def soon(i, depth):
        t = 0.0
        for j in pre[i]:
            if end[j] is not None:
                t = max(t, end[j] + lag(j, i))
            elif depth == 0 or ops[j]["q"] == ops[i]["q"]:
                return None
            else:
                s = soon(j, depth - 1)
                if s is None:
                    return None
                t = max(t, max(s, free[ops[j]["q"]]) + ops[j]["t"] + lag(j, i))
        return t
    while open_:
        st = {i: max(r, free[ops[i]["q"]]) for i, r in open_.items()}
        now = min(st.values())
        i = max((k for k in open_ if st[k] <= now + 1e-9), key=lambda k: (way[k], -k))
        q = ops[i]["q"]
        if q in "vsgt":
            near = {k: st[k] for k in open_ if ops[k]["q"] == q and way[k] > way[i]}
            edge = {k for j in open_ if ops[j]["q"] != q and way[j] > way[i] and st[j] < now + ops[i]["t"] for k in suc[j]}
            edge |= {m for k in edge if ops[k]["q"] != q for m in suc[k]}
            for k in edge:
                if ops[k]["q"] == q and way[k] > way[i] and k not in open_:
                    s = soon(k, 3)
                    if s is not None:
                        near[k] = max(s, now)
            hold = [s for k, s in near.items() if s < now + ops[i]["t"] and
                    max(s + way[k], s + ops[k]["t"] + way[i]) + IDLE * (s - now) < max(now + way[i], now + ops[i]["t"] + way[k])]
            if hold and min(hold) > now + 1e-6:
                free[q] = min(hold); continue
        o = ops[i]
        if o["kind"] in line:
            e = max(now + o["t0"], line[o["kind"]]) + o["t"] - o["t0"]; line[o["kind"]] = e; end[i] = e; free[q] = now + o["busy"]
        else:
            end[i] = now + o["t"]; free[q] = end[i] if q != "x" else 0.0
        out.append(i); del open_[i]
        for k in suc[i]:
            left[k] -= 1
            if left[k] == 0:
                open_[k] = ready(k)
    return out, end


def rank_program(g, core, T, topo):
    rank = T.rank_of(core)
    if rank is None:
        return
    ops = []

    def A(n, c0=0, c1=None, st=1, p0=0, p1=128, ps=1):
        t, o = _WHERE[n]
        c1 = _S[n][0] if c1 is None else c1
        ap = T[t][p0:p1:ps, o + c0:o + c1:st] if ps > 1 or st > 1 else T[t][p0:p1, o + c0:o + c1]
        return (ap, [(n, c0, c1, st)], len(range(c0, c1, st)), _S[n][1], "")

    def IND(w, o):
        return (w[0].indirect(o[0]), w[1] + o[1], 16 * o[2], w[3], "i")

    def HB(ap, behind=None):
        return (ap, behind[1] if behind else [], 0, None, "")

    def op(q, call, rd, wr, t, kind="", adds=False, after=(), **more):
        ops.append(dict(q=q, call=call, rd=[x for r in rd for x in r[1]], wr=[x for r in wr for x in r[1]], t=t, kind=kind, adds=adds, after=after, **more))
        return len(ops) - 1

    def cost(out, a, per):
        if a[4]:
            return 0.06 + out[2] * GATH * CYC
        if out[4]:
            return 0.05 + a[2] * SCAT * CYC
        return max(64, out[2] * per) * CYC

    def half(*x):
        return 0.5 if all(y[3] in (b, u2) for y in x) else 1

    def in_ps(x):
        return x[1][0][0][:2] == "ps"

    chain = {}

    def dma(q, out, in_, nbytes):
        after = [chain[q]] if q in chain and out[1] else []
        chain[q] = op(q, lambda e: e.dma_start(out=out[0], in_=in_[0]), [in_], [out], DMA0 + nbytes / DMAB, "dma", t0=DMA0, busy=0.06, after=after)

    prev, nxt = T.cores[(rank - 1) % N], T.cores[(rank + 1) % N]
    mk = min(topo.mask(core, prev), topo.mask(core, nxt))
    ne = len([e for e in topo.engines(core, prev) if mk >> e & 1])
    ids = []
    for d in (prev, nxt):
        rid, pid, _ = topo.addr(d); ids.append(DstId(rid=rid, pnc=pid))

    def send(src, to_prev, to_next, sem, loc="loc", first=0.0):
        call = lambda e: e.remote_dma_fused([RemoteDMATransfer(dst_ids=ids, dma_engine_mask=mk, remote_sem=T.sem[sem], srcs=[src[0]], dsts=[to_prev[0], to_next[0]])], local_sem=T.sem[loc])
        s = op("g", call, [src], [], REM0 + first + 2 * 256 * src[2] / REMB, "rem", t0=REM0 + first, busy=0.3, loc=loc)
        op("x", sem, [], [to_prev, to_next], 0.0, after=[s])

    def cp(q, out, in_):
        if q == "s":
            act(out, in_, AF.Copy)
        elif q == "g":
            sel(out, in_, [[0, out[2]]], ALU.is_equal, 0.0, 0, 0)
        else:
            op("v", lambda e: e.tensor_copy(out=out[0], in_=in_[0]), [in_], [out], cost(out, in_, half(out, in_)))

    def tt(out, a, c, o):
        op("v", lambda e: e.tensor_tensor(out=out[0], in0=a[0], in1=c[0], op=o), [a, c], [out], cost(out, a, 1 if in_ps(a) or in_ps(c) else 2))

    def ts(out, a, s1, o1, s2=None, o2=None):
        rd = [a] + [s for s in (s1, s2) if isinstance(s, tuple)]
        kw = dict(out=out[0], in0=a[0], scalar1=s1[0] if isinstance(s1, tuple) else s1, scalar2=s2[0] if isinstance(s2, tuple) else s2, op0=o1)
        if o2 is not None:
            kw["op1"] = o2
        op("v", lambda e: e.tensor_scalar(**kw), rd, [out], cost(out, a, half(out, a)))

    def act(out, in_, fn, bias=None, scale=None, accum=None):
        kw = {}; rd = [in_]; wr = [out]
        for k, x in (("bias", bias), ("scale", scale)):
            if isinstance(x, tuple):
                kw[k] = x[0]; rd.append(x)
            elif x is not None:
                kw[k] = x
        if accum is not None:
            kw["accum_out"] = accum[0]; wr.append(accum)
        op("s", lambda e: e.activation(out=out[0], in_=in_[0], func=fn, **kw), rd, wr, cost(out, in_, 1) + (0.02 if accum else 0))

    def ms(out, c):
        op("v", lambda e: e.memset(out[0], c), [], [out], cost(out, out, half(out)))

    group = {}

    def mm(out, l, r, start=False):
        n = out[1][0][0]
        if start:
            group[n] = len(ops)
        op("t", lambda e, stop: e.matmul(out=out[0], lhsT=l[0], rhs=r[0], start=start, stop=stop), [l, r], [out],
           max(64, r[2]) * TCYC * (4 if l[3] == f else 1), adds=not start, group=group[n])

    def iota(out, pat, base=0, cmul=0):
        kw = {} if out[3] == i4 else {"allow_small_or_imprecise_dtypes": True}
        op("g", lambda e: e.iota(out[0], pat, base, cmul, **kw), [], [out], 0.23 + 2 * out[2] * CYC)

    def sel(out, in_, pat, o, fill, base, cmul):
        op("g", lambda e: e.affine_select(out[0], in_[0], pat, o, fill, base, cmul), [in_], [out], 0.27 + 2 * out[2] * CYC)

    def red(out, in_, o):
        op("v", lambda e: e.tensor_reduce(out=out[0], in_=in_[0], axis=AxisListType.X, op=o), [in_], [out], max(64, in_[2]) * CYC)

    def scan(out, d0, d1, o0, o1, init=0.0):
        op("v", lambda e: e.tensor_tensor_scan(out=out[0], data0=d0[0], data1=d1[0], initial=init, op0=o0, op1=o1), [d0, d1], [out], cost(out, d1, half(out, d0, d1)))

    def turn(out, in_):
        op("v", lambda e: e.transpose(out=out[0], in_=in_[0]), [in_], [out], cost(out, in_, 1))

    def ext(n, t, c0=0, c1=512):
        return A(n, V + 512 * t + c0, V + 512 * t + c1)

    def win(n, t):
        return A(n, 0, V + 512 * t + 256)

    def fill_ext(q, n, t, src=None, copies=2):
        for h in range(copies):
            cp(q, ext(n, t, 256 * h, 256 * h + 256), A(src or n, t, V, 4))

    def tolist(out, w, src, n, start, rows=range(16)):
        for k, i in enumerate(rows):
            mm(out, A(w, 15 - i, 143 - i), A(src, i, n, 16), start and k == 0)

    def cklist(t):
        turn(A("T1", 0, 256), A("ci", 64 + t, 1088, 4)); turn(A("T1", 256, 544), A("ci", t, 1152, 4))
        cp("v", A("CK%d" % t), IND(A("T1"), A("TL")))

    def keyinit(t):
        act(A("NH"), ext("CF", t, 0, 256), AF.Identity, bias=A("c128"), scale=1.0 / 64)
        mm(A("ps0"), A("ones"), A("KD"), True)
        for h in (0, 1):
            lo, hi, nh = A("ps0", 256 * h, 256 * h + 128), A("ps0", 256 * h + 128, 256 * h + 256), A("NH", 128 * h, 128 * h + 128)
            mm(lo, ext("CF", t, 128 * h, 128 * h + 128), A("I32")); mm(lo, nh, A("n64I")); mm(hi, nh, A("I"))

    def keymm(kk, buf, w):
        for k in (2 * kk, 2 * kk + 1):
            for h in (0, 1):
                mm(A("ps0", 256 * h + k, 256 * h + 256, 16), A(buf, 256 * k + 128 * h, 256 * k + 128 * h + 128), A(w))

    nb = [0]

    def by_scalar(out, table, off, own, sign, fn, kk, bias=None):
        s = A("pc", 512 * kk, 512 * kk + 512); bank = A("ps%d" % (2 + nb[0] % 2)); nb[0] += 1
        cp("s", s, IND(table, off))
        mm(bank, A(("I", "nI")[sign < 0]), s, True); mm(bank, A(("nI", "I")[sign < 0]), own)
        act(out, bank, fn, bias=bias)

    def distances(t):
        for kk in range(8):
            s = (512 * kk, 512 * kk + 512); off = A("CK%d" % t, 32 * kk, 32 * kk + 32)
            if kk in X_S[t]:
                by_scalar(A("ab", *s), A("xF"), off, ext("XM", t), 1, AF.Abs, kk)
            else:
                tt(A("dx", *s), IND(A("xF"), off), ext("XM", t), ALU.subtract)
                if kk in ABS_V[t]:
                    ts(A("ab", *s), A("dx", *s), 0.0, ALU.max); keymm(kk, "dx", "selDn")
                else:
                    act(A("ab", *s), A("dx", *s), AF.Abs)
            keymm(kk, "ab", "selD2" if kk in ABS_V[t] else "selD")

    def sums(start, rows):
        o = A("ps1", 0, 48)
        tolist(o, "nEK", "P", G, start); tolist(o, "BL8", "FB", G, False); tolist(o, "EK", "R", G, False, rows)

    KB = 256
    dma("s", A("RF", 0, G), HB(T.reach[:, 0:G]), G * KB); dma("y", A("ci", 64, 1088), HB(T.cand[:]), 2 * V * KB)
    dma("s", A("xF", 0, V), HB(T.x[:]), V * KB); dma("y", A("PF", 0, V), HB(T.past[:]), V * KB)
    dma("s", A("RF", G, V), HB(T.reach[:, G:V]), 256 * KB); dma("y", A("th1", p1=1), HB(T.th[:]), 32)
    send(A("RF", 0, G), A("RF", V, V + G), A("RF", V + G, W), "iR", "li", 3.0)
    send(A("PF", 0, G), A("PF", V, V + G), A("PF", V + G, W), "iP", "li")
    dma("y", A("R", 0, V), HB(T.reach[:], A("RF", V, W)), V * KB); dma("y", A("P", 0, V), HB(T.past[:]), V * KB)
    dma("y", A("si"), HB(T.succ[:]), 2 * V * KB)

    iota(A("pi"), [[0, 1]], 0, 1); iota(A("k16"), [[1, 16]]); iota(A("col"), [[1, 144]]); iota(A("gcol"), [[1, 8], [0, 16]])
    iota(A("it", 0, 32), [[1, 32]]); iota(A("it", 32, 48), [[16, 2], [1, 8]]); iota(A("dl"), [[512, 4], [16, 16]], V)
    iota(A("DM"), [[0, 32], [1, 16]]); iota(A("sv"), [[16, 8], [0, 56]]); iota(A("srow"), [[1, 128]])
    ms(A("ci", 0, 64), 0); ms(A("ci", 1088, 1152), 0); ms(A("xF", V, W), BIGX); ms(A("ones"), 1.0)
    ts(A("gi"), A("pi"), 4, ALU.arith_shift_right); ts(A("ii"), A("pi"), 15, ALU.bitwise_and)
    ts(A("ei"), A("gi"), 1, ALU.bitwise_and); ts(A("oki"), A("pi"), 1, ALU.bitwise_and)
    for o, s in (("pf", "pi"), ("gf", "gi"), ("iF", "ii"), ("modd", "ei"), ("okc", "oki")):
        cp("v", A(o), A(s))
    ts(A("meven"), A("modd"), -1.0, ALU.mult, 1.0, ALU.add)
    tt(A("tb"), A("modd"), A("okc"), ALU.not_equal); ts(A("tb2"), A("iF"), 16.0, ALU.mult)
    ts(A("tb3"), A("tb"), 272.0, ALU.mult, A("tb2"), ALU.add); ts(A("TL"), A("k16"), A("tb3"), ALU.add)
    ts(A("I"), A("col", 0, 128), A("pf"), ALU.is_equal)
    for n, w in (("nI", -1.0), ("I32", 1.0), ("nI32", -1.0), ("n64I", -64.0), ("n4I", -4.0), ("kI", -1024.0), ("I16", 16.0), ("hI", 0.5)):
        act(A(n), A("I"), AF.Copy, scale=w)
    ts(A("ka"), A("iF"), 192.0, ALU.add, 64.0, ALU.mult); ts(A("kb"), A("iF"), -3.0, ALU.add, 64.0, ALU.mult)
    for j in range(4):
        act(A("KD", 128 * j, 128 * j + 128), A("I"), AF.Copy, scale=A(("ka", "kb")[j % 2]))
    ts(A("B16"), A("gcol"), A("gf"), ALU.is_equal); act(A("nB16"), A("B16"), AF.Copy, scale=-1.0)
    sel(A("nLs"), A("nB16"), [[-1, 128]], ALU.is_gt, 0.0, 0, 1)
    for h in (0, 8):
        cp("v", A("gm", h, h + 8), A("B16", 0, 128, 16))
    for n, w in (("selD", 1024.0), ("selD2", 2048.0), ("selDn", -1024.0), ("selO", ORD)):
        act(A(n), A("gm"), AF.Copy, scale=w)
    ts(A("p128"), A("pf"), 128.0, ALU.add)
    act(A("g64"), A("gm", 0, 8), AF.Copy, scale=64.0)
    for j, w in enumerate([V + 512 * t for t in range(ROUNDS)] + [W, 256, 512]):
        act(A("gD", 8 * j, 8 * j + 8), A("gm", 0, 8), AF.Copy, scale=w + 1024.0)
    ms(A("one"), 1.0); ms(A("nord"), -ORD / 2); ms(A("c128"), 192.0 - 31.5 / 64)
    ts(A("mi"), A("k16"), A("iF"), ALU.is_equal); ts(A("sj"), A("mi"), -2.0, ALU.mult, 1.0, ALU.add); ts(A("il"), A("iF"), 10.0, ALU.is_lt)
    ts(A("IB", 0, 1), A("il"), -1.0, ALU.mult)
    for j in range(10):
        act(A("IB", 2 ** j, 2 ** (j + 1)), A("IB", 0, 2 ** j), AF.Copy, scale=A("sj", j, j + 1))
    cp("s", A("FB", 0, V), A("IB"))
    ms(A("two"), 2.0); ms(A("wr"), 0.0)
    scan(A("pw"), A("two"), A("wr"), ALU.mult, ALU.add, 0.25); tt(A("mp"), A("mi"), A("pw"), ALU.mult); red(A("tb"), A("mp"), ALU.add)
    tt(A("wcol"), A("tb"), A("il"), ALU.mult); ts(A("w8"), A("wcol"), 8192.0, ALU.mult)
    for i, w in ((10, -4096.0), (11, -256.0), (12, -1.0), (13, -4 * EQ)):
        ms(A("wr", i, i + 1), w)
    tt(A("mp2"), A("mi"), A("wr"), ALU.mult); red(A("wrow"), A("mp2"), ALU.add)
    for e, m in (("e", "meven"), ("o", "modd")):
        ts(A("sA" + e), A("il"), EQ, ALU.mult, A(m), ALU.mult); tt(A("cA" + e), A("wrow"), A(m), ALU.mult)
    ts(A("e15"), A("gf"), 16.0, ALU.mult, 15.0, ALU.add)
    ts(A("EK"), A("col"), A("e15"), ALU.is_equal)
    for n, w in (("nEK", -1.0), ("BL", A("wcol")), ("BL8", A("w8"))):
        act(A(n), A("EK"), AF.Copy, scale=w)
    ts(A("DM"), A("DM"), A("iF"), ALU.is_equal); ts(A("sv"), A("sv"), A("iF"), ALU.add); ts(A("dl"), A("dl"), A("iF"), ALU.add)
    cp("v", A("EXn"), A("it", 0, 32)); cp("v", A("EXw"), A("it", 32, 48))
    ms(A("rst"), 0.0); ms(A("rst", 0, 1024, 16), HUGE); ms(A("rs56"), 1.0); ms(A("rs56", 0, 448, 56), 0.0); ms(A("ch", 48, 56), 1.0)
    ms(A("dk"), 0.0); ts(A("dk", 12, 128, 16), A("ones", 0, 8), A("pf"), ALU.mult); ts(A("dk", 268, 384, 16), A("ones", 0, 8), A("p128"), ALU.mult)
    ms(A("mx"), HUGE); ms(A("thb"), 0.0)
    ts(A("c0"), A("pf"), -1.0, ALU.mult, 10 * EQ, ALU.add); ts(A("c1"), A("pf"), 128.0 - 10 * EQ, ALU.add)
    op("g", lambda e: e.partition_broadcast(A("th2")[0], A("th1", p1=1)[0], 128), [A("th1")], [A("th2")], 0.3)
    for j in range(4):
        ts(A("thK", 8 * j, 8 * j + 8), A("th2"), 1024.0, ALU.mult)
    cp("v", A("thC"), A("thK"))
    for j in range(3):
        ts(A("Fp", 16 * j, 16 * j + 16), A("dl", 0, 16), 256.0 * j - V, ALU.add)
    for j in range(4):
        cp("s", A("al", 16 * j, 16 * j + 16), A("Fp", 0, 16))
    cp("s", A("wins", 32, 64), A("al", 0, 32)); ms(A("c511"), 511.5)

    cklist(0)
    fill_ext("s", "XM", 0, "xF"); ms(A("xF", 0, V, 4), BIGX)
    cp("v", ext("CF", 0, 0, 256), A("ci", 64, 1088, 4))
    keyinit(0); distances(0)
    fill_ext("s", "P", 0, "PF"); fill_ext("s", "R", 0, "RF")
    cp("v", A("CF", 0, V), A("ci", 64, 1088))
    iota(A("SO", 0, V), [[0, V]]); iota(A("SE"), [[0, V]])
    dma("y", A("SO", 0, V, p0=1, ps=2), HB(T.succ[1:128:2, :]), V * KB); dma("y", A("SE", p0=0, ps=2), HB(T.succ[0:128:2, :]), V * KB)
    dma("y", A("XM", 0, V), HB(T.x[:]), V * KB)
    cp("v", A("SL0"), A("si", 0, V, 2)); cp("v", A("SL1"), A("si", 1, V, 2))
    for s, d in (("RF", "GR"), ("PF", "GP")):
        dma("y", A(d + "a", 0, G), A(s, V, V + G), G * KB); dma("y", A(d + "b", 0, G), A(s, V + G, W), G * KB)
    fill_ext("g", "SO", 0, copies=1); fill_ext("g", "R", 1)
    sums(True, range(16)); cp("v", A("Wo"), A("ps1", 0, 48))

    for t in range(ROUNDS):
        last, u, par, ck = t == ROUNDS - 1, t + 1, t % 2, "CK%d" % t
        if not last:
            cklist(u)
            for n in ("XM", "P"):
                fill_ext("g", n, u)
            fill_ext("g", "CF", u, copies=1); fill_ext("g", "SO", u, copies=1)
        for kk in range(8):
            s = (512 * kk, 512 * kk + 512); off = A(ck, 32 * kk, 32 * kk + 32)
            if kk in CMP_R[t]:
                by_scalar(A("oR", *s), A("RF"), off, ext("P", t), -1, AF.Relu, kk, A("one"))
            else:
                tt(A("oR", *s), IND(A("RF"), off), ext("P", t), ALU.is_le)
            keymm(kk, "oR", "selO")
            if kk in CMP_S[t]:
                by_scalar(A("oP", *s), A("PF"), off, ext("R", t), 1, AF.Relu, kk, A("one"))
            else:
                tt(A("oP", *s), IND(A("PF"), off), ext("R", t), ALU.is_ge)
            keymm(kk, "oP", "selO")
        scan(A("ks"), A("rst", 0, 512), A("ps0"), ALU.max, ALU.min)
        km = A("ks", 15, 512, 16)
        ts(A("wi"), km, 2.0 ** 22 - 1, ALU.min)
        ts(A("wn"), A("wi"), 63, ALU.bitwise_and)
        tt(A("Wn"), IND(A("wn"), A("EXn")), A("DM"), ALU.mult)
        for j in range(4):
            mm(A("ps6", 8 * (j // 2), 8 * (j // 2) + 8), A("Wn", 128 * j, 128 * j + 128), A("g64") if j % 2 else A("gm", 0, 8), j % 2 == 0)
        ts(A("nl"), A("ps6", 0, 16), V - 1.0, ALU.min)
        ts(A("nh"), A("ps6", 0, 16), float(V), ALU.is_ge)
        tt(A("dk", 13, 512, 16), km, A("thC"), ALU.is_ge)
        ts(A("wd", 0, 32), A("wi"), 14, ALU.arith_shift_right); ts(A("wd", 32, 64), A("wi"), 10, ALU.arith_shift_right, 15, ALU.bitwise_and)
        cp("v", A("dk", 10, 1024, 16), A("wd"))
        for h in (0, 1):
            o = A("ps7", 128 * h, 128 * h + 128)
            mm(o, A("dk", 256 * h, 256 * h + 128), A("I"), True); mm(o, A("dk", 511 + 256 * h, 639 + 256 * h), A("I"))
        cp("s", A("Kr"), A("ps7", 0, 256))
        ts(A("wD"), A("wi"), 2 ** 22 - 1024, ALU.bitwise_and)
        ts(A("bs"), A("wD", 16, 24), 0.25, ALU.mult, A("c1"), ALU.add)
        ts(A("thb", 0, 8), A("wD", 0, 8), -0.25, ALU.mult, A("c0"), ALU.add)
        ts(A("nb"), A("dk", 13, 512, 16), -32 * EQ, ALU.mult); tt(A("thr"), A("nb"), A("thb"), ALU.add)
        for h in (0, 1):
            act(A("fl", 128 * h, 128 * h + 128), A("ps0", 256 * h, 256 * h + 128), AF.Sign, bias=A("nord"))
        fb = IND(A("FB", 0, V), A("nl"))
        tt(A("Bk"), fb, A("Kr"), ALU.add)
        act(A("Ae"), fb, AF.Identity, bias=A("cAe"), scale=A("sAe"))
        act(A("Ao"), fb, AF.Identity, bias=A("cAo"), scale=A("sAo"))
        for s, gg in enumerate((0, 2, 4, 6, 1, 3, 5, 7)):
            for h in (1, 0):
                z, m = A("ps%d" % (2 + 2 * h + s % 2), 0, 256), A("mx", 16 * h + gg, 16 * h + gg + 1)
                rows = dict(p0=32 * (gg // 2), p1=32 * (gg // 2) + 32)
                mm(z, A(("Ae", "Ao")[gg % 2], 128 * h, 128 * h + 128, **rows), A("Bk", **rows), True)
                if h:
                    act(A("pc", 256 * s, 256 * s + 256), z, AF.Relu, bias=A("bs", gg, gg + 1), accum=m)
                else:
                    red(m, z, ALU.max)
        tolist(A("ps6", 16, 32), "BL", "Bk", 256, True)
        for j in (0, 16):
            act(A("wins", j, j + 16), A("ps6", 16, 32), AF.Identity, bias=A("c511"))
        tt(A("RW", 0, 256), IND(A("RF", 0, V), A("nl")), ext("R", t, 0, 256), ALU.min)
        cp("s", A("RW", 256, 512), A("RF", t, V, 4)); cp("s", A("RW", 512, 768), ext("R", t, 0, 256))
        tt(A("lose"), A("mx"), A("thr"), ALU.is_gt)
        tt(A("W2"), IND(A("lose"), A("EXw")), A("DM", 0, 256), ALU.mult)
        mm(A("ps6", 32, 96), A("I"), A("al"), True); mm(A("ps6", 32, 96), A("kI"), A("ones", 0, 64))
        for j in range(4):
            for h in (0, 1):
                c = 8 * (t if j == 0 else 3 + j)
                mm(A("ps6", 32 + 16 * j + 8 * h, 40 + 16 * j + 8 * h), A("W2", 128 * h, 128 * h + 128), A("gD", c, c + 8))
        tt(A("LLf"), A("ps6", 32, 96), A("wins"), ALU.max); cp("v", A("LL"), A("LLf"))
        bt = A("LL", 0, 16)
        cp("s", A("RF", t, V, 4), IND(A("RW"), A("LL", 32, 48))); cp("s", A("R", t, V, 4), IND(A("RW"), A("LL", 48, 64)))
        tt(A("sn"), IND(win("SO", t), bt), A("SE", t, V, 4), ALU.add); cp("v", A("SL%d" % par, t // 2, 512, 2), A("sn"))
        cp("v", IND(A("RF"), A("LL", 16, 32)), A("RW", 0, 256))
        tt(A("xs"), IND(win("XM", t), bt), ext("XM", t, 256, 512), ALU.add)
        ts(A("xi"), A("xs"), -0.5, ALU.add, 0.5, ALU.mult); cp("v" if last else "g", A("XM", t, V, 4), A("xi"))
        tt(A("nh2"), A("nh"), A("dl", 16 * t, 16 * t + 16), ALU.mult); tt(A("buf"), A("nh2"), A("wins", 0, 16), ALU.max); cp("v", A("bu"), A("buf"))

        def candidates():
            o = [A("ps1", 256 + 128 * h, 384 + 128 * h) for h in (0, 1)]; both = A("ps1", 256, 512)
            own = [ext("CF", t, 128 * h, 128 * h + 128) for h in (0, 1)]
            for h in (0, 1):
                mm(o[h], A("fl", 128 * h, 128 * h + 128), A("hI"), True); mm(o[h], A("ones"), A("hI"))
            if last:
                tt(A("dC"), IND(win("CF", t), A("bu")), A("ci", 64 + t, 1088, 4), ALU.subtract)
                tt(A("oi"), both, A("dC"), ALU.mult); tt(A("CF", t, V, 4), A("oi"), ext("CF", t, 0, 256), ALU.add)
                return
            cp("s", A("fn"), both); cp("s", A("dC"), IND(win("CF", t), A("bu")))
            for h in (0, 1):
                mm(o[h], A("I32"), A("dC", 128 * h, 128 * h + 128), True); mm(o[h], A("nI32"), own[h])
            tt(A("oi"), both, A("fn"), ALU.mult)
            for h in (0, 1):
                mm(o[h], A("I32"), A("oi", 128 * h, 128 * h + 128), True); mm(o[h], A("I32"), own[h])
            cp("s", A("CF", t, V, 4), both)
        if last:
            candidates()
            dma("y", HB(T.yx[:]), A("XM", 0, V), V * KB); dma("y", HB(T.yc[:]), A("CF", 0, V), 2 * V * KB)
        else:
            cp("v", IND(win("FB", t), bt), A("IB", t, V, 4))
            tolist(A("ps6", 96, 160), "BL", "FB", V, True)
            ts(A("FL"), A("ps6", 96, 160), 511.5, ALU.add)
            tt(A("Pn"), IND(win("P", t), bt), ext("P", t, 256, 512), ALU.max); cp("g", A("P", t, V, 4), A("Pn"))
            ts(A("SO", t, V, 4), A("sn"), A("okc"), ALU.mult)
            iota(A("XM", u, V, 4), [[0, 256]], int(BIGX))
            cp("s", A("xF", 0, V), IND(A("XM", 0, V), A("FL"))); cp("s", A("PF", 0, V), IND(A("P", 0, V), A("FL")))
            mm(A("ps4", 0, 32), A("ones"), A("lose"), True); red(A("Mf"), A("ps4", 0, 32), ALU.add)
            ts(A("Mi"), A("Mf"), -1.0, ALU.mult, 4096.0, ALU.add); ts(A("Mj"), A("Mi"), 31, ALU.bitwise_and)
            ts(A("Mk"), A("Mj"), 1024.0, ALU.mult); ts(A("thC"), A("thK"), A("Mk"), ALU.add)
            ts(A("FLf"), A("ps6", 96, 144), 511.5, ALU.add)
            tt(A("dF1"), A("FLf"), A("Fp"), ALU.subtract); ts(A("dF2"), A("FLf"), float(G), ALU.is_lt); tt(A("dF"), A("dF1"), A("dF2"), ALU.mult)
            sums(True, range(1 - par, 16, 2))
        mm(A("ps5"), A("I"), A("R", par, V, 2), True)
        for c0, c1 in ((0, 6), (6, 8)) if not last else ((0, 4), (4, 7), (7, 8)):
            for c in range(c0, c1):
                who = ["v" if d in G3_V[t] else "s" for d in (2 * c, 2 * c + 1)]
                for q, d0, d1 in [(who[0], 2 * c, 2 * c + 2)] if who[0] == who[1] else [(who[0], 2 * c, 2 * c + 1), (who[1], 2 * c + 1, 2 * c + 2)]:
                    cp(q, A("g3", 512 * d0, 512 * d1), IND(A("RF"), A("SL%d" % par, 32 * d0, 32 * d1)))
                s = (1024 * c, 1024 * c + 1024)
                scan(A("s3", *s), A("rst"), A("g3", *s), ALU.max, ALU.min)
            tt(A("R", par + 128 * c0, 128 * c1, 2), A("s3", 1024 * c0 + 15, 1024 * c1, 16), A("ps5", 64 * c0, 64 * c1), ALU.min)
            if last:
                dma("sy"[c0 % 2], HB(T.yr[:, 128 * c0:128 * c1]), A("R", 128 * c0, 128 * c1), 128 * (c1 - c0) * KB)
        if last:
            break
        msg = "MS%d" % t
        tolist(A("ps1", 0, 48), "EK", "R", G, False, range(par, 16, 2))
        tt(A("ch", 0, 48), A("ps1", 0, 48), A("Wo"), ALU.not_equal); cp("v", A("Wo"), A("ps1", 0, 48))
        scan(A("cc"), A("ones", 0, 56), A("ch"), ALU.mult, ALU.add)
        for c in range(8):
            mm(A("ps4", 56 * c, 56 * c + 56), A("B16"), A("cc"), True)
        for o in (128, 192):
            mm(A("ps6", o, o + 56), A("B16"), A("cc"), True); mm(A("ps6", o, o + 56), A("nLs"), A("ch"))
        mm(A("ps6", 192, 248), A("kI"), A("ch"))
        tt(A("f1"), A("ps4", 0, 448), A("sv"), ALU.is_le)
        scan(A("f2"), A("rs56"), A("f1"), ALU.mult, ALU.add)
        cp("v", A("cu"), A("f2", 55, 448, 56)); cp("v", A("cw"), A("ps6", 128, 184))
        ts(A("go"), A("ps6", 192, 240), 128.0 - 1024.0, ALU.is_le)
        tt(A("f3"), IND(A("cw"), A("cu")), A("srow"), ALU.is_le)
        tolist(A("ps7", 0, 8), "EK", "f3", 128, True); mm(A("ps7", 0, 8), A("I16"), A("f2", 55, 448, 56))
        ts(A("sl"), A("ps7", 0, 8), G - 1.0, ALU.min); cp("v", A(msg, 256, 264), A("ps7", 0, 8))
        tt(A("go2"), A("go"), A("dF"), ALU.mult); tt(A("Fp"), A("Fp"), A("go2"), ALU.add); cp("v", A(msg, 264, 312), A("Fp"))
        for k, n in enumerate("RP"):
            cp("v", A(msg, 128 * k, 128 * k + 128), IND(A(n, 0, G), A("sl")))
        send(A(msg), A("La%d" % t), A("Lb%d" % t), "a%d" % t)
        cp("s", A("RF", 0, V), IND(A("R", 0, V), A("FL")))
        if t + 2 < ROUNDS:
            fill_ext("g", "R", t + 2)
        keyinit(u); distances(u); candidates()
        o = A("ps7", 16, 32)
        for i in range(16):
            mm(o, A("BL", 15 - i, 143 - i), A("FB", u + 4 * i, V, 64), i == 0)
        mm(o, A("n4I"), A("al", 0, 16))
        ts(A("nsf"), o, u - 511.5, ALU.not_equal, 256.0, ALU.mult); tt(A("wins", 32, 48), A("nsf"), A("al", 0, 16), ALU.add)
        for k, n in ((1, "P"), (0, "R")):
            for j, d in enumerate("ab"):
                land = "L%s%d" % (d, t)
                cp("v", IND(A("G" + n + d), A(land, 256, 264)), A(land, 128 * k, 128 * k + 128))
                cp("v" if (n, d) in GH_V else "s", A(n + "F", V + G * j, V + G * j + G), IND(A("G" + n + d), A(land, 264, 312)))

    if "o" not in _ORDER:
        _ORDER["o"] = order(ops); _ORDER["p"] = needs(ops)
    seq, pre = _ORDER["o"], _ORDER["p"]
    eng = {"v": g.vector, "s": g.scalar, "t": g.tensor, "g": g, "y": g.sync}
    cnt = {q: 0 for q in eng}; clk = {q: {} for q in eng}; done = {}; total = {}; nd = 0
    closes = {ops[i]["group"]: i for i in seq if ops[i]["q"] == "t"}
    for i in seq:
        o = ops[i]; q = o["q"]
        if q == "x":
            done[i] = (o["call"], 2 * ne, {}); total[o["call"]] = 2 * ne
            continue
        wait = [done[j] for j in pre[i] if j not in o["after"] and not (q == "t" == ops[j]["q"]) and done[j] is not None]
        if q == "g" and o["kind"] == "" and cnt[q]:
            wait.append(("qg", cnt[q], {}))
        for sem, val, ck in sorted(wait, key=lambda w: -len(w[2])):
            if clk[q].get(sem, 0) < val:
                eng[q].wait_ge(T.sem[sem], val)
                for s, v in list(ck.items()) + [(sem, val)]:
                    clk[q][s] = max(clk[q].get(s, 0), v)
        if o["kind"] == "dma":
            sem = "d%d" % nd; nd += 1
            o["call"](eng[q]).then_inc(T.sem[sem], 16); done[i] = (sem, 16, dict(clk[q])); total[sem] = 16
        elif o["kind"] == "rem":
            o["call"](g); done[i] = (o["loc"], 2 * ne, {}); total[o["loc"]] = total.get(o["loc"], 0) + ne
        else:
            cnt[q] += 1
            ins = o["call"](eng[q], closes[o["group"]] == i) if q == "t" else o["call"](eng[q])
            ins.then_inc(T.sem["q" + q], 1); done[i] = ("q" + q, cnt[q], dict(clk[q])); total["q" + q] = cnt[q]
    for s, v in total.items():
        g.wait_ge(T.sem[s], v)
